import numpy as np
import ml_dtypes


def mxq(x, axis, fmt="e4m3"):
    dtype, down = {"e4m3": (ml_dtypes.float8_e4m3fn, 7), "e5m2": (ml_dtypes.float8_e5m2, 14)}[fmt]
    v = np.moveaxis(np.asarray(x, np.float32).astype(ml_dtypes.bfloat16).astype(np.float64), axis, -1)
    blocks = v.reshape(v.shape[:-1] + (-1, 32))
    amax = np.abs(blocks).max(-1, keepdims=True)
    byte = np.maximum(np.where(amax > 0, np.frexp(amax)[1] - 1 + 127, 0) - down, 1)
    scale = np.exp2(byte - 127.0)
    codes = (blocks / scale).astype(np.float32).astype(dtype).astype(np.float64)
    return np.moveaxis((codes * scale).reshape(v.shape), -1, axis)


WIDE = False


def mx_kscale(k):
    if not WIDE:
        return np.ones(k)
    levels = np.array([10, -10, 5, -5, 0])
    if k % 512:
        return np.exp2(np.random.permutation(np.resize(levels, k // 32))).repeat(32)
    a = np.empty((k // 512, 16))
    for p in range(k // 512):
        a[p, :8] = np.random.permutation(np.resize(levels, 8))
        for g in range(8):
            far = levels[np.abs(levels - a[p, g]) >= 10]
            a[p, g + 8] = far[np.random.randint(len(far))]
    return np.exp2(a.ravel()).repeat(32)


def f64(x):
    return np.asarray(x).astype(np.float64)


def striped(idx):
    return np.tile(idx.reshape(-1, 16).T, (8, 1)).astype(np.uint16)


def unstriped(offs):
    return offs[:16].T.reshape(-1).astype(np.int64)


E2M1 = np.array([0.0, 0.5, 1.0, 1.5, 2.0, 3.0, 4.0, 6.0, -0.0, -0.5, -1.0, -1.5, -2.0, -3.0, -4.0, -6.0])


def pack_weight(w, fmt):
    k, n = w.shape
    w = f64(np.asarray(w, np.float32).astype(ml_dtypes.bfloat16)).reshape(k // 32, 32, n)
    amax = np.abs(w).max(1)
    if fmt == "e4m3":
        byte = np.frexp(amax)[1] - 1 + 127 - 7
    else:
        mant, ex = np.frexp(amax / 6.0)
        byte = np.where(mant > 0.5, ex, ex - 1) + 127
    byte = np.clip(np.where(amax > 0, byte, 1), 1, 254)
    scaled = (w * np.exp2(127.0 - byte)[:, None, :]).reshape(k, n).astype(np.float32)
    by_word = np.ascontiguousarray(scaled.reshape(k // 512, 128, 4, n).transpose(0, 1, 3, 2))
    if fmt == "e4m3":
        words = by_word.astype(ml_dtypes.float8_e4m3fn).view(np.uint8)
    else:
        c = by_word.astype(ml_dtypes.float4_e2m1fn).view(np.uint8) & 0xF
        words = (c[..., 0::2] | (c[..., 1::2] << 4)).reshape(k // 512, 128, 2 * n)
    return np.ascontiguousarray(words), np.ascontiguousarray(byte.astype(np.uint8).reshape(k // 512, 16, n))


def unpack_weight(words, scales, fmt):
    g, _, n = scales.shape
    words = np.ascontiguousarray(words).reshape(g, 128, n, -1)
    if fmt == "e4m3":
        vals = words.view(ml_dtypes.float8_e4m3fn).astype(np.float64)
    else:
        nib = np.empty((g, 128, n, 4), np.uint8)
        nib[..., 0::2] = words & 0xF
        nib[..., 1::2] = words >> 4
        vals = E2M1[nib]
    vals = vals * np.repeat(np.exp2(scales.astype(np.float64) - 127.0), 8, axis=1)[..., None]
    return vals.transpose(0, 1, 3, 2).reshape(g * 512, n)


def gelu(v):
    return 0.5 * v * (1.0 + np.tanh(np.sqrt(2.0 / np.pi) * (v + 0.044715 * v**3)))


K, T, K2, T2, S, P, H, N = 1024, 2048, 512, 1024, 512, 512, 1024, 384

def setup_inputs():
    n = np.random.standard_normal
    s = mx_kscale(K)[:, None]
    s2 = mx_kscale(K2)[:, None]
    u = mx_kscale(H)[:, None]
    tab_words, tab_scales = pack_weight(n((K, T)) * s, "e4m3")
    w2_words, w2_scales = pack_weight(n((K, H)) / np.sqrt(K) / s * u.T, "e2m1")
    wo_words, wo_scales = pack_weight(n((H, N)) / np.sqrt(H) / u, "e4m3")
    return {
        "tab_words": tab_words, "tab_scales": tab_scales,
        "offs": striped(np.random.permutation(T)[:P]),
        "offs2": striped(np.random.permutation(T2)[:S]),
        "offs3": striped(np.random.permutation(T2)[:P]),
        "base": (n((K2, T2)) * s2).astype(np.float32),
        "xs": (np.round(16 * n((K2, S))) / 16 * s2).astype(np.float32),
        "w1": (n((K2, H)) / np.sqrt(K2) / s2 * u.T).astype(np.float32),
        "w2_words": w2_words, "w2_scales": w2_scales,
        "wg": (1.5 * n((K, H)) / np.sqrt(K) / s).astype(np.float32),
        "wo_words": wo_words, "wo_scales": wo_scales,
        "bo": (0.5 * n(N)).astype(np.float32),
    }

def reference(tab_words, tab_scales, offs, offs2, offs3, base, xs, w1, w2_words, w2_scales, wg, wo_words, wo_scales, bo):
    page = f64(base).copy()
    page[:, unstriped(offs2)] = f64(xs)
    a = mxq(f64(w1), 0, "e4m3").T @ mxq(page, 0, "e4m3")
    cell = a[:, unstriped(offs3)]
    v = unpack_weight(tab_words, tab_scales, "e4m3")[:, unstriped(offs)]
    b = unpack_weight(w2_words, w2_scales, "e2m1").T @ v
    d = mxq(f64(wg), 0, "e4m3").T @ v
    trust = 1.0 / (1.0 + np.exp(-d))
    z = b + trust * (cell - b)
    y = unpack_weight(wo_words, wo_scales, "e4m3").T @ mxq(z, 0, "e4m3")
    return y + f64(bo)[:, None]

@@ -1,0 +1,322 @@
+from contextlib import ExitStack
+
+import concourse.mybir as mybir
+
+K, T, K2, T2, S, H, N = 1024, 2048, 512, 1024, 512, 1024, 384
+FLOPS = 2 * (K2 * H * T2 + 2 * K * H * S + H * N * S)
+
+F32 = mybir.dt.float32
+BF16 = mybir.dt.bfloat16
+I32 = mybir.dt.int32
+U32 = mybir.dt.uint32
+U16 = mybir.dt.uint16
+U8 = mybir.dt.uint8
+FP8X4 = mybir.dt.float8_e4m3fn_x4
+FP4X4 = mybir.dt.float4_e2m1fn_x4
+ALU = mybir.AluOpType
+ACT = mybir.ActivationFunctionType
+
+P = 128
+PACK = 4
+KP = P * PACK
+BANK = 512
+
+
+def tile_list_foothold_terrain_blend_kernel(
+    tc, tab_words, tab_scales, offs, offs2, offs3, base, xs, w1, w2_words, w2_scales, wg, wo_words, wo_scales, bo, out
+):
+    nc = tc.nc
+    with ExitStack() as ctx:
+        lists = ctx.enter_context(tc.tile_pool(name="lists", bufs=1))
+        sb = ctx.enter_context(tc.tile_pool(name="sb", bufs=1))
+        psum = ctx.enter_context(tc.psum_pool(name="psum", bufs=4))
+
+        def new(name, shape, dtype, tag=None, bufs=1):
+            return sb.tile(shape, dtype, name=name, tag=tag or name, bufs=bufs, align_bytes=64)
+
+        def load_list(name, src):
+            tile = lists.tile([P, S // 16], U16, name=name)
+            nc.sync.dma_start(tile[:], src)
+            return tile
+
+        tab_sc = new("tab_sc", [P, 2, T], U8)
+        w2_sc_raw = new("w2_sc_raw", [P, 2, H], U8)
+        wo_sc = new("wo_sc", [P, N], U8)
+        nc.vector.memset(tab_sc[:].rearrange("p a t -> p (a t)").bitcast(I32), 0)
+        nc.vector.memset(w2_sc_raw[:].rearrange("p a t -> p (a t)").bitcast(I32), 0)
+        nc.vector.memset(wo_sc[:].bitcast(I32), 0)
+
+        warm = new("warm", [P, 2], F32)
+        nc.gpsimd.memset(warm[:, 0:1], 0.0)
+        nc.scalar.activation(out=warm[:, 1:2], in_=warm[:, 0:1], func=ACT.Sigmoid)
+
+        base_v = base.rearrange("(p t) c -> p t c", t=PACK)
+        xs_v = xs.rearrange("(p t) c -> p t c", t=PACK)
+        page = [None] * PACK
+        patch = [None] * PACK
+        page_bf = [new("page_bf%d" % h, [P, BANK, PACK], BF16) for h in range(2)]
+
+        def load_plane(t):
+            page[t] = new("page%d" % t, [P, T2], F32)
+            patch[t] = new("patch%d" % t, [P, S], F32)
+            nc.sync.dma_start(page[t][:], base_v[:, t, :])
+            nc.sync.dma_start(patch[t][:], xs_v[:, t, :])
+
+        def scatter_plane(t):
+            nc.vector.tensor_copy(page[t][:].indirect(idx2[:]), patch[t][:])
+
+        def round_plane(t):
+            for h in range(2):
+                nc.scalar.copy(out=page_bf[h][:, :, t], in_=page[t][:, h * BANK : (h + 1) * BANK])
+
+        def load_weight(name, rows, b):
+            raw = new(name, [P, PACK, KP], F32, tag="raw", bufs=3)
+            nc.sync.dma_start(raw[:], rows.rearrange("(p j) c -> p j c", j=PACK)[:, :, b * KP : (b + 1) * KP])
+            return raw
+
+        def round_weight(raw, dst, on_gpsimd):
+            for half in range(2):
+                ms = slice(half * 64, (half + 1) * 64)
+                o = dst.rearrange("p (t m j) -> p m j t", t=PACK, j=PACK)[:, ms]
+                i = raw[:].rearrange("p j (m t) -> p m j t", t=PACK)[:, ms]
+                if on_gpsimd:
+                    ts = slice(half * 2, (half + 1) * 2)
+                    o = dst.rearrange("p (t m j) -> p t m j", t=PACK, j=PACK)[:, ts]
+                    i = raw[:].rearrange("p j (m t) -> p t m j", t=PACK)[:, ts]
+                    nc.gpsimd.tensor_scalar(out=o, in0=i, scalar1=1.0, scalar2=0.0, op0=ALU.mult, op1=ALU.add)
+                else:
+                    nc.scalar.copy(out=o, in_=i)
+
+        def quantise(name, src, cols, tag=None):
+            codes = new(name + "_c", [P, cols], U32, tag=tag)
+            scales = new(name + "_s", [P, cols], U8)
+            nc.vector.quantize_mx(out=codes[:].bitcast(FP8X4), scales=scales[:], in_=src)
+            return codes, scales
+
+        idx2 = load_list("idx2", offs2)
+        load_plane(0)
+        load_plane(1)
+        raw_w1_0 = load_weight("raw_w1_0", w1, 0)
+        load_plane(2)
+        raw_wg_00 = load_weight("raw_wg_00", wg[0:KP, :], 0)
+        load_plane(3)
+        raw_wg_01 = load_weight("raw_wg_01", wg[KP : 2 * KP, :], 0)
+        idx = load_list("idx", offs)
+        tab_w = []
+        for a in range(2):
+            tile = new("tab_w%d" % a, [P, T], I32)
+            nc.sync.dma_start(tile[:], tab_words[a].rearrange("p t i -> p (t i)").bitcast(I32))
+            tab_w.append(tile)
+        for q in range(4):
+            nc.sync.dma_start(
+                tab_sc[32 * q : 32 * q + 4, :, :].bitcast(I32),
+                tab_scales[:, 4 * q : 4 * q + 4, :].rearrange("a r t -> r a t").bitcast(I32),
+            )
+        for q in range(4):
+            nc.sync.dma_start(
+                w2_sc_raw[32 * q : 32 * q + 4, :, :].bitcast(I32),
+                w2_scales[:, 4 * q : 4 * q + 4, :].rearrange("a r t -> r a t").bitcast(I32),
+            )
+        w2_raw = new("w2_raw", [P, 2, 2 * H], U8)
+        nc.sync.dma_start(w2_raw[:].bitcast(I32), w2_words.rearrange("a p c -> p a c").bitcast(I32))
+        idx3 = load_list("idx3", offs3)
+
+        stage_a = new("stage_a", [P, 2 * KP * PACK], BF16)
+        stage_b = new("stage_b", [P, KP * PACK], BF16, tag="stage", bufs=2)
+        for t in range(PACK):
+            scatter_plane(t)
+            round_plane(t)
+            if t == 0:
+                round_weight(raw_w1_0, stage_a[:, 0 : KP * PACK], True)
+            if t == 1:
+                round_weight(raw_wg_00, stage_a[:, KP * PACK :], True)
+        round_weight(raw_wg_01, stage_b[:], True)
+
+        raw_w1_1 = load_weight("raw_w1_1", w1, 1)
+        raw_wg_10 = load_weight("raw_wg_10", wg[0:KP, :], 1)
+        raw_wg_11 = load_weight("raw_wg_11", wg[KP : 2 * KP, :], 1)
+        wo_w = new("wo_w", [P, 2, N], I32)
+        nc.sync.dma_start(wo_w[:], wo_words.rearrange("a p c i -> p a (c i)").bitcast(I32))
+        for q in range(4):
+            nc.sync.dma_start(
+                wo_sc[32 * q : 32 * q + 8, :].bitcast(I32), wo_scales[:, 4 * q : 4 * q + 4, :].bitcast(I32)
+            )
+        bias = new("bias", [P, N // P], F32)
+        with nc.allow_non_contiguous_dma(reason="one bias value for each partition"):
+            nc.sync.dma_start(bias[:], bo.rearrange("(c p) -> p c", p=P))
+
+        first_c, first_s = quantise("first", stage_a[:], 2 * KP)
+        w1_q = [(first_c[:, 0:KP], first_s[:, 0:KP]), None]
+        wg_q = [[(first_c[:, KP:], first_s[:, KP:]), None], [None, None]]
+
+        v_w = new("v_w", [P, 2, S], U32)
+        v_s = new("v_s", [P, 2, S], U8)
+        nc.vector.tensor_copy(v_w[:, 0, :], tab_w[0][:].bitcast(U32).indirect(idx[:]))
+        page_q = []
+        for h in range(2):
+            c, s = quantise(
+                "page%d" % h, page_bf[h][:].rearrange("p c t -> p (c t)"), BANK, tag="tab_w0" if h == 1 else None
+            )
+            page_q.append((c, s))
+        nc.vector.tensor_copy(v_w[:, 1, :], tab_w[1][:].bitcast(U32).indirect(idx[:]))
+        c, s = quantise("wg01", stage_b[:], KP)
+        wg_q[0][1] = (c[:], s[:])
+        for a in range(2):
+            nc.vector.tensor_copy(v_s[:, a, :], tab_sc[:, a, :].indirect(idx[:]))
+
+        w2_w = new("w2_w", [P, 2, 2 * H], U8)
+        w2_s = new("w2_s", [P, 2, H], U8)
+        nc.vector.tensor_copy(
+            out=w2_w[:].bitcast(U16).rearrange("p a (b t g m) -> p (a b) g t m", b=2, t=PACK, m=8),
+            in_=w2_raw[:].bitcast(U16).rearrange("p a (b g m t) -> p (a b) g t m", b=2, t=PACK, m=8),
+        )
+        nc.vector.tensor_copy(
+            out=w2_s[:].rearrange("p a (b t g m) -> p (a b) g t m", b=2, t=PACK, m=16),
+            in_=w2_sc_raw[:].rearrange("p a (b g m t) -> p (a b) g t m", b=2, t=PACK, m=16),
+        )
+
+        a_rows = {}
+        trust = {}
+
+        def make_a(b, t):
+            cols = slice(t * P, (t + 1) * P)
+            tile = new("a%d%d" % (b, t), [P, T2], F32, tag="a", bufs=8)
+            for h in range(2):
+                acc = psum.tile([P, BANK], F32, name="acc", tag="s_bank")
+                nc.tensor.matmul_mx(
+                    out=acc[:],
+                    lhsT=w1_q[b][0][:, cols].bitcast(FP8X4),
+                    lhsT_scale=w1_q[b][1][:, cols],
+                    rhs=page_q[h][0][:].bitcast(FP8X4),
+                    rhs_scale=page_q[h][1][:],
+                    start=True,
+                    stop=True,
+                )
+                nc.scalar.copy(out=tile[:, h * BANK : (h + 1) * BANK], in_=acc[:])
+            a_rows[b, t] = tile
+
+        def make_trust(b, t):
+            cols = slice(t * P, (t + 1) * P)
+            acc = psum.tile([P, BANK], F32, name="acc", tag="s_bank")
+            for a in range(2):
+                nc.tensor.matmul_mx(
+                    out=acc[:],
+                    lhsT=wg_q[b][a][0][:, cols].bitcast(FP8X4),
+                    lhsT_scale=wg_q[b][a][1][:, cols],
+                    rhs=v_w[:, a, :].bitcast(FP8X4),
+                    rhs_scale=v_s[:, a, :],
+                    start=(a == 0),
+                    stop=(a == 1),
+                )
+            tile = new("trust%d%d" % (b, t), [P, S], F32, tag="trust", bufs=8)
+            nc.scalar.activation(out=tile[:], in_=acc[:], func=ACT.Sigmoid)
+            trust[b, t] = tile
+
+        def make_code(b, t):
+            c0 = b * KP + t * P
+            acc = psum.tile([P, BANK], F32, name="acc", tag="v_bank")
+            for a in range(2):
+                nc.tensor.matmul_mx(
+                    out=acc[:],
+                    lhsT=w2_w[:, a, 2 * c0 : 2 * (c0 + P)].bitcast(FP4X4),
+                    lhsT_scale=w2_s[:, a, c0 : c0 + P],
+                    rhs=v_w[:, a, :].bitcast(FP8X4),
+                    rhs_scale=v_s[:, a, :],
+                    start=(a == 0),
+                    stop=(a == 1),
+                )
+            return acc
+
+        def blend(b, parts):
+            width = S // parts
+            cell = [new("cell%d%d" % (b, h), [P, PACK, width], F32) for h in range(parts)]
+            rest = new("rest%d" % b, [P, PACK, S], F32)
+            codes = [make_code(b, t) for t in range(PACK)]
+
+            def pick(t, h):
+                nc.vector.tensor_tensor(
+                    out=cell[h][:, t, :],
+                    in0=a_rows[b, t][:].indirect(idx3[:, h * width // 16 : (h + 1) * width // 16]),
+                    in1=trust[b, t][:, h * width : (h + 1) * width],
+                    op=ALU.mult,
+                )
+
+            for t in range(PACK):
+                nc.vector.scalar_tensor_tensor(
+                    out=rest[:, t, :], in0=trust[b, t][:], scalar=1.0, in1=codes[t][:], op0=ALU.subtract, op1=ALU.mult
+                )
+                pick(t, 0)
+            return cell, rest, pick
+
+        def finish_z(b, h, width, cell, rest):
+            z_bf = new("z_bf%d%d" % (b, h), [P, width * PACK], BF16, tag="stage", bufs=2)
+            nc.vector.tensor_tensor(
+                out=z_bf[:].rearrange("p (c i t) -> p c t i", i=2, t=PACK),
+                in0=cell[:].rearrange("p t (c i) -> p c t i", i=2),
+                in1=rest[:, :, h * width : (h + 1) * width].rearrange("p t (c i) -> p c t i", i=2),
+                op=ALU.subtract,
+            )
+            return quantise("z%d%d" % (b, h), z_bf[:], width)
+
+        for t in range(PACK):
+            make_a(0, t)
+        for t in range(PACK):
+            make_trust(0, t)
+        cell0, rest0, pick0 = blend(0, 1)
+
+        round_weight(raw_w1_1, stage_a[:, 0 : KP * PACK], False)
+        c, s = quantise("w1_1", stage_a[:, 0 : KP * PACK], KP)
+        w1_q[1] = (c[:], s[:])
+        round_weight(raw_wg_10, stage_a[:, KP * PACK :], False)
+        c, s = quantise("wg10", stage_a[:, KP * PACK :], KP)
+        wg_q[1][0] = (c[:], s[:])
+        stage_c = new("stage_c", [P, KP * PACK], BF16, tag="stage", bufs=2)
+        round_weight(raw_wg_11, stage_c[:], False)
+        z0 = finish_z(0, 0, S, cell0[0], rest0)
+        c, s = quantise("wg11", stage_c[:], KP)
+        wg_q[1][1] = (c[:], s[:])
+
+        for t in range(PACK):
+            make_a(1, t)
+            make_trust(1, t)
+        cell1, rest1, pick1 = blend(1, 2)
+
+        half = S // 2
+        outs = [
+            [psum.tile([P, half], F32, name="acc", tag=tag) for c in range(N // P)] for tag in ("v_bank", "s_bank")
+        ]
+
+        def read_out(b, h, codes, scales):
+            for c in range(N // P):
+                cols = slice(c * P, (c + 1) * P)
+                nc.tensor.matmul_mx(
+                    out=outs[h][c][:],
+                    lhsT=wo_w[:, b, cols].bitcast(FP8X4),
+                    lhsT_scale=wo_sc[4 * b : P, cols],
+                    rhs=codes.bitcast(FP8X4),
+                    rhs_scale=scales,
+                    start=(b == 0),
+                    stop=(b == 1),
+                )
+
+        def store(h):
+            for c in range(N // P):
+                res = new("res%d%d" % (h, c), [P, half], F32)
+                if h == 1 and c == 1:
+                    nc.vector.tensor_scalar(
+                        out=res[:], in0=outs[h][c][:], scalar1=bias[:, c : c + 1], scalar2=None, op0=ALU.add
+                    )
+                else:
+                    nc.scalar.activation(out=res[:], in_=outs[h][c][:], func=ACT.Identity, bias=bias[:, c : c + 1])
+                nc.sync.dma_start(out[c * P : (c + 1) * P, h * half : (h + 1) * half], res[:])
+
+        for h in range(2):
+            read_out(0, h, z0[0][:, h * half : (h + 1) * half], z0[1][:, h * half : (h + 1) * half])
+        c, s = finish_z(1, 0, half, cell1[0], rest1)
+        read_out(1, 0, c[:], s[:])
+        store(0)
+        for t in range(PACK):
+            pick1(t, 1)
+        c, s = finish_z(1, 1, half, cell1[1], rest1)
+        read_out(1, 1, c[:], s[:])
+        store(1)

@@ -54,7 +54,6 @@ def tile_list_foothold_terrain_blend_kernel(
         xs_v = xs.rearrange("(p t) c -> p t c", t=PACK)
         page = [None] * PACK
         patch = [None] * PACK
-        page_bf = [new("page_bf%d" % h, [P, BANK, PACK], BF16) for h in range(2)]
 
         def load_plane(t):
             page[t] = new("page%d" % t, [P, T2], F32)
@@ -65,27 +64,20 @@ def tile_list_foothold_terrain_blend_kernel(
         def scatter_plane(t):
             nc.vector.tensor_copy(page[t][:].indirect(idx2[:]), patch[t][:])
 
-        def round_plane(t):
-            for h in range(2):
-                nc.scalar.copy(out=page_bf[h][:, :, t], in_=page[t][:, h * BANK : (h + 1) * BANK])
-
-        def load_weight(name, rows, b):
-            raw = new(name, [P, PACK, KP], F32, tag="raw", bufs=3)
-            nc.sync.dma_start(raw[:], rows.rearrange("(p j) c -> p j c", j=PACK)[:, :, b * KP : (b + 1) * KP])
+        def load_weight(name, rows, c0, width, tag, bufs):
+            raw = new(name, [P, PACK, width], F32, tag=tag, bufs=bufs)
+            nc.sync.dma_start(raw[:], rows.rearrange("(p j) c -> p j c", j=PACK)[:, :, c0 : c0 + width])
             return raw
 
-        def round_weight(raw, dst, on_gpsimd):
+        def round_half(src, dst, half):
+            nc.scalar.copy(
+                out=dst.rearrange("p (t m j) -> p m j t", t=PACK, j=PACK)[:, half * 64 : (half + 1) * 64],
+                in_=src.rearrange("p j (m t) -> p m j t", t=PACK),
+            )
+
+        def round_weight(raw, dst):
             for half in range(2):
-                ms = slice(half * 64, (half + 1) * 64)
-                o = dst.rearrange("p (t m j) -> p m j t", t=PACK, j=PACK)[:, ms]
-                i = raw[:].rearrange("p j (m t) -> p m j t", t=PACK)[:, ms]
-                if on_gpsimd:
-                    ts = slice(half * 2, (half + 1) * 2)
-                    o = dst.rearrange("p (t m j) -> p t m j", t=PACK, j=PACK)[:, ts]
-                    i = raw[:].rearrange("p j (m t) -> p t m j", t=PACK)[:, ts]
-                    nc.gpsimd.tensor_scalar(out=o, in0=i, scalar1=1.0, scalar2=0.0, op0=ALU.mult, op1=ALU.add)
-                else:
-                    nc.scalar.copy(out=o, in_=i)
+                round_half(raw[:, :, half * 256 : (half + 1) * 256], dst, half)
 
         def quantise(name, src, cols, tag=None):
             codes = new(name + "_c", [P, cols], U32, tag=tag)
@@ -93,48 +85,99 @@ def tile_list_foothold_terrain_blend_kernel(
             nc.vector.quantize_mx(out=codes[:].bitcast(FP8X4), scales=scales[:], in_=src)
             return codes, scales
 
+        def load_scale_rows(tile, scales, r):
+            nc.sync.dma_start(
+                tile[r:P:32, :, :].bitcast(I32),
+                scales[:, r:16:4, :].rearrange("a q t -> q a t").bitcast(I32),
+            )
+
         idx2 = load_list("idx2", offs2)
         load_plane(0)
+        raw_w1_0a = load_weight("raw_w1_0a", w1, 0, 256, "pairs", 1)
         load_plane(1)
-        raw_w1_0 = load_weight("raw_w1_0", w1, 0)
+        raw_w1_0b = load_weight("raw_w1_0b", w1, 256, 256, "raw_w1_0b", 1)
         load_plane(2)
-        raw_wg_00 = load_weight("raw_wg_00", wg[0:KP, :], 0)
+        raw_wg_00 = load_weight("raw_wg_00", wg[0:KP, :], 0, KP, "raw", 4)
         load_plane(3)
-        raw_wg_01 = load_weight("raw_wg_01", wg[KP : 2 * KP, :], 0)
+        raw_wg_01 = load_weight("raw_wg_01", wg[KP : 2 * KP, :], 0, KP, "raw", 4)
         idx = load_list("idx", offs)
         tab_w = []
         for a in range(2):
             tile = new("tab_w%d" % a, [P, T], I32)
             nc.sync.dma_start(tile[:], tab_words[a].rearrange("p t i -> p (t i)").bitcast(I32))
             tab_w.append(tile)
-        for q in range(4):
-            nc.sync.dma_start(
-                tab_sc[32 * q : 32 * q + 4, :, :].bitcast(I32),
-                tab_scales[:, 4 * q : 4 * q + 4, :].rearrange("a r t -> r a t").bitcast(I32),
-            )
-        for q in range(4):
-            nc.sync.dma_start(
-                w2_sc_raw[32 * q : 32 * q + 4, :, :].bitcast(I32),
-                w2_scales[:, 4 * q : 4 * q + 4, :].rearrange("a r t -> r a t").bitcast(I32),
-            )
+            load_scale_rows(tab_sc, tab_scales, 2 * a)
+            load_scale_rows(tab_sc, tab_scales, 2 * a + 1)
+        load_scale_rows(w2_sc_raw, w2_scales, 0)
+        load_scale_rows(w2_sc_raw, w2_scales, 1)
         w2_raw = new("w2_raw", [P, 2, 2 * H], U8)
         nc.sync.dma_start(w2_raw[:].bitcast(I32), w2_words.rearrange("a p c -> p a c").bitcast(I32))
+        load_scale_rows(w2_sc_raw, w2_scales, 2)
+        load_scale_rows(w2_sc_raw, w2_scales, 3)
         idx3 = load_list("idx3", offs3)
+        raw_w1_1 = load_weight("raw_w1_1", w1, KP, KP, "raw", 4)
 
-        stage_a = new("stage_a", [P, 2 * KP * PACK], BF16)
+        stage_a = new("stage_a", [P, KP * PACK], BF16)
+        stage_d = new("stage_d", [P, KP * PACK], BF16)
         stage_b = new("stage_b", [P, KP * PACK], BF16, tag="stage", bufs=2)
-        for t in range(PACK):
-            scatter_plane(t)
-            round_plane(t)
-            if t == 0:
-                round_weight(raw_w1_0, stage_a[:, 0 : KP * PACK], True)
-            if t == 1:
-                round_weight(raw_wg_00, stage_a[:, KP * PACK :], True)
-        round_weight(raw_wg_01, stage_b[:], True)
+        round_half(raw_w1_0a[:], stage_a[:], 0)
+        pairs = new("pairs", [P, 2, 2, BANK, 2], BF16)
+        page_bf = [new("page_bf%d" % h, [P, BANK, PACK], BF16) for h in range(2)]
 
-        raw_w1_1 = load_weight("raw_w1_1", w1, 1)
-        raw_wg_10 = load_weight("raw_wg_10", wg[0:KP, :], 1)
-        raw_wg_11 = load_weight("raw_wg_11", wg[KP : 2 * KP, :], 1)
+        def round_plane(t, halves):
+            nc.scalar.copy(
+                out=pairs[:, halves, t // 2, :, t % 2],
+                in_=page[t][:].rearrange("p (h c) -> p h c", h=2)[:, halves, :],
+            )
+
+        def weave_page(h):
+            nc.scalar.copy(
+                out=page_bf[h][:].bitcast(F32),
+                in_=pairs[:, h].rearrange("p u c e -> p u (c e)").bitcast(F32).rearrange("p u c -> p c u"),
+            )
+
+        scatter_plane(0)
+        round_plane(0, slice(0, 2))
+        round_half(raw_w1_0b[:], stage_a[:], 1)
+        scatter_plane(1)
+        round_plane(1, slice(0, 2))
+        scatter_plane(2)
+        round_plane(2, slice(0, 2))
+        round_weight(raw_wg_00, stage_d[:])
+        scatter_plane(3)
+        for h in range(2):
+            round_plane(3, slice(h, h + 1))
+            weave_page(h)
+
+        raw_wg_10 = load_weight("raw_wg_10", wg[0:KP, :], KP, KP, "raw", 4)
+
+        c, s = quantise("w1_0", stage_a[:], KP, tag="patch3")
+        w1_q = [(c[:], s[:]), None]
+        c, s = quantise("wg00", stage_d[:], KP)
+        wg_q = [[(c[:], s[:]), None], [None, None]]
+
+        v_w = new("v_w", [P, 2, S], U32)
+        v_s = new("v_s", [P, 2, S], U8)
+        nc.vector.tensor_copy(v_w[:, 0, :], tab_w[0][:].bitcast(U32).indirect(idx[:]))
+        page_c = new("page_c", [P, T2], U32, tag="tab_w0")
+        page_s = new("page_s", [P, T2], U8)
+        page_q = []
+        for h in range(2):
+            cols = slice(h * BANK, (h + 1) * BANK)
+            nc.vector.quantize_mx(
+                out=page_c[:, cols].bitcast(FP8X4),
+                scales=page_s[:, cols],
+                in_=page_bf[h][:].rearrange("p c t -> p (c t)"),
+            )
+            page_q.append((page_c[:, cols], page_s[:, cols]))
+        nc.vector.tensor_copy(v_w[:, 1, :], tab_w[1][:].bitcast(U32).indirect(idx[:]))
+        for a in range(2):
+            nc.vector.tensor_copy(v_s[:, a, :], tab_sc[:, a, :].indirect(idx[:]))
+        round_weight(raw_wg_01, stage_b[:])
+        c, s = quantise("wg01", stage_b[:], KP, tag="tab_sc")
+        wg_q[0][1] = (c[:], s[:])
+
+        raw_wg_11 = load_weight("raw_wg_11", wg[KP : 2 * KP, :], KP, KP, "raw", 4)
         wo_w = new("wo_w", [P, 2, N], I32)
         nc.sync.dma_start(wo_w[:], wo_words.rearrange("a p c i -> p a (c i)").bitcast(I32))
         for q in range(4):
@@ -145,34 +188,15 @@ def tile_list_foothold_terrain_blend_kernel(
         with nc.allow_non_contiguous_dma(reason="one bias value for each partition"):
             nc.sync.dma_start(bias[:], bo.rearrange("(c p) -> p c", p=P))
 
-        first_c, first_s = quantise("first", stage_a[:], 2 * KP)
-        w1_q = [(first_c[:, 0:KP], first_s[:, 0:KP]), None]
-        wg_q = [[(first_c[:, KP:], first_s[:, KP:]), None], [None, None]]
-
-        v_w = new("v_w", [P, 2, S], U32)
-        v_s = new("v_s", [P, 2, S], U8)
-        nc.vector.tensor_copy(v_w[:, 0, :], tab_w[0][:].bitcast(U32).indirect(idx[:]))
-        page_q = []
-        for h in range(2):
-            c, s = quantise(
-                "page%d" % h, page_bf[h][:].rearrange("p c t -> p (c t)"), BANK, tag="tab_w0" if h == 1 else None
-            )
-            page_q.append((c, s))
-        nc.vector.tensor_copy(v_w[:, 1, :], tab_w[1][:].bitcast(U32).indirect(idx[:]))
-        c, s = quantise("wg01", stage_b[:], KP)
-        wg_q[0][1] = (c[:], s[:])
-        for a in range(2):
-            nc.vector.tensor_copy(v_s[:, a, :], tab_sc[:, a, :].indirect(idx[:]))
-
         w2_w = new("w2_w", [P, 2, 2 * H], U8)
         w2_s = new("w2_s", [P, 2, H], U8)
         nc.vector.tensor_copy(
-            out=w2_w[:].bitcast(U16).rearrange("p a (b t g m) -> p (a b) g t m", b=2, t=PACK, m=8),
-            in_=w2_raw[:].bitcast(U16).rearrange("p a (b g m t) -> p (a b) g t m", b=2, t=PACK, m=8),
-        )
-        nc.vector.tensor_copy(
             out=w2_s[:].rearrange("p a (b t g m) -> p (a b) g t m", b=2, t=PACK, m=16),
             in_=w2_sc_raw[:].rearrange("p a (b g m t) -> p (a b) g t m", b=2, t=PACK, m=16),
+        )
+        nc.vector.tensor_copy(
+            out=w2_w[:].bitcast(U16).rearrange("p a (b t g m) -> p (a b) g t m", b=2, t=PACK, m=8),
+            in_=w2_raw[:].bitcast(U16).rearrange("p a (b g m t) -> p (a b) g t m", b=2, t=PACK, m=8),
         )
 
         a_rows = {}
@@ -180,15 +204,15 @@ def tile_list_foothold_terrain_blend_kernel(
 
         def make_a(b, t):
             cols = slice(t * P, (t + 1) * P)
-            tile = new("a%d%d" % (b, t), [P, T2], F32, tag="a", bufs=8)
+            tile = new("a%d%d" % (b, t), [P, T2], F32)
             for h in range(2):
                 acc = psum.tile([P, BANK], F32, name="acc", tag="s_bank")
                 nc.tensor.matmul_mx(
                     out=acc[:],
                     lhsT=w1_q[b][0][:, cols].bitcast(FP8X4),
                     lhsT_scale=w1_q[b][1][:, cols],
-                    rhs=page_q[h][0][:].bitcast(FP8X4),
-                    rhs_scale=page_q[h][1][:],
+                    rhs=page_q[h][0].bitcast(FP8X4),
+                    rhs_scale=page_q[h][1],
                     start=True,
                     stop=True,
                 )
@@ -208,7 +232,7 @@ def tile_list_foothold_terrain_blend_kernel(
                     start=(a == 0),
                     stop=(a == 1),
                 )
-            tile = new("trust%d%d" % (b, t), [P, S], F32, tag="trust", bufs=8)
+            tile = new("trust%d%d" % (b, t), [P, S], F32, tag="trust", bufs=6)
             nc.scalar.activation(out=tile[:], in_=acc[:], func=ACT.Sigmoid)
             trust[b, t] = tile
 
@@ -258,27 +282,29 @@ def tile_list_foothold_terrain_blend_kernel(
             )
             return quantise("z%d%d" % (b, h), z_bf[:], width)
 
-        for t in range(PACK):
-            make_a(0, t)
-        for t in range(PACK):
-            make_trust(0, t)
+        def make_rows(b):
+            make_a(b, 0)
+            make_a(b, 1)
+            make_trust(b, 0)
+            make_trust(b, 1)
+            for t in range(2, PACK):
+                make_a(b, t)
+                make_trust(b, t)
+
+        make_rows(0)
         cell0, rest0, pick0 = blend(0, 1)
 
-        round_weight(raw_w1_1, stage_a[:, 0 : KP * PACK], False)
-        c, s = quantise("w1_1", stage_a[:, 0 : KP * PACK], KP)
-        w1_q[1] = (c[:], s[:])
-        round_weight(raw_wg_10, stage_a[:, KP * PACK :], False)
-        c, s = quantise("wg10", stage_a[:, KP * PACK :], KP)
-        wg_q[1][0] = (c[:], s[:])
-        stage_c = new("stage_c", [P, KP * PACK], BF16, tag="stage", bufs=2)
-        round_weight(raw_wg_11, stage_c[:], False)
+        late = []
+        for name, raw, tag in (("w1_1", raw_w1_1, "stage_a"), ("wg10", raw_wg_10, "stage_d"), ("wg11", raw_wg_11, "page_bf0")):
+            stage = new("stage_" + name, [P, KP * PACK], BF16, tag=tag)
+            round_weight(raw, stage[:])
+            c, s = quantise(name, stage[:], KP)
+            late.append((c[:], s[:]))
+        w1_q[1] = late[0]
+        wg_q[1] = late[1:]
         z0 = finish_z(0, 0, S, cell0[0], rest0)
-        c, s = quantise("wg11", stage_c[:], KP)
-        wg_q[1][1] = (c[:], s[:])
 
-        for t in range(PACK):
-            make_a(1, t)
-            make_trust(1, t)
+        make_rows(1)
         cell1, rest1, pick1 = blend(1, 2)
 
         half = S // 2

@@ -18,8 +18,17 @@ ACT = mybir.ActivationFunctionType
 
 P = 128
 PACK = 4
-KP = P * PACK
+PASS = P * PACK
 BANK = 512
+QUAD = 32
+ROWS = 4
+BLOCKS = 16
+PER_COLUMN = 16
+PIECE = PASS // 2
+SIDE = S // 2
+OUT_TILES = N // P
+RAW_BUFS = 3
+TRUST_BUFS = 6
 
 
 def tile_list_foothold_terrain_blend_kernel(
@@ -29,105 +38,125 @@ def tile_list_foothold_terrain_blend_kernel(
     with ExitStack() as ctx:
         lists = ctx.enter_context(tc.tile_pool(name="lists", bufs=1))
         sb = ctx.enter_context(tc.tile_pool(name="sb", bufs=1))
-        psum = ctx.enter_context(tc.psum_pool(name="psum", bufs=4))
+        psum = ctx.enter_context(tc.psum_pool(name="psum", bufs=1))
 
-        def new(name, shape, dtype, tag=None, bufs=1):
-            return sb.tile(shape, dtype, name=name, tag=tag or name, bufs=bufs, align_bytes=64)
+        def new(name, shape, dtype, on=None, bufs=1):
+            return sb.tile(shape, dtype, name=name, tag=on or name, bufs=bufs, align_bytes=64)
 
-        def load_list(name, src):
-            tile = lists.tile([P, S // 16], U16, name=name)
-            nc.sync.dma_start(tile[:], src)
-            return tile
+        def bank(kind, number, width):
+            return psum.tile([P, width], F32, name="acc", tag="%s_bank%d" % (kind, number))
 
-        tab_sc = new("tab_sc", [P, 2, T], U8)
-        w2_sc_raw = new("w2_sc_raw", [P, 2, H], U8)
-        wo_sc = new("wo_sc", [P, N], U8)
-        nc.vector.memset(tab_sc[:].rearrange("p a t -> p (a t)").bitcast(I32), 0)
-        nc.vector.memset(w2_sc_raw[:].rearrange("p a t -> p (a t)").bitcast(I32), 0)
-        nc.vector.memset(wo_sc[:].bitcast(I32), 0)
+        tab_planes = new("tab_planes", [P, T], U8)
+        w2_planes_raw = new("w2_planes_raw", [P, 2, H], U8)
+        wo_planes = new("wo_planes", [P, N], U8)
+        v_plane1 = new("v_plane1", [P, S], U8)
+        nc.vector.memset(tab_planes[:].bitcast(I32), 0)
+        nc.vector.memset(v_plane1[:].bitcast(I32), 0)
+        nc.vector.memset(w2_planes_raw[:].rearrange("p ps c -> p (ps c)").bitcast(I32), 0)
+        nc.vector.memset(wo_planes[:].bitcast(I32), 0)
 
         warm = new("warm", [P, 2], F32)
         nc.gpsimd.memset(warm[:, 0:1], 0.0)
         nc.scalar.activation(out=warm[:, 1:2], in_=warm[:, 0:1], func=ACT.Sigmoid)
 
-        base_v = base.rearrange("(p t) c -> p t c", t=PACK)
-        xs_v = xs.rearrange("(p t) c -> p t c", t=PACK)
+        def load_list(name, src):
+            tile = lists.tile([P, S // PER_COLUMN], U16, name=name)
+            nc.sync.dma_start(tile[:], src)
+            return tile
+
         page = [None] * PACK
         patch = [None] * PACK
 
-        def load_plane(t):
+        def load_grid_rows(t):
             page[t] = new("page%d" % t, [P, T2], F32)
             patch[t] = new("patch%d" % t, [P, S], F32)
-            nc.sync.dma_start(page[t][:], base_v[:, t, :])
-            nc.sync.dma_start(patch[t][:], xs_v[:, t, :])
+            nc.sync.dma_start(page[t][:], base.rearrange("(p t) c -> p t c", t=PACK)[:, t, :])
+            nc.sync.dma_start(patch[t][:], xs.rearrange("(p t) c -> p t c", t=PACK)[:, t, :])
 
-        def scatter_plane(t):
-            nc.vector.tensor_copy(page[t][:].indirect(idx2[:]), patch[t][:])
-
-        def load_weight(name, rows, c0, width, tag, bufs):
-            raw = new(name, [P, PACK, width], F32, tag=tag, bufs=bufs)
-            nc.sync.dma_start(raw[:], rows.rearrange("(p j) c -> p j c", j=PACK)[:, :, c0 : c0 + width])
+        def load_weight(name, rows, first, width, on=None, bufs=1):
+            raw = new(name, [P, PACK, width], F32, on=on, bufs=bufs)
+            nc.sync.dma_start(raw[:], rows.rearrange("(p j) c -> p j c", j=PACK)[:, :, first : first + width])
             return raw
 
-        def round_half(src, dst, half):
-            nc.scalar.copy(
-                out=dst.rearrange("p (t m j) -> p m j t", t=PACK, j=PACK)[:, half * 64 : (half + 1) * 64],
-                in_=src.rearrange("p j (m t) -> p m j t", t=PACK),
-            )
+        def load_wg(g, ps):
+            rows = wg[ps * PASS : (ps + 1) * PASS, :]
+            return load_weight("raw_wg%d%d" % (g, ps), rows, g * PASS, PASS, on="raw_wg", bufs=RAW_BUFS)
 
-        def round_weight(raw, dst):
-            for half in range(2):
-                round_half(raw[:, :, half * 256 : (half + 1) * 256], dst, half)
+        def load_table_words(ps):
+            tile = new("tab_w%d" % ps, [P, T], I32)
+            nc.sync.dma_start(tile[:], tab_words[ps].rearrange("p c i -> p (c i)").bitcast(I32))
+            return tile
 
-        def quantise(name, src, cols, tag=None):
-            codes = new(name + "_c", [P, cols], U32, tag=tag)
-            scales = new(name + "_s", [P, cols], U8)
-            nc.vector.quantize_mx(out=codes[:].bitcast(FP8X4), scales=scales[:], in_=src)
-            return codes, scales
+        def load_table_scale_rows(row):
+            for ps in range(2):
+                nc.sync.dma_start(
+                    tab_planes[ROWS * ps + row : P : QUAD, :].bitcast(I32),
+                    tab_scales[ps, row:BLOCKS:ROWS, :].bitcast(I32),
+                )
 
-        def load_scale_rows(tile, scales, r):
+        def load_w2_scale_rows(row):
             nc.sync.dma_start(
-                tile[r:P:32, :, :].bitcast(I32),
-                scales[:, r:16:4, :].rearrange("a q t -> q a t").bitcast(I32),
+                w2_planes_raw[row:P:QUAD, :, :].bitcast(I32),
+                w2_scales[:, row:BLOCKS:ROWS, :].rearrange("ps quad c -> quad ps c").bitcast(I32),
             )
 
         idx2 = load_list("idx2", offs2)
-        load_plane(0)
-        raw_w1_0a = load_weight("raw_w1_0a", w1, 0, 256, "pairs", 1)
-        load_plane(1)
-        raw_w1_0b = load_weight("raw_w1_0b", w1, 256, 256, "raw_w1_0b", 1)
-        load_plane(2)
-        raw_wg_00 = load_weight("raw_wg_00", wg[0:KP, :], 0, KP, "raw", 4)
-        load_plane(3)
-        raw_wg_01 = load_weight("raw_wg_01", wg[KP : 2 * KP, :], 0, KP, "raw", 4)
+        load_grid_rows(0)
+        raw_w1_0 = [load_weight("raw_w1_00", w1, 0, PIECE, on="pairs"), None]
+        load_grid_rows(1)
+        raw_w1_0[1] = load_weight("raw_w1_01", w1, PIECE, PIECE)
+        load_grid_rows(2)
+        raw_wg00 = load_wg(0, 0)
+        load_grid_rows(3)
         idx = load_list("idx", offs)
-        tab_w = []
-        for a in range(2):
-            tile = new("tab_w%d" % a, [P, T], I32)
-            nc.sync.dma_start(tile[:], tab_words[a].rearrange("p t i -> p (t i)").bitcast(I32))
-            tab_w.append(tile)
-            load_scale_rows(tab_sc, tab_scales, 2 * a)
-            load_scale_rows(tab_sc, tab_scales, 2 * a + 1)
-        load_scale_rows(w2_sc_raw, w2_scales, 0)
-        load_scale_rows(w2_sc_raw, w2_scales, 1)
+        load_table_scale_rows(0)
+        load_table_scale_rows(1)
+        tab_w0 = load_table_words(0)
+        raw_wg01 = load_wg(0, 1)
+        load_table_scale_rows(2)
+        load_table_scale_rows(3)
+        tab_w1 = load_table_words(1)
+        load_w2_scale_rows(0)
+        load_w2_scale_rows(1)
         w2_raw = new("w2_raw", [P, 2, 2 * H], U8)
-        nc.sync.dma_start(w2_raw[:].bitcast(I32), w2_words.rearrange("a p c -> p a c").bitcast(I32))
-        load_scale_rows(w2_sc_raw, w2_scales, 2)
-        load_scale_rows(w2_sc_raw, w2_scales, 3)
+        nc.sync.dma_start(w2_raw[:].bitcast(I32), w2_words.rearrange("ps p c -> p ps c").bitcast(I32))
+        load_w2_scale_rows(2)
+        load_w2_scale_rows(3)
         idx3 = load_list("idx3", offs3)
-        raw_w1_1 = load_weight("raw_w1_1", w1, KP, KP, "raw", 4)
 
-        stage_a = new("stage_a", [P, KP * PACK], BF16)
-        stage_d = new("stage_d", [P, KP * PACK], BF16)
-        stage_b = new("stage_b", [P, KP * PACK], BF16, tag="stage", bufs=2)
-        round_half(raw_w1_0a[:], stage_a[:], 0)
+        def round_piece(copy, src, dst, piece):
+            span = PIECE // PACK
+            copy(
+                out=dst.rearrange("p (t x j) -> p x j t", t=PACK, j=PACK)[:, piece * span : (piece + 1) * span],
+                in_=src.rearrange("p j (x t) -> p x j t", t=PACK),
+            )
+
+        def round_block(raw, dst, copies):
+            for piece, copy in enumerate(copies):
+                round_piece(copy, raw[:, :, piece * PIECE : (piece + 1) * PIECE], dst, piece)
+
+        on_scalar = (nc.scalar.copy, nc.scalar.copy)
+
+        def quantise(name, src, columns, on=None):
+            codes = new(name + "_codes", [P, columns], U32, on=on)
+            plane = new(name + "_plane", [P, columns], U8)
+            nc.vector.quantize_mx(out=codes[:].bitcast(FP8X4), scales=plane[:], in_=src)
+            return codes, plane
+
+        w1_bf = new("w1_bf", [P, PASS * PACK], BF16)
+        wg_bf = new("wg_bf", [P, 2 * PASS * PACK], BF16)
+        round_piece(nc.scalar.copy, raw_w1_0[0][:], w1_bf[:], 0)
+
         pairs = new("pairs", [P, 2, 2, BANK, 2], BF16)
         page_bf = [new("page_bf%d" % h, [P, BANK, PACK], BF16) for h in range(2)]
 
-        def round_plane(t, halves):
+        def scatter_patch(t):
+            nc.vector.tensor_copy(page[t][:].indirect(idx2[:]), patch[t][:])
+
+        def round_page(t, column_halves):
             nc.scalar.copy(
-                out=pairs[:, halves, t // 2, :, t % 2],
-                in_=page[t][:].rearrange("p (h c) -> p h c", h=2)[:, halves, :],
+                out=pairs[:, column_halves, t // 2, :, t % 2],
+                in_=page[t][:].rearrange("p (h c) -> p h c", h=2)[:, column_halves, :],
             )
 
         def weave_page(h):
@@ -136,213 +165,211 @@ def tile_list_foothold_terrain_blend_kernel(
                 in_=pairs[:, h].rearrange("p u c e -> p u (c e)").bitcast(F32).rearrange("p u c -> p c u"),
             )
 
-        scatter_plane(0)
-        round_plane(0, slice(0, 2))
-        round_half(raw_w1_0b[:], stage_a[:], 1)
-        scatter_plane(1)
-        round_plane(1, slice(0, 2))
-        scatter_plane(2)
-        round_plane(2, slice(0, 2))
-        round_weight(raw_wg_00, stage_d[:])
-        scatter_plane(3)
+        scatter_patch(0)
+        round_page(0, slice(0, 2))
+        round_piece(nc.scalar.copy, raw_w1_0[1][:], w1_bf[:], 1)
+        for t in (1, 2):
+            scatter_patch(t)
+            round_page(t, slice(0, 2))
+        round_block(raw_wg00, wg_bf[:, 0 : PASS * PACK], on_scalar)
+        scatter_patch(3)
         for h in range(2):
-            round_plane(3, slice(h, h + 1))
+            round_page(3, slice(h, h + 1))
             weave_page(h)
 
-        raw_wg_10 = load_weight("raw_wg_10", wg[0:KP, :], KP, KP, "raw", 4)
+        codes, plane = quantise("w1_0", w1_bf[:], PASS, on="patch3")
+        w1_q = [(codes[:], plane[:]), None]
 
-        c, s = quantise("w1_0", stage_a[:], KP, tag="patch3")
-        w1_q = [(c[:], s[:]), None]
-        c, s = quantise("wg00", stage_d[:], KP)
-        wg_q = [[(c[:], s[:]), None], [None, None]]
+        v_words = new("v_words", [P, 2, S], U32)
+        v_planes = new("v_planes", [P, S], U8)
+        round_block(raw_wg01, wg_bf[:, PASS * PACK :], (nc.scalar.copy, nc.vector.tensor_copy))
 
-        v_w = new("v_w", [P, 2, S], U32)
-        v_s = new("v_s", [P, 2, S], U8)
-        nc.vector.tensor_copy(v_w[:, 0, :], tab_w[0][:].bitcast(U32).indirect(idx[:]))
-        page_c = new("page_c", [P, T2], U32, tag="tab_w0")
-        page_s = new("page_s", [P, T2], U8)
-        page_q = []
+        nc.vector.tensor_copy(v_words[:, 0, :], tab_w0[:].bitcast(U32).indirect(idx[:]))
+        nc.vector.tensor_copy(v_planes[:], tab_planes[:].indirect(idx[:]))
+        for row in range(ROWS):
+            nc.sync.dma_start(v_plane1[row:P:QUAD, :].bitcast(I32), v_planes[ROWS + row : P : QUAD, :].bitcast(I32))
+        raw_wg10 = load_wg(1, 0)
+        raw_wg11 = load_wg(1, 1)
+
+        page_codes = new("page_codes", [P, T2], U32, on="tab_planes")
+        page_plane = new("page_plane", [P, T2], U8)
         for h in range(2):
-            cols = slice(h * BANK, (h + 1) * BANK)
+            columns = slice(h * BANK, (h + 1) * BANK)
             nc.vector.quantize_mx(
-                out=page_c[:, cols].bitcast(FP8X4),
-                scales=page_s[:, cols],
+                out=page_codes[:, columns].bitcast(FP8X4),
+                scales=page_plane[:, columns],
                 in_=page_bf[h][:].rearrange("p c t -> p (c t)"),
             )
-            page_q.append((page_c[:, cols], page_s[:, cols]))
-        nc.vector.tensor_copy(v_w[:, 1, :], tab_w[1][:].bitcast(U32).indirect(idx[:]))
-        for a in range(2):
-            nc.vector.tensor_copy(v_s[:, a, :], tab_sc[:, a, :].indirect(idx[:]))
-        round_weight(raw_wg_01, stage_b[:])
-        c, s = quantise("wg01", stage_b[:], KP, tag="tab_sc")
-        wg_q[0][1] = (c[:], s[:])
+        nc.vector.tensor_copy(v_words[:, 1, :], tab_w1[:].bitcast(U32).indirect(idx[:]))
+        codes, plane = quantise("wg0", wg_bf[:], 2 * PASS, on="tab_w1")
+        wg_q = [[(codes[:, 0:PASS], plane[:, 0:PASS]), (codes[:, PASS:], plane[:, PASS:])], None]
 
-        raw_wg_11 = load_weight("raw_wg_11", wg[KP : 2 * KP, :], KP, KP, "raw", 4)
+        w2_sorted = new("w2_sorted", [P, 2, 2 * H], U8)
+        nc.vector.tensor_copy(
+            out=w2_sorted[:].bitcast(U16).rearrange("p ps (g t run y) -> p (ps g) run t y", g=2, t=PACK, y=8),
+            in_=w2_raw[:].bitcast(U16).rearrange("p ps (g run y t) -> p (ps g) run t y", g=2, t=PACK, y=8),
+        )
+        w2_planes = new("w2_planes", [P, 2, H], U8)
+        nc.vector.tensor_copy(
+            out=w2_planes[:].rearrange("p ps (g t run y) -> p (ps g) run t y", g=2, t=PACK, y=16),
+            in_=w2_planes_raw[:].rearrange("p ps (g run y t) -> p (ps g) run t y", g=2, t=PACK, y=16),
+        )
+
+        raw_w1_1 = load_weight("raw_w1_1", w1, PASS, PASS)
         wo_w = new("wo_w", [P, 2, N], I32)
-        nc.sync.dma_start(wo_w[:], wo_words.rearrange("a p c i -> p a (c i)").bitcast(I32))
-        for q in range(4):
+        nc.sync.dma_start(wo_w[:], wo_words.rearrange("ps p c i -> p ps (c i)").bitcast(I32))
+        for quad in range(P // QUAD):
             nc.sync.dma_start(
-                wo_sc[32 * q : 32 * q + 8, :].bitcast(I32), wo_scales[:, 4 * q : 4 * q + 4, :].bitcast(I32)
+                wo_planes[QUAD * quad : QUAD * quad + 2 * ROWS, :].bitcast(I32),
+                wo_scales[:, ROWS * quad : ROWS * (quad + 1), :].bitcast(I32),
             )
-        bias = new("bias", [P, N // P], F32)
+        bias = new("bias", [P, OUT_TILES], F32)
         with nc.allow_non_contiguous_dma(reason="one bias value for each partition"):
-            nc.sync.dma_start(bias[:], bo.rearrange("(c p) -> p c", p=P))
-
-        w2_w = new("w2_w", [P, 2, 2 * H], U8)
-        w2_s = new("w2_s", [P, 2, H], U8)
-        nc.vector.tensor_copy(
-            out=w2_s[:].rearrange("p a (b t g m) -> p (a b) g t m", b=2, t=PACK, m=16),
-            in_=w2_sc_raw[:].rearrange("p a (b g m t) -> p (a b) g t m", b=2, t=PACK, m=16),
-        )
-        nc.vector.tensor_copy(
-            out=w2_w[:].bitcast(U16).rearrange("p a (b t g m) -> p (a b) g t m", b=2, t=PACK, m=8),
-            in_=w2_raw[:].bitcast(U16).rearrange("p a (b g m t) -> p (a b) g t m", b=2, t=PACK, m=8),
-        )
+            nc.sync.dma_start(bias[:], bo.rearrange("(o p) -> p o", p=P))
 
         a_rows = {}
         trust = {}
 
-        def make_a(b, t):
-            cols = slice(t * P, (t + 1) * P)
-            tile = new("a%d%d" % (b, t), [P, T2], F32)
+        def make_a(g, t, first_bank):
+            rows = slice(t * P, (t + 1) * P)
+            tile = new("a%d%d" % (g, t), [P, T2], F32)
             for h in range(2):
-                acc = psum.tile([P, BANK], F32, name="acc", tag="s_bank")
+                columns = slice(h * BANK, (h + 1) * BANK)
+                acc = bank("s", first_bank + h, BANK)
                 nc.tensor.matmul_mx(
                     out=acc[:],
-                    lhsT=w1_q[b][0][:, cols].bitcast(FP8X4),
-                    lhsT_scale=w1_q[b][1][:, cols],
-                    rhs=page_q[h][0].bitcast(FP8X4),
-                    rhs_scale=page_q[h][1],
+                    lhsT=w1_q[g][0][:, rows].bitcast(FP8X4),
+                    lhsT_scale=w1_q[g][1][:, rows],
+                    rhs=page_codes[:, columns].bitcast(FP8X4),
+                    rhs_scale=page_plane[:, columns],
                     start=True,
                     stop=True,
                 )
-                nc.scalar.copy(out=tile[:, h * BANK : (h + 1) * BANK], in_=acc[:])
-            a_rows[b, t] = tile
+                nc.scalar.copy(out=tile[:, columns], in_=acc[:])
+            a_rows[g, t] = tile
 
-        def make_trust(b, t):
-            cols = slice(t * P, (t + 1) * P)
-            acc = psum.tile([P, BANK], F32, name="acc", tag="s_bank")
-            for a in range(2):
+        def make_trust(g, t, number):
+            rows = slice(t * P, (t + 1) * P)
+            acc = bank("s", number, BANK)
+            for ps in range(2):
                 nc.tensor.matmul_mx(
                     out=acc[:],
-                    lhsT=wg_q[b][a][0][:, cols].bitcast(FP8X4),
-                    lhsT_scale=wg_q[b][a][1][:, cols],
-                    rhs=v_w[:, a, :].bitcast(FP8X4),
-                    rhs_scale=v_s[:, a, :],
-                    start=(a == 0),
-                    stop=(a == 1),
+                    lhsT=wg_q[g][ps][0][:, rows].bitcast(FP8X4),
+                    lhsT_scale=wg_q[g][ps][1][:, rows],
+                    rhs=v_words[:, ps, :].bitcast(FP8X4),
+                    rhs_scale=v_planes[ROWS * ps : P, :],
+                    start=(ps == 0),
+                    stop=(ps == 1),
                 )
-            tile = new("trust%d%d" % (b, t), [P, S], F32, tag="trust", bufs=6)
+            tile = new("trust%d%d" % (g, t), [P, S], F32, on="trust", bufs=TRUST_BUFS)
             nc.scalar.activation(out=tile[:], in_=acc[:], func=ACT.Sigmoid)
-            trust[b, t] = tile
+            trust[g, t] = tile
 
-        def make_code(b, t):
-            c0 = b * KP + t * P
-            acc = psum.tile([P, BANK], F32, name="acc", tag="v_bank")
-            for a in range(2):
+        def make_b(g, t):
+            first = g * PASS + t * P
+            acc = bank("v", t, BANK)
+            for ps in range(2):
                 nc.tensor.matmul_mx(
                     out=acc[:],
-                    lhsT=w2_w[:, a, 2 * c0 : 2 * (c0 + P)].bitcast(FP4X4),
-                    lhsT_scale=w2_s[:, a, c0 : c0 + P],
-                    rhs=v_w[:, a, :].bitcast(FP8X4),
-                    rhs_scale=v_s[:, a, :],
-                    start=(a == 0),
-                    stop=(a == 1),
+                    lhsT=w2_sorted[:, ps, 2 * first : 2 * (first + P)].bitcast(FP4X4),
+                    lhsT_scale=w2_planes[:, ps, first : first + P],
+                    rhs=v_words[:, ps, :].bitcast(FP8X4),
+                    rhs_scale=(v_planes, v_plane1)[ps][:],
+                    start=(ps == 0),
+                    stop=(ps == 1),
                 )
             return acc
 
-        def blend(b, parts):
-            width = S // parts
-            cell = [new("cell%d%d" % (b, h), [P, PACK, width], F32) for h in range(parts)]
-            rest = new("rest%d" % b, [P, PACK, S], F32)
-            codes = [make_code(b, t) for t in range(PACK)]
+        def pick_cells(g, t, weighted, first, width):
+            nc.vector.tensor_tensor(
+                out=weighted[:, t, :],
+                in0=a_rows[g, t][:].indirect(idx3[:, first // PER_COLUMN : (first + width) // PER_COLUMN]),
+                in1=trust[g, t][:, first : first + width],
+                op=ALU.mult,
+            )
 
-            def pick(t, h):
-                nc.vector.tensor_tensor(
-                    out=cell[h][:, t, :],
-                    in0=a_rows[b, t][:].indirect(idx3[:, h * width // 16 : (h + 1) * width // 16]),
-                    in1=trust[b, t][:, h * width : (h + 1) * width],
-                    op=ALU.mult,
-                )
-
+        def blend(g, weighted, width):
+            rest = new("rest%d" % g, [P, PACK, S], F32)
+            b_banks = [make_b(g, t) for t in range(PACK)]
             for t in range(PACK):
                 nc.vector.scalar_tensor_tensor(
-                    out=rest[:, t, :], in0=trust[b, t][:], scalar=1.0, in1=codes[t][:], op0=ALU.subtract, op1=ALU.mult
+                    out=rest[:, t, :], in0=trust[g, t][:], scalar=1.0, in1=b_banks[t][:], op0=ALU.subtract, op1=ALU.mult
                 )
-                pick(t, 0)
-            return cell, rest, pick
+                pick_cells(g, t, weighted, 0, width)
+            return rest
 
-        def finish_z(b, h, width, cell, rest):
-            z_bf = new("z_bf%d%d" % (b, h), [P, width * PACK], BF16, tag="stage", bufs=2)
+        def finish_z(name, weighted, rest, first, width, on):
+            z_bf = new(name + "_bf", [P, width * PACK], BF16, on=on)
             nc.vector.tensor_tensor(
-                out=z_bf[:].rearrange("p (c i t) -> p c t i", i=2, t=PACK),
-                in0=cell[:].rearrange("p t (c i) -> p c t i", i=2),
-                in1=rest[:, :, h * width : (h + 1) * width].rearrange("p t (c i) -> p c t i", i=2),
+                out=z_bf[:].rearrange("p (c e t) -> p c t e", e=2, t=PACK),
+                in0=weighted[:].rearrange("p t (c e) -> p c t e", e=2),
+                in1=rest[:, :, first : first + width].rearrange("p t (c e) -> p c t e", e=2),
                 op=ALU.subtract,
             )
-            return quantise("z%d%d" % (b, h), z_bf[:], width)
+            return quantise(name, z_bf[:], width)
 
-        def make_rows(b):
-            make_a(b, 0)
-            make_a(b, 1)
-            make_trust(b, 0)
-            make_trust(b, 1)
-            for t in range(2, PACK):
-                make_a(b, t)
-                make_trust(b, t)
-
-        make_rows(0)
-        cell0, rest0, pick0 = blend(0, 1)
+        make_a(0, 0, 0)
+        make_a(0, 1, 2)
+        for t in (2, 3):
+            make_trust(0, 2 * t - 4, 0)
+            make_trust(0, 2 * t - 3, 1)
+            make_a(0, t, 2)
+        weighted0 = new("weighted0", [P, PACK, S], F32)
+        rest0 = blend(0, weighted0, S)
 
         late = []
-        for name, raw, tag in (("w1_1", raw_w1_1, "stage_a"), ("wg10", raw_wg_10, "stage_d"), ("wg11", raw_wg_11, "page_bf0")):
-            stage = new("stage_" + name, [P, KP * PACK], BF16, tag=tag)
-            round_weight(raw, stage[:])
-            c, s = quantise(name, stage[:], KP)
-            late.append((c[:], s[:]))
-        w1_q[1] = late[0]
-        wg_q[1] = late[1:]
-        z0 = finish_z(0, 0, S, cell0[0], rest0)
+        for name, raw, on in (("wg10", raw_wg10, "page_bf1"), ("wg11", raw_wg11, None), ("w1_1", raw_w1_1, "w1_bf")):
+            rounded = new(name + "_bf", [P, PASS * PACK], BF16, on=on)
+            round_block(raw, rounded[:], on_scalar)
+            codes, plane = quantise(name, rounded[:], PASS)
+            late.append((codes[:], plane[:]))
+        wg_q[1] = late[0:2]
+        w1_q[1] = late[2]
+        z0_codes, z0_plane = finish_z("z0", weighted0, rest0, 0, S, "wg11_bf")
 
-        make_rows(1)
-        cell1, rest1, pick1 = blend(1, 2)
+        for t in range(PACK):
+            make_trust(1, t, t)
+        for t in range(PACK):
+            make_a(1, t, 2 * (t % 2))
+        weighted1 = [new("weighted1%d" % side, [P, PACK, SIDE], F32) for side in range(2)]
+        rest1 = blend(1, weighted1[0], SIDE)
 
-        half = S // 2
-        outs = [
-            [psum.tile([P, half], F32, name="acc", tag=tag) for c in range(N // P)] for tag in ("v_bank", "s_bank")
-        ]
+        sums = [[bank(kind, o, SIDE) for o in range(OUT_TILES)] for kind in ("v", "s")]
 
-        def read_out(b, h, codes, scales):
-            for c in range(N // P):
-                cols = slice(c * P, (c + 1) * P)
+        def read_out(g, side, codes, plane):
+            for o in range(OUT_TILES):
+                rows = slice(o * P, (o + 1) * P)
                 nc.tensor.matmul_mx(
-                    out=outs[h][c][:],
-                    lhsT=wo_w[:, b, cols].bitcast(FP8X4),
-                    lhsT_scale=wo_sc[4 * b : P, cols],
+                    out=sums[side][o][:],
+                    lhsT=wo_w[:, g, rows].bitcast(FP8X4),
+                    lhsT_scale=wo_planes[ROWS * g : P, rows],
                     rhs=codes.bitcast(FP8X4),
-                    rhs_scale=scales,
-                    start=(b == 0),
-                    stop=(b == 1),
+                    rhs_scale=plane,
+                    start=(g == 0),
+                    stop=(g == 1),
                 )
 
-        def store(h):
-            for c in range(N // P):
-                res = new("res%d%d" % (h, c), [P, half], F32)
-                if h == 1 and c == 1:
+        def store(side, vector_tiles):
+            for o in range(OUT_TILES):
+                result = new("result%d%d" % (side, o), [P, SIDE], F32)
+                if o < vector_tiles:
                     nc.vector.tensor_scalar(
-                        out=res[:], in0=outs[h][c][:], scalar1=bias[:, c : c + 1], scalar2=None, op0=ALU.add
+                        out=result[:], in0=sums[side][o][:], scalar1=bias[:, o : o + 1], scalar2=None, op0=ALU.add
                     )
                 else:
-                    nc.scalar.activation(out=res[:], in_=outs[h][c][:], func=ACT.Identity, bias=bias[:, c : c + 1])
-                nc.sync.dma_start(out[c * P : (c + 1) * P, h * half : (h + 1) * half], res[:])
+                    nc.scalar.activation(
+                        out=result[:], in_=sums[side][o][:], func=ACT.Identity, bias=bias[:, o : o + 1]
+                    )
+                nc.sync.dma_start(out[o * P : (o + 1) * P, side * SIDE : (side + 1) * SIDE], result[:])
 
-        for h in range(2):
-            read_out(0, h, z0[0][:, h * half : (h + 1) * half], z0[1][:, h * half : (h + 1) * half])
-        c, s = finish_z(1, 0, half, cell1[0], rest1)
-        read_out(1, 0, c[:], s[:])
-        store(0)
+        for side in range(2):
+            columns = slice(side * SIDE, (side + 1) * SIDE)
+            read_out(0, side, z0_codes[:, columns], z0_plane[:, columns])
+        codes, plane = finish_z("z10", weighted1[0], rest1, 0, SIDE, "page_bf0")
+        read_out(1, 0, codes[:], plane[:])
+        store(0, 0)
         for t in range(PACK):
-            pick1(t, 1)
-        c, s = finish_z(1, 1, half, cell1[1], rest1)
-        read_out(1, 1, c[:], s[:])
-        store(1)
+            pick_cells(1, t, weighted1[1], SIDE, SIDE)
+        codes, plane = finish_z("z11", weighted1[1], rest1, SIDE, SIDE, "page_bf1")
+        read_out(1, 1, codes[:], plane[:])
+        store(1, 2)

@@ -43,20 +43,20 @@ def tile_list_foothold_terrain_blend_kernel(
         def new(name, shape, dtype, on=None, bufs=1):
             return sb.tile(shape, dtype, name=name, tag=on or name, bufs=bufs, align_bytes=64)
 
-        def bank(kind, number, width):
-            return psum.tile([P, width], F32, name="acc", tag="%s_bank%d" % (kind, number))
+        def bank(tag, shape):
+            return psum.tile(shape, F32, name="acc", tag=tag)
 
         tab_planes = new("tab_planes", [P, T], U8)
-        w2_planes_raw = new("w2_planes_raw", [P, 2, H], U8)
+        w2_planes = new("w2_planes", [P, 2, H], U8)
         wo_planes = new("wo_planes", [P, N], U8)
         v_plane1 = new("v_plane1", [P, S], U8)
         nc.vector.memset(tab_planes[:].bitcast(I32), 0)
+        nc.vector.memset(w2_planes[:].rearrange("p ps c -> p (ps c)").bitcast(I32), 0)
         nc.vector.memset(v_plane1[:].bitcast(I32), 0)
-        nc.vector.memset(w2_planes_raw[:].rearrange("p ps c -> p (ps c)").bitcast(I32), 0)
         nc.vector.memset(wo_planes[:].bitcast(I32), 0)
 
         warm = new("warm", [P, 2], F32)
-        nc.gpsimd.memset(warm[:, 0:1], 0.0)
+        nc.vector.memset(warm[:, 0:1], 0.0)
         nc.scalar.activation(out=warm[:, 1:2], in_=warm[:, 0:1], func=ACT.Sigmoid)
 
         def load_list(name, src):
@@ -67,62 +67,51 @@ def tile_list_foothold_terrain_blend_kernel(
         page = [None] * PACK
         patch = [None] * PACK
 
-        def load_grid_rows(t):
+        def load_page(t):
             page[t] = new("page%d" % t, [P, T2], F32)
-            patch[t] = new("patch%d" % t, [P, S], F32)
             nc.sync.dma_start(page[t][:], base.rearrange("(p t) c -> p t c", t=PACK)[:, t, :])
+
+        def load_patch(t):
+            patch[t] = new("patch%d" % t, [P, S], F32)
             nc.sync.dma_start(patch[t][:], xs.rearrange("(p t) c -> p t c", t=PACK)[:, t, :])
 
-        def load_weight(name, rows, first, width, on=None, bufs=1):
-            raw = new(name, [P, PACK, width], F32, on=on, bufs=bufs)
+        def load_weight(name, rows, first, width, on=None):
+            raw = new(name, [P, PACK, width], F32, on=on)
             nc.sync.dma_start(raw[:], rows.rearrange("(p j) c -> p j c", j=PACK)[:, :, first : first + width])
             return raw
 
         def load_wg(g, ps):
-            rows = wg[ps * PASS : (ps + 1) * PASS, :]
-            return load_weight("raw_wg%d%d" % (g, ps), rows, g * PASS, PASS, on="raw_wg", bufs=RAW_BUFS)
+            return load_weight("raw_wg%d%d" % (g, ps), wg[ps * PASS : (ps + 1) * PASS, :], g * PASS, PASS)
 
         def load_table_words(ps):
             tile = new("tab_w%d" % ps, [P, T], I32)
             nc.sync.dma_start(tile[:], tab_words[ps].rearrange("p c i -> p (c i)").bitcast(I32))
             return tile
 
-        def load_table_scale_rows(row):
+        def load_table_scale_rows(queue, row):
             for ps in range(2):
-                nc.sync.dma_start(
+                queue.dma_start(
                     tab_planes[ROWS * ps + row : P : QUAD, :].bitcast(I32),
                     tab_scales[ps, row:BLOCKS:ROWS, :].bitcast(I32),
                 )
 
-        def load_w2_scale_rows(row):
-            nc.sync.dma_start(
-                w2_planes_raw[row:P:QUAD, :, :].bitcast(I32),
+        def load_w2_scale_rows(queue, row):
+            queue.dma_start(
+                w2_planes[row:P:QUAD, :, :].bitcast(I32),
                 w2_scales[:, row:BLOCKS:ROWS, :].rearrange("ps quad c -> quad ps c").bitcast(I32),
             )
 
-        idx2 = load_list("idx2", offs2)
-        load_grid_rows(0)
-        raw_w1_0 = [load_weight("raw_w1_00", w1, 0, PIECE, on="pairs"), None]
-        load_grid_rows(1)
-        raw_w1_0[1] = load_weight("raw_w1_01", w1, PIECE, PIECE)
-        load_grid_rows(2)
-        raw_wg00 = load_wg(0, 0)
-        load_grid_rows(3)
-        idx = load_list("idx", offs)
-        load_table_scale_rows(0)
-        load_table_scale_rows(1)
-        tab_w0 = load_table_words(0)
-        raw_wg01 = load_wg(0, 1)
-        load_table_scale_rows(2)
-        load_table_scale_rows(3)
-        tab_w1 = load_table_words(1)
-        load_w2_scale_rows(0)
-        load_w2_scale_rows(1)
-        w2_raw = new("w2_raw", [P, 2, 2 * H], U8)
-        nc.sync.dma_start(w2_raw[:].bitcast(I32), w2_words.rearrange("ps p c -> p ps c").bitcast(I32))
-        load_w2_scale_rows(2)
-        load_w2_scale_rows(3)
-        idx3 = load_list("idx3", offs3)
+        def load_wo_scale_rows(queue, quad):
+            queue.dma_start(
+                wo_planes[QUAD * quad : QUAD * quad + 2 * ROWS, :].bitcast(I32),
+                wo_scales[:, ROWS * quad : ROWS * (quad + 1), :].bitcast(I32),
+            )
+
+        def quantise(name, src, columns, on=None):
+            codes = new(name + "_codes", [P, columns], U32, on=on)
+            plane = new(name + "_plane", [P, columns], U8)
+            nc.vector.quantize_mx(out=codes[:].bitcast(FP8X4), scales=plane[:], in_=src)
+            return codes, plane
 
         def round_piece(copy, src, dst, piece):
             span = PIECE // PACK
@@ -131,24 +120,52 @@ def tile_list_foothold_terrain_blend_kernel(
                 in_=src.rearrange("p j (x t) -> p x j t", t=PACK),
             )
 
-        def round_block(raw, dst, copies):
-            for piece, copy in enumerate(copies):
-                round_piece(copy, raw[:, :, piece * PIECE : (piece + 1) * PIECE], dst, piece)
+        def dealt(name, copy, raw, on=None):
+            tile = new(name, [P, PASS * PACK], BF16, on=on)
+            copy(
+                out=tile[:].rearrange("p (t x j) -> p x j t", t=PACK, j=PACK),
+                in_=raw[:].rearrange("p j (x t) -> p x j t", t=PACK),
+            )
+            return tile
 
-        on_scalar = (nc.scalar.copy, nc.scalar.copy)
+        def finish_z(name, picked, left, first, width, on):
+            z_bf = new(name + "_bf", [P, width * PACK], BF16, on=on)
+            nc.vector.tensor_tensor(
+                out=z_bf[:].rearrange("p (c e t) -> p c t e", e=2, t=PACK),
+                in0=picked.rearrange("p t (c e) -> p c t e", e=2),
+                in1=left[:, :, first : first + width].rearrange("p t (c e) -> p c t e", e=2),
+                op=ALU.subtract,
+            )
+            return z_bf
 
-        def quantise(name, src, columns, on=None):
-            codes = new(name + "_codes", [P, columns], U32, on=on)
-            plane = new(name + "_plane", [P, columns], U8)
-            nc.vector.quantize_mx(out=codes[:].bitcast(FP8X4), scales=plane[:], in_=src)
-            return codes, plane
+        def pick_into(tile, s, first, width):
+            nc.vector.tensor_tensor(
+                out=tile,
+                in0=a_rows[s][:].indirect(idx3[:, first // PER_COLUMN : (first + width) // PER_COLUMN]),
+                in1=trust[s][:, first : first + width],
+                op=ALU.mult,
+            )
 
-        w1_bf = new("w1_bf", [P, PASS * PACK], BF16)
-        wg_bf = new("wg_bf", [P, 2 * PASS * PACK], BF16)
-        round_piece(nc.scalar.copy, raw_w1_0[0][:], w1_bf[:], 0)
+        def make_b(s, words, planes, number):
+            first = (s % PACK) * P
+            acc = bank("b%d" % number, [P, BANK])
+            for ps in range(2):
+                nc.tensor.matmul_mx(
+                    out=acc[:],
+                    lhsT=words[:, ps, 2 * first : 2 * (first + P)].bitcast(FP4X4),
+                    lhsT_scale=planes[:, ps, first : first + P],
+                    rhs=v_words[:, ps, :].bitcast(FP8X4),
+                    rhs_scale=(v_planes, v_plane1)[ps][:],
+                    start=(ps == 0),
+                    stop=(ps == 1),
+                )
+            return acc
 
-        pairs = new("pairs", [P, 2, 2, BANK, 2], BF16)
-        page_bf = [new("page_bf%d" % h, [P, BANK, PACK], BF16) for h in range(2)]
+        def rest_into(dst, s, acc):
+            nc.vector.scalar_tensor_tensor(
+                out=dst, in0=trust[s][:], scalar=1.0, in1=acc[:], op0=ALU.subtract, op1=ALU.mult
+            )
+
 
         def scatter_patch(t):
             nc.vector.tensor_copy(page[t][:].indirect(idx2[:]), patch[t][:])
@@ -159,217 +176,228 @@ def tile_list_foothold_terrain_blend_kernel(
                 in_=page[t][:].rearrange("p (h c) -> p h c", h=2)[:, column_halves, :],
             )
 
-        def weave_page(h):
-            nc.scalar.copy(
+        def weave_page(h, copy):
+            copy(
                 out=page_bf[h][:].bitcast(F32),
                 in_=pairs[:, h].rearrange("p u c e -> p u (c e)").bitcast(F32).rearrange("p u c -> p c u"),
             )
 
-        scatter_patch(0)
-        round_page(0, slice(0, 2))
-        round_piece(nc.scalar.copy, raw_w1_0[1][:], w1_bf[:], 1)
-        for t in (1, 2):
-            scatter_patch(t)
-            round_page(t, slice(0, 2))
-        round_block(raw_wg00, wg_bf[:, 0 : PASS * PACK], on_scalar)
-        scatter_patch(3)
-        for h in range(2):
-            round_page(3, slice(h, h + 1))
-            weave_page(h)
-
-        codes, plane = quantise("w1_0", w1_bf[:], PASS, on="patch3")
-        w1_q = [(codes[:], plane[:]), None]
-
-        v_words = new("v_words", [P, 2, S], U32)
-        v_planes = new("v_planes", [P, S], U8)
-        round_block(raw_wg01, wg_bf[:, PASS * PACK :], (nc.scalar.copy, nc.vector.tensor_copy))
-
-        nc.vector.tensor_copy(v_words[:, 0, :], tab_w0[:].bitcast(U32).indirect(idx[:]))
-        nc.vector.tensor_copy(v_planes[:], tab_planes[:].indirect(idx[:]))
-        for row in range(ROWS):
-            nc.sync.dma_start(v_plane1[row:P:QUAD, :].bitcast(I32), v_planes[ROWS + row : P : QUAD, :].bitcast(I32))
-        raw_wg10 = load_wg(1, 0)
-        raw_wg11 = load_wg(1, 1)
-
-        page_codes = new("page_codes", [P, T2], U32, on="tab_planes")
-        page_plane = new("page_plane", [P, T2], U8)
-        for h in range(2):
-            columns = slice(h * BANK, (h + 1) * BANK)
-            nc.vector.quantize_mx(
-                out=page_codes[:, columns].bitcast(FP8X4),
-                scales=page_plane[:, columns],
-                in_=page_bf[h][:].rearrange("p c t -> p (c t)"),
-            )
-        nc.vector.tensor_copy(v_words[:, 1, :], tab_w1[:].bitcast(U32).indirect(idx[:]))
-        codes, plane = quantise("wg0", wg_bf[:], 2 * PASS, on="tab_w1")
-        wg_q = [[(codes[:, 0:PASS], plane[:, 0:PASS]), (codes[:, PASS:], plane[:, PASS:])], None]
-
-        w2_sorted = new("w2_sorted", [P, 2, 2 * H], U8)
-        nc.vector.tensor_copy(
-            out=w2_sorted[:].bitcast(U16).rearrange("p ps (g t run y) -> p (ps g) run t y", g=2, t=PACK, y=8),
-            in_=w2_raw[:].bitcast(U16).rearrange("p ps (g run y t) -> p (ps g) run t y", g=2, t=PACK, y=8),
-        )
-        w2_planes = new("w2_planes", [P, 2, H], U8)
-        nc.vector.tensor_copy(
-            out=w2_planes[:].rearrange("p ps (g t run y) -> p (ps g) run t y", g=2, t=PACK, y=16),
-            in_=w2_planes_raw[:].rearrange("p ps (g run y t) -> p (ps g) run t y", g=2, t=PACK, y=16),
-        )
-
-        raw_w1_1 = load_weight("raw_w1_1", w1, PASS, PASS)
-        wo_w = new("wo_w", [P, 2, N], I32)
-        nc.sync.dma_start(wo_w[:], wo_words.rearrange("ps p c i -> p ps (c i)").bitcast(I32))
-        for quad in range(P // QUAD):
-            nc.sync.dma_start(
-                wo_planes[QUAD * quad : QUAD * quad + 2 * ROWS, :].bitcast(I32),
-                wo_scales[:, ROWS * quad : ROWS * (quad + 1), :].bitcast(I32),
-            )
-        bias = new("bias", [P, OUT_TILES], F32)
-        with nc.allow_non_contiguous_dma(reason="one bias value for each partition"):
-            nc.sync.dma_start(bias[:], bo.rearrange("(o p) -> p o", p=P))
-
+        page_q = [None, None]
+        w1_q = [None, None]
+        wg_q = {}
         a_rows = {}
         trust = {}
+        rest = {}
+        weighted = {}
+        used = []
 
-        def make_a(g, t, first_bank):
-            rows = slice(t * P, (t + 1) * P)
-            tile = new("a%d%d" % (g, t), [P, T2], F32)
-            for h in range(2):
-                columns = slice(h * BANK, (h + 1) * BANK)
-                acc = bank("s", first_bank + h, BANK)
-                nc.tensor.matmul_mx(
-                    out=acc[:],
-                    lhsT=w1_q[g][0][:, rows].bitcast(FP8X4),
-                    lhsT_scale=w1_q[g][1][:, rows],
-                    rhs=page_codes[:, columns].bitcast(FP8X4),
-                    rhs_scale=page_plane[:, columns],
-                    start=True,
-                    stop=True,
-                )
-                nc.scalar.copy(out=tile[:, columns], in_=acc[:])
-            a_rows[g, t] = tile
+        def next_bank(shape):
+            used.append(shape)
+            return bank("s%d" % ((len(used) - 1) % 4), shape)
 
-        def make_trust(g, t, number):
-            rows = slice(t * P, (t + 1) * P)
-            acc = bank("s", number, BANK)
+        def make_a(s, h, on=None, negate=False):
+            g, x = divmod(s, PACK)
+            rows = slice(x * P, (x + 1) * P)
+            if h == 0:
+                a_rows[s] = new("a%d" % s, [P, T2], F32, on=on)
+            acc = next_bank([P, BANK])
+            nc.tensor.matmul_mx(
+                out=acc[:],
+                lhsT=w1_q[g][0][:, rows].bitcast(FP8X4),
+                lhsT_scale=w1_q[g][1][:, rows],
+                rhs=page_q[h][0][:].bitcast(FP8X4),
+                rhs_scale=page_q[h][1][:],
+                start=True,
+                stop=True,
+            )
+            if negate:
+                nc.scalar.activation(out=a_rows[s][:, h * BANK : (h + 1) * BANK], in_=acc[:], func=ACT.Copy, scale=-1.0)
+            else:
+                nc.scalar.copy(out=a_rows[s][:, h * BANK : (h + 1) * BANK], in_=acc[:])
+
+        def make_trust(s, on=None):
+            g, x = divmod(s, PACK)
+            rows = slice(x * P, (x + 1) * P)
+            acc = next_bank([P, BANK])
             for ps in range(2):
                 nc.tensor.matmul_mx(
                     out=acc[:],
-                    lhsT=wg_q[g][ps][0][:, rows].bitcast(FP8X4),
-                    lhsT_scale=wg_q[g][ps][1][:, rows],
+                    lhsT=wg_q[g, ps][0][:, rows].bitcast(FP8X4),
+                    lhsT_scale=wg_q[g, ps][1][:, rows],
                     rhs=v_words[:, ps, :].bitcast(FP8X4),
                     rhs_scale=v_planes[ROWS * ps : P, :],
                     start=(ps == 0),
                     stop=(ps == 1),
                 )
-            tile = new("trust%d%d" % (g, t), [P, S], F32, on="trust", bufs=TRUST_BUFS)
-            nc.scalar.activation(out=tile[:], in_=acc[:], func=ACT.Sigmoid)
-            trust[g, t] = tile
+            trust[s] = new("trust%d" % s, [P, S], F32, on=on)
+            nc.scalar.activation(out=trust[s][:], in_=acc[:], func=ACT.Sigmoid)
 
-        def make_b(g, t):
-            first = g * PASS + t * P
-            acc = bank("v", t, BANK)
-            for ps in range(2):
-                nc.tensor.matmul_mx(
-                    out=acc[:],
-                    lhsT=w2_sorted[:, ps, 2 * first : 2 * (first + P)].bitcast(FP4X4),
-                    lhsT_scale=w2_planes[:, ps, first : first + P],
-                    rhs=v_words[:, ps, :].bitcast(FP8X4),
-                    rhs_scale=(v_planes, v_plane1)[ps][:],
-                    start=(ps == 0),
-                    stop=(ps == 1),
-                )
-            return acc
-
-        def pick_cells(g, t, weighted, first, width):
-            nc.vector.tensor_tensor(
-                out=weighted[:, t, :],
-                in0=a_rows[g, t][:].indirect(idx3[:, first // PER_COLUMN : (first + width) // PER_COLUMN]),
-                in1=trust[g, t][:, first : first + width],
-                op=ALU.mult,
+        def read_out(acc, g, o, codes, plane):
+            rows = slice(o * P, (o + 1) * P)
+            nc.tensor.matmul_mx(
+                out=acc,
+                lhsT=wo_w[:, g, rows].bitcast(FP8X4),
+                lhsT_scale=wo_planes[ROWS * g : P, rows],
+                rhs=codes.bitcast(FP8X4),
+                rhs_scale=plane,
+                start=(g == 0),
+                stop=(g == 1),
             )
 
-        def blend(g, weighted, width):
-            rest = new("rest%d" % g, [P, PACK, S], F32)
-            b_banks = [make_b(g, t) for t in range(PACK)]
-            for t in range(PACK):
-                nc.vector.scalar_tensor_tensor(
-                    out=rest[:, t, :], in0=trust[g, t][:], scalar=1.0, in1=b_banks[t][:], op0=ALU.subtract, op1=ALU.mult
+        def store(acc, side, o, on_vector):
+            result = new("result%d%d" % (side, o), [P, SIDE], F32)
+            if on_vector:
+                nc.vector.tensor_scalar(
+                    out=result[:], in0=acc, scalar1=bias[:, o : o + 1], scalar2=None, op0=ALU.add
                 )
-                pick_cells(g, t, weighted, 0, width)
-            return rest
+            else:
+                nc.scalar.activation(out=result[:], in_=acc, func=ACT.Identity, bias=bias[:, o : o + 1])
+            nc.sync.dma_start(out[o * P : (o + 1) * P, side * SIDE : (side + 1) * SIDE], result[:])
 
-        def finish_z(name, weighted, rest, first, width, on):
-            z_bf = new(name + "_bf", [P, width * PACK], BF16, on=on)
-            nc.vector.tensor_tensor(
-                out=z_bf[:].rearrange("p (c e t) -> p c t e", e=2, t=PACK),
-                in0=weighted[:].rearrange("p t (c e) -> p c t e", e=2),
-                in1=rest[:, :, first : first + width].rearrange("p t (c e) -> p c t e", e=2),
-                op=ALU.subtract,
-            )
-            return quantise(name, z_bf[:], width)
+        for row in range(ROWS):
+            load_w2_scale_rows(nc.gpsimd, row)
 
-        make_a(0, 0, 0)
-        make_a(0, 1, 2)
-        for t in (2, 3):
-            make_trust(0, 2 * t - 4, 0)
-            make_trust(0, 2 * t - 3, 1)
-            make_a(0, t, 2)
-        weighted0 = new("weighted0", [P, PACK, S], F32)
-        rest0 = blend(0, weighted0, S)
+        idx2 = load_list("idx2", offs2)
+        load_page(0)
+        load_patch(0)
+        raw_w1_00 = load_weight("raw_w1_00", w1, 0, PIECE, on="pairs")
+        load_page(1)
+        load_patch(1)
+        raw_w1_01 = load_weight("raw_w1_01", w1, PIECE, PIECE)
+        load_table_scale_rows(nc.sync, 0)
+        raw_wg00a = load_weight("raw_wg00a", wg[0:PASS, :], 0, PIECE)
+        load_table_scale_rows(nc.sync, 1)
+        load_page(2)
+        load_patch(2)
+        load_table_scale_rows(nc.sync, 2)
+        raw_wg00b = load_weight("raw_wg00b", wg[0:PASS, :], PIECE, PIECE)
+        load_table_scale_rows(nc.sync, 3)
+        load_page(3)
+        load_patch(3)
+        idx = load_list("idx", offs)
+        tab_w0 = load_table_words(0)
+        raw_wg01a = load_weight("raw_wg01a", wg[PASS:, :], 0, PIECE)
+        raw_wg01b = load_weight("raw_wg01b", wg[PASS:, :], PIECE, PIECE)
+        tab_w1 = load_table_words(1)
+        w2_raw = new("w2_raw", [P, 2, 2 * H], U8)
+        nc.sync.dma_start(w2_raw[:].bitcast(I32), w2_words.rearrange("ps p c -> p ps c").bitcast(I32))
+        idx3 = load_list("idx3", offs3)
 
-        late = []
-        for name, raw, on in (("wg10", raw_wg10, "page_bf1"), ("wg11", raw_wg11, None), ("w1_1", raw_w1_1, "w1_bf")):
-            rounded = new(name + "_bf", [P, PASS * PACK], BF16, on=on)
-            round_block(raw, rounded[:], on_scalar)
-            codes, plane = quantise(name, rounded[:], PASS)
-            late.append((codes[:], plane[:]))
-        wg_q[1] = late[0:2]
-        w1_q[1] = late[2]
-        z0_codes, z0_plane = finish_z("z0", weighted0, rest0, 0, S, "wg11_bf")
+        w2_dealt_planes = new("w2_dealt_planes", [P, 2, H], U8)
+        nc.gpsimd.tensor_copy(
+            out=w2_dealt_planes[:].rearrange("p ps (g t run y) -> p (ps g) run t y", g=2, t=PACK, y=16),
+            in_=w2_planes[:].rearrange("p ps (g run y t) -> p (ps g) run t y", g=2, t=PACK, y=16),
+        )
 
-        for t in range(PACK):
-            make_trust(1, t, t)
-        for t in range(PACK):
-            make_a(1, t, 2 * (t % 2))
-        weighted1 = [new("weighted1%d" % side, [P, PACK, SIDE], F32) for side in range(2)]
-        rest1 = blend(1, weighted1[0], SIDE)
+        first_bf = new("first_bf", [P, 2, PASS * PACK], BF16)
+        wg_bf01 = new("wg_bf01", [P, PASS * PACK], BF16)
+        round_piece(nc.scalar.copy, raw_w1_00[:], first_bf[:, 0, :], 0)
+        pairs = new("pairs", [P, 2, 2, BANK, 2], BF16)
+        page_bf = [new("page_bf%d" % h, [P, BANK, PACK], BF16) for h in range(2)]
+        scatter_patch(0)
+        round_page(0, slice(0, 2))
+        scatter_patch(1)
+        round_page(1, slice(0, 2))
+        round_piece(nc.scalar.copy, raw_w1_01[:], first_bf[:, 0, :], 1)
+        round_piece(nc.scalar.copy, raw_wg00a[:], first_bf[:, 1, :], 0)
+        scatter_patch(2)
+        round_page(2, slice(0, 2))
+        round_piece(nc.scalar.copy, raw_wg00b[:], first_bf[:, 1, :], 1)
+        scatter_patch(3)
+        for h in range(2):
+            round_page(3, slice(h, h + 1))
+        weave_page(1, nc.scalar.copy)
+        round_piece(nc.scalar.copy, raw_wg01a[:], wg_bf01[:], 0)
+        round_piece(nc.scalar.copy, raw_wg01b[:], wg_bf01[:], 1)
 
-        sums = [[bank(kind, o, SIDE) for o in range(OUT_TILES)] for kind in ("v", "s")]
+        v_words = new("v_words", [P, 2, S], U32)
+        v_planes = new("v_planes", [P, S], U8)
+        nc.vector.tensor_copy(v_planes[:], tab_planes[:].indirect(idx[:]))
+        for row in range(ROWS):
+            nc.sync.dma_start(v_plane1[row:P:QUAD, :].bitcast(I32), v_planes[ROWS + row : P : QUAD, :].bitcast(I32))
+        raw_wg10 = load_wg(1, 0)
+        raw_wg11 = load_wg(1, 1)
+        raw_w1_1 = load_weight("raw_w1_1", w1, PASS, PASS)
+        wo_w = new("wo_w", [P, 2, N], I32)
+        nc.sync.dma_start(wo_w[:], wo_words.rearrange("ps p c i -> p ps (c i)").bitcast(I32))
+        for quad in range(P // QUAD):
+            load_wo_scale_rows(nc.sync, quad)
+        bias = new("bias", [P, OUT_TILES], F32)
+        with nc.allow_non_contiguous_dma(reason="one bias value for each partition"):
+            nc.sync.dma_start(bias[:], bo.rearrange("(o p) -> p o", p=P))
 
-        def read_out(g, side, codes, plane):
-            for o in range(OUT_TILES):
-                rows = slice(o * P, (o + 1) * P)
-                nc.tensor.matmul_mx(
-                    out=sums[side][o][:],
-                    lhsT=wo_w[:, g, rows].bitcast(FP8X4),
-                    lhsT_scale=wo_planes[ROWS * g : P, rows],
-                    rhs=codes.bitcast(FP8X4),
-                    rhs_scale=plane,
-                    start=(g == 0),
-                    stop=(g == 1),
-                )
+        codes, plane = quantise("first", first_bf[:].rearrange("p b c -> p (b c)"), 2 * PASS, on="tab_planes")
+        w1_q[0] = (codes[:, 0:PASS], plane[:, 0:PASS])
+        wg_q[0, 0] = (codes[:, PASS:], plane[:, PASS:])
+        weave_page(0, nc.vector.tensor_copy)
+        page_q[1] = quantise("page1", page_bf[1][:].rearrange("p c t -> p (c t)"), BANK)
+        page_q[0] = quantise("page0", page_bf[0][:].rearrange("p c t -> p (c t)"), BANK)
+        nc.vector.tensor_copy(v_words[:, 0, :], tab_w0[:].bitcast(U32).indirect(idx[:]))
+        wg_q[0, 1] = quantise("wg01", wg_bf01[:], PASS)
+        nc.vector.tensor_copy(v_words[:, 1, :], tab_w1[:].bitcast(U32).indirect(idx[:]))
+        w2_dealt = new("w2_dealt", [P, 2, 2 * H], U8)
+        nc.vector.tensor_copy(
+            out=w2_dealt[:].bitcast(U16).rearrange("p ps (g t run y) -> p (ps g) run t y", g=2, t=PACK, y=8),
+            in_=w2_raw[:].bitcast(U16).rearrange("p ps (g run y t) -> p (ps g) run t y", g=2, t=PACK, y=8),
+        )
+        w2_half = [
+            (w2_dealt[:, :, g * 2 * PASS : (g + 1) * 2 * PASS], w2_dealt_planes[:, :, g * PASS : (g + 1) * PASS])
+            for g in range(2)
+        ]
 
-        def store(side, vector_tiles):
-            for o in range(OUT_TILES):
-                result = new("result%d%d" % (side, o), [P, SIDE], F32)
-                if o < vector_tiles:
-                    nc.vector.tensor_scalar(
-                        out=result[:], in0=sums[side][o][:], scalar1=bias[:, o : o + 1], scalar2=None, op0=ALU.add
-                    )
-                else:
-                    nc.scalar.activation(
-                        out=result[:], in_=sums[side][o][:], func=ACT.Identity, bias=bias[:, o : o + 1]
-                    )
-                nc.sync.dma_start(out[o * P : (o + 1) * P, side * SIDE : (side + 1) * SIDE], result[:])
-
+        picked0 = new("picked0", [P, PACK, S], F32)
+        rest0 = new("rest0", [P, PACK, S], F32)
+        make_a(0, 0, "raw_wg01a")
+        make_a(0, 1)
+        make_a(1, 0, "raw_wg01b")
+        make_a(1, 1)
+        make_trust(0)
+        make_a(2, 0, "page0")
+        make_trust(1)
+        make_a(2, 1)
+        make_trust(2)
+        make_a(3, 0, "page1")
+        make_trust(3)
+        make_a(3, 1)
+        for s in range(PACK):
+            pick_into(picked0[:, s, :], s, 0, S)
+        for s in range(PACK):
+            rest_into(rest0[:, s, :], s, make_b(s, w2_half[0][0], w2_half[0][1], s))
+        wg_bf10 = dealt("wg_bf10", nc.scalar.copy, raw_wg10)
+        wg_bf11 = dealt("wg_bf11", nc.scalar.copy, raw_wg11)
+        w1_bf1 = dealt("w1_bf1", nc.scalar.copy, raw_w1_1)
+        wg_q[1, 0] = quantise("wg10", wg_bf10[:], PASS)
+        wg_q[1, 1] = quantise("wg11", wg_bf11[:], PASS)
+        w1_q[1] = quantise("w1_1", w1_bf1[:], PASS)
+        z0_bf = finish_z("z0", picked0[:], rest0, 0, S, "wg_bf11")
+        for s in range(PACK, 2 * PACK):
+            make_trust(s)
+        for s, on in zip(range(PACK, 2 * PACK), ("page2", "page3", "raw_wg00a", "raw_wg00b")):
+            make_a(s, 0, on)
+            make_a(s, 1)
+        rest1 = new("rest1", [P, PACK, S], F32)
+        for s in range(PACK, 2 * PACK):
+            rest_into(rest1[:, s - PACK, :], s, make_b(s, w2_half[1][0], w2_half[1][1], s - PACK))
+        z0 = quantise("z0", z0_bf[:], S)
+        picked1 = new("picked1", [P, 2 * PACK - 1, SIDE], F32)
+        for s in range(PACK, 2 * PACK):
+            pick_into(picked1[:, s - 1, :], s, 0, SIDE)
+            if s < 2 * PACK - 1:
+                pick_into(picked1[:, s - PACK, :], s, SIDE, SIDE)
+        z10_bf = finish_z("z10", picked1[:, PACK - 1 :, :], rest1, 0, SIDE, "page_bf0")
+        pick_into(picked1[:, PACK - 1, :], 2 * PACK - 1, SIDE, SIDE)
+        z10 = quantise("z10", z10_bf[:], SIDE)
+        z11_bf = finish_z("z11", picked1[:, 0:PACK, :], rest1, SIDE, SIDE, "page_bf1")
+        z11 = quantise("z11", z11_bf[:], SIDE)
+        sums = [[bank("b%d" % o, [P, SIDE])[:] for o in range(OUT_TILES)], [next_bank([P, SIDE])[:] for o in range(OUT_TILES)]]
         for side in range(2):
-            columns = slice(side * SIDE, (side + 1) * SIDE)
-            read_out(0, side, z0_codes[:, columns], z0_plane[:, columns])
-        codes, plane = finish_z("z10", weighted1[0], rest1, 0, SIDE, "page_bf0")
-        read_out(1, 0, codes[:], plane[:])
-        store(0, 0)
-        for t in range(PACK):
-            pick_cells(1, t, weighted1[1], SIDE, SIDE)
-        codes, plane = finish_z("z11", weighted1[1], rest1, SIDE, SIDE, "page_bf1")
-        read_out(1, 1, codes[:], plane[:])
-        store(1, 2)
+            for o in range(OUT_TILES):
+                read_out(sums[side][o], 0, o, z0[0][:, side * SIDE : (side + 1) * SIDE], z0[1][:, side * SIDE : (side + 1) * SIDE])
+        for o in range(OUT_TILES):
+            read_out(sums[0][o], 1, o, z10[0][:], z10[1][:])
+        for o in range(OUT_TILES):
+            store(sums[0][o], 0, o, False)
+        for o in range(OUT_TILES):
+            read_out(sums[1][o], 1, o, z11[0][:], z11[1][:])
+        for o in range(OUT_TILES):
+            store(sums[1][o], 1, o, o < 2)

@@ -120,6 +120,13 @@ def tile_list_foothold_terrain_blend_kernel(
                 in_=src.rearrange("p j (x t) -> p x j t", t=PACK),
             )
 
+        def round_piece_in_order(src, dst, piece):
+            span = PIECE // PACK
+            nc.gpsimd.tensor_copy(
+                out=dst.rearrange("p (t x j) -> p t x j", t=PACK, j=PACK)[:, :, piece * span : (piece + 1) * span],
+                in_=src.rearrange("p j (x t) -> p t x j", t=PACK),
+            )
+
         def dealt(name, copy, raw, on=None):
             tile = new(name, [P, PASS * PACK], BF16, on=on)
             copy(
@@ -215,10 +222,10 @@ def tile_list_foothold_terrain_blend_kernel(
             else:
                 nc.scalar.copy(out=a_rows[s][:, h * BANK : (h + 1) * BANK], in_=acc[:])
 
-        def make_trust(s, on=None):
+        def make_trust(s, on=None, tag=None):
             g, x = divmod(s, PACK)
             rows = slice(x * P, (x + 1) * P)
-            acc = next_bank([P, BANK])
+            acc = bank(tag, [P, BANK]) if tag else next_bank([P, BANK])
             for ps in range(2):
                 nc.tensor.matmul_mx(
                     out=acc[:],
@@ -265,23 +272,21 @@ def tile_list_foothold_terrain_blend_kernel(
         load_patch(1)
         raw_w1_01 = load_weight("raw_w1_01", w1, PIECE, PIECE)
         load_table_scale_rows(nc.sync, 0)
-        raw_wg00a = load_weight("raw_wg00a", wg[0:PASS, :], 0, PIECE)
-        load_table_scale_rows(nc.sync, 1)
         load_page(2)
+        load_table_scale_rows(nc.sync, 1)
         load_patch(2)
         load_table_scale_rows(nc.sync, 2)
-        raw_wg00b = load_weight("raw_wg00b", wg[0:PASS, :], PIECE, PIECE)
+        raw_wg00 = load_wg(0, 0)
         load_table_scale_rows(nc.sync, 3)
         load_page(3)
         load_patch(3)
         idx = load_list("idx", offs)
-        tab_w0 = load_table_words(0)
         raw_wg01a = load_weight("raw_wg01a", wg[PASS:, :], 0, PIECE)
+        tab_w0 = load_table_words(0)
         raw_wg01b = load_weight("raw_wg01b", wg[PASS:, :], PIECE, PIECE)
         tab_w1 = load_table_words(1)
         w2_raw = new("w2_raw", [P, 2, 2 * H], U8)
         nc.sync.dma_start(w2_raw[:].bitcast(I32), w2_words.rearrange("ps p c -> p ps c").bitcast(I32))
-        idx3 = load_list("idx3", offs3)
 
         w2_dealt_planes = new("w2_dealt_planes", [P, 2, H], U8)
         nc.gpsimd.tensor_copy(
@@ -299,15 +304,15 @@ def tile_list_foothold_terrain_blend_kernel(
         scatter_patch(1)
         round_page(1, slice(0, 2))
         round_piece(nc.scalar.copy, raw_w1_01[:], first_bf[:, 0, :], 1)
-        round_piece(nc.scalar.copy, raw_wg00a[:], first_bf[:, 1, :], 0)
         scatter_patch(2)
         round_page(2, slice(0, 2))
-        round_piece(nc.scalar.copy, raw_wg00b[:], first_bf[:, 1, :], 1)
+        round_piece(nc.scalar.copy, raw_wg00[:, :, 0:PIECE], first_bf[:, 1, :], 0)
+        round_piece_in_order(raw_wg00[:, :, PIECE:], first_bf[:, 1, :], 1)
         scatter_patch(3)
         for h in range(2):
             round_page(3, slice(h, h + 1))
         weave_page(1, nc.scalar.copy)
-        round_piece(nc.scalar.copy, raw_wg01a[:], wg_bf01[:], 0)
+        round_piece_in_order(raw_wg01a[:], wg_bf01[:], 0)
         round_piece(nc.scalar.copy, raw_wg01b[:], wg_bf01[:], 1)
 
         v_words = new("v_words", [P, 2, S], U32)
@@ -317,6 +322,7 @@ def tile_list_foothold_terrain_blend_kernel(
             nc.sync.dma_start(v_plane1[row:P:QUAD, :].bitcast(I32), v_planes[ROWS + row : P : QUAD, :].bitcast(I32))
         raw_wg10 = load_wg(1, 0)
         raw_wg11 = load_wg(1, 1)
+        idx3 = load_list("idx3", offs3)
         raw_w1_1 = load_weight("raw_w1_1", w1, PASS, PASS)
         wo_w = new("wo_w", [P, 2, N], I32)
         nc.sync.dma_start(wo_w[:], wo_words.rearrange("ps p c i -> p ps (c i)").bitcast(I32))
@@ -345,11 +351,11 @@ def tile_list_foothold_terrain_blend_kernel(
             for g in range(2)
         ]
 
-        picked0 = new("picked0", [P, PACK, S], F32)
-        rest0 = new("rest0", [P, PACK, S], F32)
-        make_a(0, 0, "raw_wg01a")
+        wg_bf10 = dealt("wg_bf10", nc.vector.tensor_copy, raw_wg10)
+        picked0 = [new("picked0%d" % pair, [P, 2, S], F32) for pair in range(2)]
+        make_a(0, 0, "raw_wg01b")
         make_a(0, 1)
-        make_a(1, 0, "raw_wg01b")
+        make_a(1, 0, "wg_bf01")
         make_a(1, 1)
         make_trust(0)
         make_a(2, 0, "page0")
@@ -359,45 +365,61 @@ def tile_list_foothold_terrain_blend_kernel(
         make_a(3, 0, "page1")
         make_trust(3)
         make_a(3, 1)
-        for s in range(PACK):
-            pick_into(picked0[:, s, :], s, 0, S)
-        for s in range(PACK):
-            rest_into(rest0[:, s, :], s, make_b(s, w2_half[0][0], w2_half[0][1], s))
-        wg_bf10 = dealt("wg_bf10", nc.scalar.copy, raw_wg10)
-        wg_bf11 = dealt("wg_bf11", nc.scalar.copy, raw_wg11)
-        w1_bf1 = dealt("w1_bf1", nc.scalar.copy, raw_w1_1)
         wg_q[1, 0] = quantise("wg10", wg_bf10[:], PASS)
+        wg_bf11 = dealt("wg_bf11", nc.scalar.copy, raw_wg11)
         wg_q[1, 1] = quantise("wg11", wg_bf11[:], PASS)
-        w1_q[1] = quantise("w1_1", w1_bf1[:], PASS)
-        z0_bf = finish_z("z0", picked0[:], rest0, 0, S, "wg_bf11")
+        w1_bf1 = new("w1_bf1", [P, PASS * PACK], BF16)
+        w1_codes1 = new("w1_codes1", [P, PASS], U32)
+        w1_plane1 = new("w1_plane1", [P, PASS], U8)
+        for pair in range(2):
+            nc.scalar.copy(
+                out=w1_bf1[:].rearrange("p (t x j) -> p x j t", t=PACK, j=PACK)[:, :, :, 2 * pair : 2 * pair + 2],
+                in_=raw_w1_1[:].rearrange("p j (x t) -> p x j t", t=PACK)[:, :, :, 2 * pair : 2 * pair + 2],
+            )
+            columns = slice(pair * PIECE, (pair + 1) * PIECE)
+            nc.vector.quantize_mx(
+                out=w1_codes1[:, columns].bitcast(FP8X4),
+                scales=w1_plane1[:, columns],
+                in_=w1_bf1[:, pair * PIECE * PACK : (pair + 1) * PIECE * PACK],
+            )
+        w1_q[1] = (w1_codes1, w1_plane1)
+        for s in range(PACK):
+            pick_into(picked0[s // 2][:, s % 2, :], s, 0, S)
+        z0_rows = new("z0_rows", [P, PACK, S], BF16)
+        rest_late = new("rest_late", [P, 2, S], F32, on="raw_wg11")
+        for s in (2, 3):
+            rest_into(rest_late[:, s - 2, :], s, make_b(s, w2_half[0][0], w2_half[0][1], s))
+        nc.vector.tensor_tensor(out=z0_rows[:, 2:, :], in0=picked0[1][:], in1=rest_late[:], op=ALU.subtract)
+        rest_early = new("rest_early", [P, 2, S], F32, on="picked01")
+        for s in range(2):
+            rest_into(rest_early[:, s, :], s, make_b(s, w2_half[0][0], w2_half[0][1], s))
+            nc.gpsimd.tensor_tensor(out=z0_rows[:, s, :], in0=picked0[0][:, s, :], in1=rest_early[:, s, :], op=ALU.subtract)
         for s in range(PACK, 2 * PACK):
             make_trust(s)
-        for s, on in zip(range(PACK, 2 * PACK), ("page2", "page3", "raw_wg00a", "raw_wg00b")):
-            make_a(s, 0, on)
-            make_a(s, 1)
         rest1 = new("rest1", [P, PACK, S], F32)
         for s in range(PACK, 2 * PACK):
-            rest_into(rest1[:, s - PACK, :], s, make_b(s, w2_half[1][0], w2_half[1][1], s - PACK))
+            rest_into(rest1[:, s - PACK, :], s, make_b(s, w2_half[1][0], w2_half[1][1], (s - 2) % PACK))
+        for s, on in zip(range(PACK, 2 * PACK), ("page2", "page3", "raw_wg00", "raw_w1_01")):
+            make_a(s, 0, on)
+            make_a(s, 1)
+        z0_bf = new("z0_bf", [P, S * PACK], BF16, on="w1_codes1")
+        nc.scalar.copy(
+            out=z0_bf[:].rearrange("p (c i t) -> p c t i", i=PACK, t=PACK),
+            in_=z0_rows[:].rearrange("p t (c i) -> p c t i", i=PACK),
+        )
         z0 = quantise("z0", z0_bf[:], S)
-        picked1 = new("picked1", [P, 2 * PACK - 1, SIDE], F32)
+        picked1 = [new("picked1%d" % side, [P, PACK, SIDE], F32) for side in range(2)]
         for s in range(PACK, 2 * PACK):
-            pick_into(picked1[:, s - 1, :], s, 0, SIDE)
-            if s < 2 * PACK - 1:
-                pick_into(picked1[:, s - PACK, :], s, SIDE, SIDE)
-        z10_bf = finish_z("z10", picked1[:, PACK - 1 :, :], rest1, 0, SIDE, "page_bf0")
-        pick_into(picked1[:, PACK - 1, :], 2 * PACK - 1, SIDE, SIDE)
-        z10 = quantise("z10", z10_bf[:], SIDE)
-        z11_bf = finish_z("z11", picked1[:, 0:PACK, :], rest1, SIDE, SIDE, "page_bf1")
-        z11 = quantise("z11", z11_bf[:], SIDE)
+            for side in range(2):
+                pick_into(picked1[side][:, s - PACK, :], s, side * SIDE, SIDE)
         sums = [[bank("b%d" % o, [P, SIDE])[:] for o in range(OUT_TILES)], [next_bank([P, SIDE])[:] for o in range(OUT_TILES)]]
         for side in range(2):
             for o in range(OUT_TILES):
                 read_out(sums[side][o], 0, o, z0[0][:, side * SIDE : (side + 1) * SIDE], z0[1][:, side * SIDE : (side + 1) * SIDE])
-        for o in range(OUT_TILES):
-            read_out(sums[0][o], 1, o, z10[0][:], z10[1][:])
-        for o in range(OUT_TILES):
-            store(sums[0][o], 0, o, False)
-        for o in range(OUT_TILES):
-            read_out(sums[1][o], 1, o, z11[0][:], z11[1][:])
-        for o in range(OUT_TILES):
-            store(sums[1][o], 1, o, o < 2)
+        z1_bf = [finish_z("z1%d" % side, picked1[side][:], rest1, side * SIDE, SIDE, ("z0_rows", "w1_codes1")[side]) for side in range(2)]
+        for side in range(2):
+            codes, plane = quantise("z1%d" % side, z1_bf[side][:], SIDE)
+            for o in range(OUT_TILES):
+                read_out(sums[side][o], 1, o, codes[:], plane[:])
+            for o in range(OUT_TILES):
+                store(sums[side][o], side, o, side == 1 and o < 2)

@@ -276,13 +276,14 @@ def tile_list_foothold_terrain_blend_kernel(
         load_table_scale_rows(nc.sync, 1)
         load_patch(2)
         load_table_scale_rows(nc.sync, 2)
-        raw_wg00 = load_wg(0, 0)
+        raw_wg00a = load_weight("raw_wg00a", wg[0:PASS, :], 0, PIECE)
         load_table_scale_rows(nc.sync, 3)
         load_page(3)
         load_patch(3)
         idx = load_list("idx", offs)
-        raw_wg01a = load_weight("raw_wg01a", wg[PASS:, :], 0, PIECE)
+        raw_wg00b = load_weight("raw_wg00b", wg[0:PASS, :], PIECE, PIECE)
         tab_w0 = load_table_words(0)
+        raw_wg01a = load_weight("raw_wg01a", wg[PASS:, :], 0, PIECE)
         raw_wg01b = load_weight("raw_wg01b", wg[PASS:, :], PIECE, PIECE)
         tab_w1 = load_table_words(1)
         w2_raw = new("w2_raw", [P, 2, 2 * H], U8)
@@ -306,13 +307,13 @@ def tile_list_foothold_terrain_blend_kernel(
         round_piece(nc.scalar.copy, raw_w1_01[:], first_bf[:, 0, :], 1)
         scatter_patch(2)
         round_page(2, slice(0, 2))
-        round_piece(nc.scalar.copy, raw_wg00[:, :, 0:PIECE], first_bf[:, 1, :], 0)
-        round_piece_in_order(raw_wg00[:, :, PIECE:], first_bf[:, 1, :], 1)
+        round_piece(nc.scalar.copy, raw_wg00a[:], first_bf[:, 1, :], 0)
+        round_piece_in_order(raw_wg00b[:], first_bf[:, 1, :], 1)
         scatter_patch(3)
         for h in range(2):
             round_page(3, slice(h, h + 1))
         weave_page(1, nc.scalar.copy)
-        round_piece_in_order(raw_wg01a[:], wg_bf01[:], 0)
+        round_piece(nc.scalar.copy, raw_wg01a[:], wg_bf01[:], 0)
         round_piece(nc.scalar.copy, raw_wg01b[:], wg_bf01[:], 1)
 
         v_words = new("v_words", [P, 2, S], U32)
@@ -332,12 +333,11 @@ def tile_list_foothold_terrain_blend_kernel(
         with nc.allow_non_contiguous_dma(reason="one bias value for each partition"):
             nc.sync.dma_start(bias[:], bo.rearrange("(o p) -> p o", p=P))
 
-        codes, plane = quantise("first", first_bf[:].rearrange("p b c -> p (b c)"), 2 * PASS, on="tab_planes")
-        w1_q[0] = (codes[:, 0:PASS], plane[:, 0:PASS])
-        wg_q[0, 0] = (codes[:, PASS:], plane[:, PASS:])
+        w1_q[0] = quantise("w1_0", first_bf[:, 0, :], PASS, on="tab_planes")
         weave_page(0, nc.vector.tensor_copy)
         page_q[1] = quantise("page1", page_bf[1][:].rearrange("p c t -> p (c t)"), BANK)
         page_q[0] = quantise("page0", page_bf[0][:].rearrange("p c t -> p (c t)"), BANK)
+        wg_q[0, 0] = quantise("wg00", first_bf[:, 1, :], PASS)
         nc.vector.tensor_copy(v_words[:, 0, :], tab_w0[:].bitcast(U32).indirect(idx[:]))
         wg_q[0, 1] = quantise("wg01", wg_bf01[:], PASS)
         nc.vector.tensor_copy(v_words[:, 1, :], tab_w1[:].bitcast(U32).indirect(idx[:]))
@@ -353,9 +353,9 @@ def tile_list_foothold_terrain_blend_kernel(
 
         wg_bf10 = dealt("wg_bf10", nc.vector.tensor_copy, raw_wg10)
         picked0 = [new("picked0%d" % pair, [P, 2, S], F32) for pair in range(2)]
-        make_a(0, 0, "raw_wg01b")
+        make_a(0, 0, "raw_wg01a")
         make_a(0, 1)
-        make_a(1, 0, "wg_bf01")
+        make_a(1, 0, "raw_wg01b")
         make_a(1, 1)
         make_trust(0)
         make_a(2, 0, "page0")
@@ -399,7 +399,7 @@ def tile_list_foothold_terrain_blend_kernel(
         rest1 = new("rest1", [P, PACK, S], F32)
         for s in range(PACK, 2 * PACK):
             rest_into(rest1[:, s - PACK, :], s, make_b(s, w2_half[1][0], w2_half[1][1], (s - 2) % PACK))
-        for s, on in zip(range(PACK, 2 * PACK), ("page2", "page3", "raw_wg00", "raw_w1_01")):
+        for s, on in zip(range(PACK, 2 * PACK), ("page2", "page3", "raw_wg00a", "raw_w1_01")):
             make_a(s, 0, on)
             make_a(s, 1)
         z0_bf = new("z0_bf", [P, S * PACK], BF16, on="w1_codes1")

@@ -202,12 +202,12 @@ def tile_list_foothold_terrain_blend_kernel(
             used.append(shape)
             return bank("s%d" % ((len(used) - 1) % 4), shape)
 
-        def make_a(s, h, on=None, negate=False):
+        def make_a(s, h, on=None, tag=None, negate=False):
             g, x = divmod(s, PACK)
             rows = slice(x * P, (x + 1) * P)
             if h == 0:
                 a_rows[s] = new("a%d" % s, [P, T2], F32, on=on)
-            acc = next_bank([P, BANK])
+            acc = bank(tag, [P, BANK]) if tag else next_bank([P, BANK])
             nc.tensor.matmul_mx(
                 out=acc[:],
                 lhsT=w1_q[g][0][:, rows].bitcast(FP8X4),
@@ -264,6 +264,11 @@ def tile_list_foothold_terrain_blend_kernel(
         for row in range(ROWS):
             load_w2_scale_rows(nc.gpsimd, row)
 
+        w2_raw = [new("w2_raw%d" % ps, [P, 2 * H], U8) for ps in range(2)]
+
+        def load_w2(ps):
+            nc.sync.dma_start(w2_raw[ps][:].bitcast(I32), w2_words[ps].bitcast(I32))
+
         idx2 = load_list("idx2", offs2)
         load_page(0)
         load_patch(0)
@@ -275,6 +280,7 @@ def tile_list_foothold_terrain_blend_kernel(
         load_page(2)
         load_table_scale_rows(nc.sync, 1)
         load_patch(2)
+        load_w2(0)
         load_table_scale_rows(nc.sync, 2)
         raw_wg00a = load_weight("raw_wg00a", wg[0:PASS, :], 0, PIECE)
         load_table_scale_rows(nc.sync, 3)
@@ -286,13 +292,19 @@ def tile_list_foothold_terrain_blend_kernel(
         raw_wg01a = load_weight("raw_wg01a", wg[PASS:, :], 0, PIECE)
         raw_wg01b = load_weight("raw_wg01b", wg[PASS:, :], PIECE, PIECE)
         tab_w1 = load_table_words(1)
-        w2_raw = new("w2_raw", [P, 2, 2 * H], U8)
-        nc.sync.dma_start(w2_raw[:].bitcast(I32), w2_words.rearrange("ps p c -> p ps c").bitcast(I32))
+        idx3 = load_list("idx3", offs3)
+        raw_wg10 = load_wg(1, 0)
+        load_w2(1)
 
         w2_dealt_planes = new("w2_dealt_planes", [P, 2, H], U8)
         nc.gpsimd.tensor_copy(
             out=w2_dealt_planes[:].rearrange("p ps (g t run y) -> p (ps g) run t y", g=2, t=PACK, y=16),
             in_=w2_planes[:].rearrange("p ps (g run y t) -> p (ps g) run t y", g=2, t=PACK, y=16),
+        )
+        w2_dealt = new("w2_dealt", [P, 2, 2 * H], U8)
+        nc.gpsimd.tensor_copy(
+            out=w2_dealt[:, 0, :].rearrange("p (g t x b) -> p g t x b", g=2, t=PACK, b=2),
+            in_=w2_raw[0][:].rearrange("p (g x t b) -> p g t x b", g=2, t=PACK, b=2),
         )
 
         first_bf = new("first_bf", [P, 2, PASS * PACK], BF16)
@@ -312,7 +324,6 @@ def tile_list_foothold_terrain_blend_kernel(
         scatter_patch(3)
         for h in range(2):
             round_page(3, slice(h, h + 1))
-        weave_page(1, nc.scalar.copy)
         round_piece(nc.scalar.copy, raw_wg01a[:], wg_bf01[:], 0)
         round_piece(nc.scalar.copy, raw_wg01b[:], wg_bf01[:], 1)
 
@@ -321,9 +332,7 @@ def tile_list_foothold_terrain_blend_kernel(
         nc.vector.tensor_copy(v_planes[:], tab_planes[:].indirect(idx[:]))
         for row in range(ROWS):
             nc.sync.dma_start(v_plane1[row:P:QUAD, :].bitcast(I32), v_planes[ROWS + row : P : QUAD, :].bitcast(I32))
-        raw_wg10 = load_wg(1, 0)
         raw_wg11 = load_wg(1, 1)
-        idx3 = load_list("idx3", offs3)
         raw_w1_1 = load_weight("raw_w1_1", w1, PASS, PASS)
         wo_w = new("wo_w", [P, 2, N], I32)
         nc.sync.dma_start(wo_w[:], wo_words.rearrange("ps p c i -> p ps (c i)").bitcast(I32))
@@ -334,37 +343,41 @@ def tile_list_foothold_terrain_blend_kernel(
             nc.sync.dma_start(bias[:], bo.rearrange("(o p) -> p o", p=P))
 
         w1_q[0] = quantise("w1_0", first_bf[:, 0, :], PASS, on="tab_planes")
-        weave_page(0, nc.vector.tensor_copy)
-        page_q[1] = quantise("page1", page_bf[1][:].rearrange("p c t -> p (c t)"), BANK)
-        page_q[0] = quantise("page0", page_bf[0][:].rearrange("p c t -> p (c t)"), BANK)
+        for h in range(2):
+            weave_page(h, nc.vector.tensor_copy)
+        for h in range(2):
+            page_q[h] = quantise("page%d" % h, page_bf[h][:].rearrange("p c t -> p (c t)"), BANK)
         wg_q[0, 0] = quantise("wg00", first_bf[:, 1, :], PASS)
         nc.vector.tensor_copy(v_words[:, 0, :], tab_w0[:].bitcast(U32).indirect(idx[:]))
         wg_q[0, 1] = quantise("wg01", wg_bf01[:], PASS)
         nc.vector.tensor_copy(v_words[:, 1, :], tab_w1[:].bitcast(U32).indirect(idx[:]))
-        w2_dealt = new("w2_dealt", [P, 2, 2 * H], U8)
-        nc.vector.tensor_copy(
-            out=w2_dealt[:].bitcast(U16).rearrange("p ps (g t run y) -> p (ps g) run t y", g=2, t=PACK, y=8),
-            in_=w2_raw[:].bitcast(U16).rearrange("p ps (g run y t) -> p (ps g) run t y", g=2, t=PACK, y=8),
-        )
+
+        def deal_w2(ps):
+            nc.vector.tensor_copy(
+                out=w2_dealt[:, ps, :].bitcast(U16).rearrange("p (g t run y) -> p g run t y", g=2, t=PACK, y=8),
+                in_=w2_raw[ps][:].bitcast(U16).rearrange("p (g run y t) -> p g run t y", g=2, t=PACK, y=8),
+            )
+
         w2_half = [
             (w2_dealt[:, :, g * 2 * PASS : (g + 1) * 2 * PASS], w2_dealt_planes[:, :, g * PASS : (g + 1) * PASS])
             for g in range(2)
         ]
 
         wg_bf10 = dealt("wg_bf10", nc.vector.tensor_copy, raw_wg10)
-        picked0 = [new("picked0%d" % pair, [P, 2, S], F32) for pair in range(2)]
+        deal_w2(1)
+        picked0 = [new("picked0%d" % pair, [P, 2, S], F32, on=("raw_wg10", "wg_bf10")[pair]) for pair in range(2)]
         make_a(0, 0, "raw_wg01a")
-        make_a(0, 1)
         make_a(1, 0, "raw_wg01b")
+        make_a(0, 1)
         make_a(1, 1)
+        make_a(2, 0, "wg_bf01", "b0")
+        make_a(2, 1, None, "b1")
+        make_a(3, 0, "tab_w1", "b2")
         make_trust(0)
-        make_a(2, 0, "page0")
         make_trust(1)
-        make_a(2, 1)
+        make_a(3, 1, None, "b3")
         make_trust(2)
-        make_a(3, 0, "page1")
         make_trust(3)
-        make_a(3, 1)
         wg_q[1, 0] = quantise("wg10", wg_bf10[:], PASS)
         wg_bf11 = dealt("wg_bf11", nc.scalar.copy, raw_wg11)
         wg_q[1, 1] = quantise("wg11", wg_bf11[:], PASS)
@@ -390,18 +403,30 @@ def tile_list_foothold_terrain_blend_kernel(
         for s in (2, 3):
             rest_into(rest_late[:, s - 2, :], s, make_b(s, w2_half[0][0], w2_half[0][1], s))
         nc.vector.tensor_tensor(out=z0_rows[:, 2:, :], in0=picked0[1][:], in1=rest_late[:], op=ALU.subtract)
-        rest_early = new("rest_early", [P, 2, S], F32, on="picked01")
+        rest_early = new("rest_early", [P, 2, S], F32, on="wg_bf10")
         for s in range(2):
             rest_into(rest_early[:, s, :], s, make_b(s, w2_half[0][0], w2_half[0][1], s))
             nc.gpsimd.tensor_tensor(out=z0_rows[:, s, :], in0=picked0[0][:, s, :], in1=rest_early[:, s, :], op=ALU.subtract)
         for s in range(PACK, 2 * PACK):
             make_trust(s)
         rest1 = new("rest1", [P, PACK, S], F32)
-        for s in range(PACK, 2 * PACK):
-            rest_into(rest1[:, s - PACK, :], s, make_b(s, w2_half[1][0], w2_half[1][1], (s - 2) % PACK))
-        for s, on in zip(range(PACK, 2 * PACK), ("page2", "page3", "raw_wg00a", "raw_w1_01")):
+
+        def second_rest(s):
+            rest_into(rest1[:, s - PACK, :], s, make_b(s, w2_half[1][0], w2_half[1][1], s - PACK))
+
+        def both_halves(s, on):
             make_a(s, 0, on)
             make_a(s, 1)
+
+        second_rest(6)
+        second_rest(7)
+        both_halves(4, "page2")
+        make_a(5, 0, "page3")
+        second_rest(4)
+        second_rest(5)
+        make_a(5, 1)
+        both_halves(6, "raw_wg00a")
+        both_halves(7, "raw_w1_01")
         z0_bf = new("z0_bf", [P, S * PACK], BF16, on="w1_codes1")
         nc.scalar.copy(
             out=z0_bf[:].rearrange("p (c i t) -> p c t i", i=PACK, t=PACK),

@@ -13,6 +13,8 @@ U16 = mybir.dt.uint16
 U8 = mybir.dt.uint8
 FP8X4 = mybir.dt.float8_e4m3fn_x4
 FP4X4 = mybir.dt.float4_e2m1fn_x4
+ALIGN = 64
+SHARE = 64
 ALU = mybir.AluOpType
 ACT = mybir.ActivationFunctionType
 
@@ -27,8 +29,6 @@ PER_COLUMN = 16
 PIECE = PASS // 2
 SIDE = S // 2
 OUT_TILES = N // P
-RAW_BUFS = 3
-TRUST_BUFS = 6
 
 
 def tile_list_foothold_terrain_blend_kernel(
@@ -40,19 +40,31 @@ def tile_list_foothold_terrain_blend_kernel(
         sb = ctx.enter_context(tc.tile_pool(name="sb", bufs=1))
         psum = ctx.enter_context(tc.psum_pool(name="psum", bufs=1))
 
-        def new(name, shape, dtype, on=None, bufs=1):
-            return sb.tile(shape, dtype, name=name, tag=on or name, bufs=bufs, align_bytes=64)
+        place = {}
+        top = [0]
+
+        def new(name, shape, dtype, on=None, skip=0):
+            if on is None:
+                place[name] = top[0]
+                size = 1 if dtype == U8 else 2 if dtype == BF16 else 4
+                for n in shape[1:]:
+                    size = size * n
+                top[0] = top[0] + (size + ALIGN - 1) // ALIGN * ALIGN
+            else:
+                place[name] = place[on] + skip
+            return sb.tile(shape, dtype, name=name, offset=place[name], align_bytes=ALIGN)
 
         def bank(tag, shape):
             return psum.tile(shape, F32, name="acc", tag=tag)
 
-        tab_planes = new("tab_planes", [P, T], U8)
+        tab_rows = new("tab_rows", [P, T], U8)
         w2_planes = new("w2_planes", [P, 2, H], U8)
+        v_planes = new("v_planes", [P, 2, S], U8)
         wo_planes = new("wo_planes", [P, N], U8)
-        v_plane1 = new("v_plane1", [P, S], U8)
-        nc.vector.memset(tab_planes[:].bitcast(I32), 0)
         nc.vector.memset(w2_planes[:].rearrange("p ps c -> p (ps c)").bitcast(I32), 0)
-        nc.vector.memset(v_plane1[:].bitcast(I32), 0)
+        nc.vector.memset(tab_rows[QUAD : 2 * QUAD, :].bitcast(I32), 0)
+        nc.vector.memset(tab_rows[2 * QUAD :, :].bitcast(I32), 0)
+        nc.vector.memset(v_planes[:].rearrange("p ps c -> p (ps c)").bitcast(I32), 0)
         nc.vector.memset(wo_planes[:].bitcast(I32), 0)
 
         warm = new("warm", [P, 2], F32)
@@ -88,12 +100,11 @@ def tile_list_foothold_terrain_blend_kernel(
             nc.sync.dma_start(tile[:], tab_words[ps].rearrange("p c i -> p (c i)").bitcast(I32))
             return tile
 
-        def load_table_scale_rows(queue, row):
-            for ps in range(2):
-                queue.dma_start(
-                    tab_planes[ROWS * ps + row : P : QUAD, :].bitcast(I32),
-                    tab_scales[ps, row:BLOCKS:ROWS, :].bitcast(I32),
-                )
+        def move_table_plane(ps, row):
+            nc.sync.dma_start(
+                v_planes[row:P:QUAD, ps, :].bitcast(I32),
+                v_rows[BLOCKS * ps + row : BLOCKS * (ps + 1) : ROWS, :].bitcast(I32),
+            )
 
         def load_w2_scale_rows(queue, row):
             queue.dma_start(
@@ -107,9 +118,9 @@ def tile_list_foothold_terrain_blend_kernel(
                 wo_scales[:, ROWS * quad : ROWS * (quad + 1), :].bitcast(I32),
             )
 
-        def quantise(name, src, columns, on=None):
-            codes = new(name + "_codes", [P, columns], U32, on=on)
-            plane = new(name + "_plane", [P, columns], U8)
+        def quantise(name, src, columns, on=None, skip=0):
+            codes = new(name + "_codes", [P, columns], U32)
+            plane = new(name + "_plane", [P, columns], U8, on=on, skip=skip)
             nc.vector.quantize_mx(out=codes[:].bitcast(FP8X4), scales=plane[:], in_=src)
             return codes, plane
 
@@ -125,6 +136,13 @@ def tile_list_foothold_terrain_blend_kernel(
             nc.gpsimd.tensor_copy(
                 out=dst.rearrange("p (t x j) -> p t x j", t=PACK, j=PACK)[:, :, piece * span : (piece + 1) * span],
                 in_=src.rearrange("p j (x t) -> p t x j", t=PACK),
+            )
+
+        def round_columns(copy, raw, dst, at, first=0, last=None):
+            last = last or raw.shape[2]
+            copy(
+                out=dst[:].rearrange("p (t x j) -> p x j t", t=PACK, j=PACK)[:, (at + first) // PACK : (at + last) // PACK],
+                in_=raw[:].rearrange("p j (x t) -> p x j t", t=PACK)[:, first // PACK : last // PACK],
             )
 
         def dealt(name, copy, raw, on=None):
@@ -162,7 +180,7 @@ def tile_list_foothold_terrain_blend_kernel(
                     lhsT=words[:, ps, 2 * first : 2 * (first + P)].bitcast(FP4X4),
                     lhsT_scale=planes[:, ps, first : first + P],
                     rhs=v_words[:, ps, :].bitcast(FP8X4),
-                    rhs_scale=(v_planes, v_plane1)[ps][:],
+                    rhs_scale=v_planes[:, ps, :],
                     start=(ps == 0),
                     stop=(ps == 1),
                 )
@@ -202,11 +220,11 @@ def tile_list_foothold_terrain_blend_kernel(
             used.append(shape)
             return bank("s%d" % ((len(used) - 1) % 4), shape)
 
-        def make_a(s, h, on=None, tag=None, negate=False):
+        def make_a(s, h, on=None, tag=None, skip=0):
             g, x = divmod(s, PACK)
             rows = slice(x * P, (x + 1) * P)
             if h == 0:
-                a_rows[s] = new("a%d" % s, [P, T2], F32, on=on)
+                a_rows[s] = new("a%d" % s, [P, T2], F32, on=on, skip=skip)
             acc = bank(tag, [P, BANK]) if tag else next_bank([P, BANK])
             nc.tensor.matmul_mx(
                 out=acc[:],
@@ -217,10 +235,7 @@ def tile_list_foothold_terrain_blend_kernel(
                 start=True,
                 stop=True,
             )
-            if negate:
-                nc.scalar.activation(out=a_rows[s][:, h * BANK : (h + 1) * BANK], in_=acc[:], func=ACT.Copy, scale=-1.0)
-            else:
-                nc.scalar.copy(out=a_rows[s][:, h * BANK : (h + 1) * BANK], in_=acc[:])
+            nc.scalar.copy(out=a_rows[s][:, h * BANK : (h + 1) * BANK], in_=acc[:])
 
         def make_trust(s, on=None, tag=None):
             g, x = divmod(s, PACK)
@@ -232,7 +247,7 @@ def tile_list_foothold_terrain_blend_kernel(
                     lhsT=wg_q[g, ps][0][:, rows].bitcast(FP8X4),
                     lhsT_scale=wg_q[g, ps][1][:, rows],
                     rhs=v_words[:, ps, :].bitcast(FP8X4),
-                    rhs_scale=v_planes[ROWS * ps : P, :],
+                    rhs_scale=v_planes[:, ps, :],
                     start=(ps == 0),
                     stop=(ps == 1),
                 )
@@ -269,29 +284,43 @@ def tile_list_foothold_terrain_blend_kernel(
         def load_w2(ps):
             nc.sync.dma_start(w2_raw[ps][:].bitcast(I32), w2_words[ps].bitcast(I32))
 
+        idx = load_list("idx", offs)
+        nc.sync.dma_start(
+            tab_rows[0:QUAD, :].bitcast(I32), tab_scales.rearrange("ps q c -> (ps q) c").bitcast(I32)
+        )
         idx2 = load_list("idx2", offs2)
+        top[0] = top[0] + 4096
+        v_rows = new("v_rows", [P, S], U8)
+        top[0] = top[0] + 1024
+        nc.vector.tensor_copy(v_rows[:], tab_rows[:].indirect(idx[:]))
         load_page(0)
         load_patch(0)
-        raw_w1_00 = load_weight("raw_w1_00", w1, 0, PIECE, on="pairs")
+        raw_w1_00 = load_weight("raw_w1_00", w1, 0, PIECE)
+        raw_w1_01 = new("raw_w1_01", [P, PACK, PIECE], F32)
         load_page(1)
         load_patch(1)
-        raw_w1_01 = load_weight("raw_w1_01", w1, PIECE, PIECE)
-        load_table_scale_rows(nc.sync, 0)
+        nc.sync.dma_start(raw_w1_01[:], w1.rearrange("(p j) c -> p j c", j=PACK)[:, :, PIECE:PASS])
         load_page(2)
-        load_table_scale_rows(nc.sync, 1)
+        raw_wg00a = load_weight("raw_wg00a", wg[0:PASS, :], 0, PIECE)
         load_patch(2)
         load_w2(0)
-        load_table_scale_rows(nc.sync, 2)
-        raw_wg00a = load_weight("raw_wg00a", wg[0:PASS, :], 0, PIECE)
-        load_table_scale_rows(nc.sync, 3)
         load_page(3)
-        load_patch(3)
-        idx = load_list("idx", offs)
         raw_wg00b = load_weight("raw_wg00b", wg[0:PASS, :], PIECE, PIECE)
-        tab_w0 = load_table_words(0)
+        load_patch(3)
+        move_table_plane(0, 0)
+        move_table_plane(0, 1)
         raw_wg01a = load_weight("raw_wg01a", wg[PASS:, :], 0, PIECE)
-        raw_wg01b = load_weight("raw_wg01b", wg[PASS:, :], PIECE, PIECE)
+        move_table_plane(0, 2)
+        move_table_plane(0, 3)
+        move_table_plane(1, 0)
+        tab_w0 = load_table_words(0)
+        move_table_plane(1, 1)
+        move_table_plane(1, 2)
+        move_table_plane(1, 3)
         tab_w1 = load_table_words(1)
+        top[0] = top[0] + 2048
+        raw_wg01b = load_weight("raw_wg01b", wg[PASS:, :], PIECE, PIECE)
+        top[0] = top[0] + 2048
         idx3 = load_list("idx3", offs3)
         raw_wg10 = load_wg(1, 0)
         load_w2(1)
@@ -310,28 +339,25 @@ def tile_list_foothold_terrain_blend_kernel(
         first_bf = new("first_bf", [P, 2, PASS * PACK], BF16)
         wg_bf01 = new("wg_bf01", [P, PASS * PACK], BF16)
         round_piece(nc.scalar.copy, raw_w1_00[:], first_bf[:, 0, :], 0)
-        pairs = new("pairs", [P, 2, 2, BANK, 2], BF16)
-        page_bf = [new("page_bf%d" % h, [P, BANK, PACK], BF16) for h in range(2)]
+        round_piece(nc.scalar.copy, raw_w1_01[:], first_bf[:, 0, :], 1)
+        pairs = new("pairs", [P, 2, 2, BANK, 2], BF16, on="raw_w1_00")
+        page_bf = [new("page_bf0", [P, BANK, PACK], BF16, on="v_rows", skip=64 - 4096), new("page_bf1", [P, BANK, PACK], BF16)]
         scatter_patch(0)
         round_page(0, slice(0, 2))
         scatter_patch(1)
         round_page(1, slice(0, 2))
-        round_piece(nc.scalar.copy, raw_w1_01[:], first_bf[:, 0, :], 1)
+        round_piece(nc.scalar.copy, raw_wg00a[:], first_bf[:, 1, :], 0)
         scatter_patch(2)
         round_page(2, slice(0, 2))
-        round_piece(nc.scalar.copy, raw_wg00a[:], first_bf[:, 1, :], 0)
-        round_piece_in_order(raw_wg00b[:], first_bf[:, 1, :], 1)
+        round_piece(nc.scalar.copy, raw_wg00b[:], first_bf[:, 1, :], 1)
+        round_piece_in_order(raw_wg01a[:], wg_bf01[:], 0)
         scatter_patch(3)
         for h in range(2):
             round_page(3, slice(h, h + 1))
-        round_piece(nc.scalar.copy, raw_wg01a[:], wg_bf01[:], 0)
+        weave_page(1, nc.scalar.copy)
         round_piece(nc.scalar.copy, raw_wg01b[:], wg_bf01[:], 1)
 
         v_words = new("v_words", [P, 2, S], U32)
-        v_planes = new("v_planes", [P, S], U8)
-        nc.vector.tensor_copy(v_planes[:], tab_planes[:].indirect(idx[:]))
-        for row in range(ROWS):
-            nc.sync.dma_start(v_plane1[row:P:QUAD, :].bitcast(I32), v_planes[ROWS + row : P : QUAD, :].bitcast(I32))
         raw_wg11 = load_wg(1, 1)
         raw_w1_1 = load_weight("raw_w1_1", w1, PASS, PASS)
         wo_w = new("wo_w", [P, 2, N], I32)
@@ -342,15 +368,15 @@ def tile_list_foothold_terrain_blend_kernel(
         with nc.allow_non_contiguous_dma(reason="one bias value for each partition"):
             nc.sync.dma_start(bias[:], bo.rearrange("(o p) -> p o", p=P))
 
-        w1_q[0] = quantise("w1_0", first_bf[:, 0, :], PASS, on="tab_planes")
-        for h in range(2):
-            weave_page(h, nc.vector.tensor_copy)
-        for h in range(2):
-            page_q[h] = quantise("page%d" % h, page_bf[h][:].rearrange("p c t -> p (c t)"), BANK)
-        wg_q[0, 0] = quantise("wg00", first_bf[:, 1, :], PASS)
         nc.vector.tensor_copy(v_words[:, 0, :], tab_w0[:].bitcast(U32).indirect(idx[:]))
-        wg_q[0, 1] = quantise("wg01", wg_bf01[:], PASS)
+        weave_page(0, nc.vector.tensor_copy)
+        first_codes, first_plane = quantise("first", first_bf[:].rearrange("p w c -> p (w c)"), 2 * PASS, "v_rows", 448)
+        w1_q[0] = (first_codes[:, 0:PASS], first_plane[:, 0:PASS])
+        wg_q[0, 0] = (first_codes[:, PASS:], first_plane[:, PASS:])
+        for h in range(2):
+            page_q[h] = quantise("page%d" % h, page_bf[h][:].rearrange("p c t -> p (c t)"), BANK, (None, "first_bf")[h])
         nc.vector.tensor_copy(v_words[:, 1, :], tab_w1[:].bitcast(U32).indirect(idx[:]))
+        wg_q[0, 1] = quantise("wg01", wg_bf01[:], PASS)
 
         def deal_w2(ps):
             nc.vector.tensor_copy(
@@ -366,47 +392,55 @@ def tile_list_foothold_terrain_blend_kernel(
         wg_bf10 = dealt("wg_bf10", nc.vector.tensor_copy, raw_wg10)
         deal_w2(1)
         picked0 = [new("picked0%d" % pair, [P, 2, S], F32, on=("raw_wg10", "wg_bf10")[pair]) for pair in range(2)]
-        make_a(0, 0, "raw_wg01a")
-        make_a(1, 0, "raw_wg01b")
-        make_a(0, 1)
-        make_a(1, 1)
-        make_a(2, 0, "wg_bf01", "b0")
-        make_a(2, 1, None, "b1")
-        make_a(3, 0, "tab_w1", "b2")
-        make_trust(0)
-        make_trust(1)
-        make_a(3, 1, None, "b3")
-        make_trust(2)
-        make_trust(3)
+        make_a(0, 0, "raw_wg01b", "s0", -2048)
+        make_a(1, 0, "raw_wg01b", "s1", 2048)
+        make_a(0, 1, None, "s2")
+        make_a(1, 1, None, "s3")
+        make_a(2, 0, "page0", "s0")
+        make_trust(0, None, "b0")
+        make_trust(1, None, "b1")
+        make_a(2, 1, None, "b0")
+        make_trust(2, None, "s1")
+        make_a(3, 0, "page1", "b1")
+        make_trust(3, None, "s2")
+        make_a(3, 1, None, "s1")
         wg_q[1, 0] = quantise("wg10", wg_bf10[:], PASS)
-        wg_bf11 = dealt("wg_bf11", nc.scalar.copy, raw_wg11)
+        wg_bf11 = new("wg_bf11", [P, PASS * PACK], BF16)
+        round_columns(nc.scalar.copy, raw_wg11, wg_bf11, 0, 0, PASS - SHARE)
+        for s in range(PACK):
+            pick_into(picked0[s // 2][:, s % 2, :], s, 0, S)
+        round_columns(nc.vector.tensor_copy, raw_wg11, wg_bf11, 0, PASS - SHARE, PASS)
+        rest_late = new("rest_late", [P, 2, S], F32)
+        for s in (2, 3):
+            rest_into(rest_late[:, s - 2, :], s, make_b(s, w2_half[0][0], w2_half[0][1], s))
         wg_q[1, 1] = quantise("wg11", wg_bf11[:], PASS)
-        w1_bf1 = new("w1_bf1", [P, PASS * PACK], BF16)
-        w1_codes1 = new("w1_codes1", [P, PASS], U32)
+        z0_rows = new("z0_rows", [P, 2, S, 2], BF16, on="raw_wg11")
+        nc.vector.tensor_tensor(
+            out=z0_rows[:, 1].rearrange("p (c e) t -> p c t e", e=PACK),
+            in0=picked0[1][:].rearrange("p t (c e) -> p c t e", e=PACK),
+            in1=rest_late[:].rearrange("p t (c e) -> p c t e", e=PACK),
+            op=ALU.subtract,
+        )
+        w1_bf1 = [new("w1_bf1", [P, PIECE * PACK], BF16)[:], z0_rows[:, 0].rearrange("p c e -> p (c e)")]
+        w1_codes1 = new("w1_codes1", [P, PASS], U32, on="tab_w0")
         w1_plane1 = new("w1_plane1", [P, PASS], U8)
-        for pair in range(2):
+        w1_q[1] = (w1_codes1, w1_plane1)
+
+        def second_w1(pair):
             nc.scalar.copy(
-                out=w1_bf1[:].rearrange("p (t x j) -> p x j t", t=PACK, j=PACK)[:, :, :, 2 * pair : 2 * pair + 2],
+                out=w1_bf1[pair].rearrange("p (t x j) -> p x j t", t=2, j=PACK),
                 in_=raw_w1_1[:].rearrange("p j (x t) -> p x j t", t=PACK)[:, :, :, 2 * pair : 2 * pair + 2],
             )
             columns = slice(pair * PIECE, (pair + 1) * PIECE)
-            nc.vector.quantize_mx(
-                out=w1_codes1[:, columns].bitcast(FP8X4),
-                scales=w1_plane1[:, columns],
-                in_=w1_bf1[:, pair * PIECE * PACK : (pair + 1) * PIECE * PACK],
-            )
-        w1_q[1] = (w1_codes1, w1_plane1)
-        for s in range(PACK):
-            pick_into(picked0[s // 2][:, s % 2, :], s, 0, S)
-        z0_rows = new("z0_rows", [P, PACK, S], BF16)
-        rest_late = new("rest_late", [P, 2, S], F32, on="raw_wg11")
-        for s in (2, 3):
-            rest_into(rest_late[:, s - 2, :], s, make_b(s, w2_half[0][0], w2_half[0][1], s))
-        nc.vector.tensor_tensor(out=z0_rows[:, 2:, :], in0=picked0[1][:], in1=rest_late[:], op=ALU.subtract)
-        rest_early = new("rest_early", [P, 2, S], F32, on="wg_bf10")
+            nc.vector.quantize_mx(out=w1_codes1[:, columns].bitcast(FP8X4), scales=w1_plane1[:, columns], in_=w1_bf1[pair])
+
+        second_w1(0)
+        rest_early = [new("rest_early%d" % s, [P, S], F32, on=(None, "raw_w1_1")[s]) for s in range(2)]
+        rest_into(rest_early[0][:], 0, make_b(0, w2_half[0][0], w2_half[0][1], 0))
+        second_w1(1)
+        rest_into(rest_early[1][:], 1, make_b(1, w2_half[0][0], w2_half[0][1], 1))
         for s in range(2):
-            rest_into(rest_early[:, s, :], s, make_b(s, w2_half[0][0], w2_half[0][1], s))
-            nc.gpsimd.tensor_tensor(out=z0_rows[:, s, :], in0=picked0[0][:, s, :], in1=rest_early[:, s, :], op=ALU.subtract)
+            nc.gpsimd.tensor_tensor(out=z0_rows[:, 0, :, s], in0=picked0[0][:, s, :], in1=rest_early[s][:], op=ALU.subtract)
         for s in range(PACK, 2 * PACK):
             make_trust(s)
         rest1 = new("rest1", [P, PACK, S], F32)
@@ -426,11 +460,11 @@ def tile_list_foothold_terrain_blend_kernel(
         second_rest(5)
         make_a(5, 1)
         both_halves(6, "raw_wg00a")
-        both_halves(7, "raw_w1_01")
+        both_halves(7, "raw_wg00b")
         z0_bf = new("z0_bf", [P, S * PACK], BF16, on="w1_codes1")
         nc.scalar.copy(
-            out=z0_bf[:].rearrange("p (c i t) -> p c t i", i=PACK, t=PACK),
-            in_=z0_rows[:].rearrange("p t (c i) -> p c t i", i=PACK),
+            out=z0_bf[:].bitcast(F32),
+            in_=z0_rows[:].rearrange("p u c e -> p u (c e)").bitcast(F32).rearrange("p u c -> p c u"),
         )
         z0 = quantise("z0", z0_bf[:], S)
         picked1 = [new("picked1%d" % side, [P, PACK, SIDE], F32) for side in range(2)]

@@ -61,7 +61,6 @@ def tile_list_foothold_terrain_blend_kernel(
         w2_planes = new("w2_planes", [P, 2, H], U8)
         v_planes = new("v_planes", [P, 2, S], U8)
         wo_planes = new("wo_planes", [P, N], U8)
-        nc.vector.memset(w2_planes[:].rearrange("p ps c -> p (ps c)").bitcast(I32), 0)
         nc.vector.memset(tab_rows[QUAD : 2 * QUAD, :].bitcast(I32), 0)
         nc.vector.memset(tab_rows[2 * QUAD :, :].bitcast(I32), 0)
         nc.vector.memset(v_planes[:].rearrange("p ps c -> p (ps c)").bitcast(I32), 0)
@@ -69,6 +68,7 @@ def tile_list_foothold_terrain_blend_kernel(
 
         warm = new("warm", [P, 2], F32)
         nc.vector.memset(warm[:, 0:1], 0.0)
+        nc.vector.memset(w2_planes[:].rearrange("p ps c -> p (ps c)").bitcast(I32), 0)
         nc.scalar.activation(out=warm[:, 1:2], in_=warm[:, 0:1], func=ACT.Sigmoid)
 
         def load_list(name, src):
@@ -153,8 +153,8 @@ def tile_list_foothold_terrain_blend_kernel(
             )
             return tile
 
-        def finish_z(name, picked, left, first, width, on):
-            z_bf = new(name + "_bf", [P, width * PACK], BF16, on=on)
+        def finish_z(name, picked, left, first, width, skip):
+            z_bf = new(name + "_bf", [P, width * PACK], BF16, on="z0_rows", skip=skip)
             nc.vector.tensor_tensor(
                 out=z_bf[:].rearrange("p (c e t) -> p c t e", e=2, t=PACK),
                 in0=picked.rearrange("p t (c e) -> p c t e", e=2),
@@ -285,27 +285,23 @@ def tile_list_foothold_terrain_blend_kernel(
             nc.sync.dma_start(w2_raw[ps][:].bitcast(I32), w2_words[ps].bitcast(I32))
 
         idx = load_list("idx", offs)
-        nc.sync.dma_start(
+        nc.scalar.dma_start(
             tab_rows[0:QUAD, :].bitcast(I32), tab_scales.rearrange("ps q c -> (ps q) c").bitcast(I32)
         )
-        idx2 = load_list("idx2", offs2)
         top[0] = top[0] + 4096
         v_rows = new("v_rows", [P, S], U8)
         top[0] = top[0] + 1024
         nc.vector.tensor_copy(v_rows[:], tab_rows[:].indirect(idx[:]))
         load_page(0)
         load_patch(0)
-        raw_w1_00 = load_weight("raw_w1_00", w1, 0, PIECE)
-        raw_w1_01 = new("raw_w1_01", [P, PACK, PIECE], F32)
+        idx2 = load_list("idx2", offs2)
         load_page(1)
         load_patch(1)
-        nc.sync.dma_start(raw_w1_01[:], w1.rearrange("(p j) c -> p j c", j=PACK)[:, :, PIECE:PASS])
+        raw_w1_0 = load_weight("raw_w1_0", w1, 0, PASS)
         load_page(2)
-        raw_wg00a = load_weight("raw_wg00a", wg[0:PASS, :], 0, PIECE)
         load_patch(2)
-        load_w2(0)
+        raw_wg00 = load_wg(0, 0)
         load_page(3)
-        raw_wg00b = load_weight("raw_wg00b", wg[0:PASS, :], PIECE, PIECE)
         load_patch(3)
         move_table_plane(0, 0)
         move_table_plane(0, 1)
@@ -322,6 +318,7 @@ def tile_list_foothold_terrain_blend_kernel(
         raw_wg01b = load_weight("raw_wg01b", wg[PASS:, :], PIECE, PIECE)
         top[0] = top[0] + 2048
         idx3 = load_list("idx3", offs3)
+        load_w2(0)
         raw_wg10 = load_wg(1, 0)
         load_w2(1)
 
@@ -331,25 +328,20 @@ def tile_list_foothold_terrain_blend_kernel(
             in_=w2_planes[:].rearrange("p ps (g run y t) -> p (ps g) run t y", g=2, t=PACK, y=16),
         )
         w2_dealt = new("w2_dealt", [P, 2, 2 * H], U8)
-        nc.gpsimd.tensor_copy(
-            out=w2_dealt[:, 0, :].rearrange("p (g t x b) -> p g t x b", g=2, t=PACK, b=2),
-            in_=w2_raw[0][:].rearrange("p (g x t b) -> p g t x b", g=2, t=PACK, b=2),
-        )
 
         first_bf = new("first_bf", [P, 2, PASS * PACK], BF16)
         wg_bf01 = new("wg_bf01", [P, PASS * PACK], BF16)
-        round_piece(nc.scalar.copy, raw_w1_00[:], first_bf[:, 0, :], 0)
-        round_piece(nc.scalar.copy, raw_w1_01[:], first_bf[:, 0, :], 1)
-        pairs = new("pairs", [P, 2, 2, BANK, 2], BF16, on="raw_w1_00")
+        round_columns(nc.scalar.copy, raw_w1_0, first_bf[:, 0, :], 0)
+        pairs = new("pairs", [P, 2, 2, BANK, 2], BF16, on="raw_w1_0")
         page_bf = [new("page_bf0", [P, BANK, PACK], BF16, on="v_rows", skip=64 - 4096), new("page_bf1", [P, BANK, PACK], BF16)]
         scatter_patch(0)
         round_page(0, slice(0, 2))
         scatter_patch(1)
         round_page(1, slice(0, 2))
-        round_piece(nc.scalar.copy, raw_wg00a[:], first_bf[:, 1, :], 0)
+        round_piece_in_order(raw_wg00[:, :, 0:PIECE], first_bf[:, 1, :], 0)
         scatter_patch(2)
         round_page(2, slice(0, 2))
-        round_piece(nc.scalar.copy, raw_wg00b[:], first_bf[:, 1, :], 1)
+        round_piece(nc.scalar.copy, raw_wg00[:, :, PIECE:], first_bf[:, 1, :], 1)
         round_piece_in_order(raw_wg01a[:], wg_bf01[:], 0)
         scatter_patch(3)
         for h in range(2):
@@ -389,25 +381,27 @@ def tile_list_foothold_terrain_blend_kernel(
             for g in range(2)
         ]
 
+        deal_w2(0)
         wg_bf10 = dealt("wg_bf10", nc.vector.tensor_copy, raw_wg10)
         deal_w2(1)
-        picked0 = [new("picked0%d" % pair, [P, 2, S], F32, on=("raw_wg10", "wg_bf10")[pair]) for pair in range(2)]
+        picked0 = [new("picked0%d" % pair, [P, 2, S], F32, on=("raw_wg10", None)[pair]) for pair in range(2)]
         make_a(0, 0, "raw_wg01b", "s0", -2048)
         make_a(1, 0, "raw_wg01b", "s1", 2048)
         make_a(0, 1, None, "s2")
-        make_a(1, 1, None, "s3")
-        make_a(2, 0, "page0", "s0")
         make_trust(0, None, "b0")
         make_trust(1, None, "b1")
-        make_a(2, 1, None, "b0")
-        make_trust(2, None, "s1")
+        make_a(1, 1, None, "b0")
+        make_a(2, 0, "page0", "b1")
+        make_trust(2, None, "s0")
+        make_a(2, 1, None, "s0")
+        make_trust(3, None, "s1")
         make_a(3, 0, "page1", "b1")
-        make_trust(3, None, "s2")
-        make_a(3, 1, None, "s1")
-        wg_q[1, 0] = quantise("wg10", wg_bf10[:], PASS)
+        make_a(3, 1, None, "b0")
         wg_bf11 = new("wg_bf11", [P, PASS * PACK], BF16)
         round_columns(nc.scalar.copy, raw_wg11, wg_bf11, 0, 0, PASS - SHARE)
-        for s in range(PACK):
+        pick_into(picked0[0][:, 0, :], 0, 0, S)
+        wg_q[1, 0] = quantise("wg10", wg_bf10[:], PASS)
+        for s in range(1, PACK):
             pick_into(picked0[s // 2][:, s % 2, :], s, 0, S)
         round_columns(nc.vector.tensor_copy, raw_wg11, wg_bf11, 0, PASS - SHARE, PASS)
         rest_late = new("rest_late", [P, 2, S], F32)
@@ -459,26 +453,31 @@ def tile_list_foothold_terrain_blend_kernel(
         second_rest(4)
         second_rest(5)
         make_a(5, 1)
-        both_halves(6, "raw_wg00a")
-        both_halves(7, "raw_wg00b")
+        both_halves(6, "raw_wg00")
+        both_halves(7, "raw_wg01a")
         z0_bf = new("z0_bf", [P, S * PACK], BF16, on="w1_codes1")
         nc.scalar.copy(
             out=z0_bf[:].bitcast(F32),
             in_=z0_rows[:].rearrange("p u c e -> p u (c e)").bitcast(F32).rearrange("p u c -> p c u"),
         )
-        z0 = quantise("z0", z0_bf[:], S)
         picked1 = [new("picked1%d" % side, [P, PACK, SIDE], F32) for side in range(2)]
         for s in range(PACK, 2 * PACK):
             for side in range(2):
                 pick_into(picked1[side][:, s - PACK, :], s, side * SIDE, SIDE)
         sums = [[bank("b%d" % o, [P, SIDE])[:] for o in range(OUT_TILES)], [next_bank([P, SIDE])[:] for o in range(OUT_TILES)]]
-        for side in range(2):
+
+        def last_passes(g, side, src):
+            codes, plane = quantise("z%d%d" % (g, side), src, SIDE)
             for o in range(OUT_TILES):
-                read_out(sums[side][o], 0, o, z0[0][:, side * SIDE : (side + 1) * SIDE], z0[1][:, side * SIDE : (side + 1) * SIDE])
-        z1_bf = [finish_z("z1%d" % side, picked1[side][:], rest1, side * SIDE, SIDE, ("z0_rows", "w1_codes1")[side]) for side in range(2)]
-        for side in range(2):
-            codes, plane = quantise("z1%d" % side, z1_bf[side][:], SIDE)
-            for o in range(OUT_TILES):
-                read_out(sums[side][o], 1, o, codes[:], plane[:])
-            for o in range(OUT_TILES):
-                store(sums[side][o], side, o, side == 1 and o < 2)
+                read_out(sums[side][o], g, o, codes[:], plane[:])
+
+        last_passes(0, 0, z0_bf[:, 0 : SIDE * PACK])
+        z10_bf = finish_z("z10", picked1[0][:], rest1, 0, SIDE, 0)
+        last_passes(0, 1, z0_bf[:, SIDE * PACK :])
+        last_passes(1, 0, z10_bf[:])
+        for o in range(OUT_TILES):
+            store(sums[0][o], 0, o, False)
+        z11_bf = finish_z("z11", picked1[1][:], rest1, SIDE, SIDE, 2048)
+        last_passes(1, 1, z11_bf[:])
+        for o in range(OUT_TILES):
+            store(sums[1][o], 1, o, o != 1)

@@ -13,8 +13,6 @@ U16 = mybir.dt.uint16
 U8 = mybir.dt.uint8
 FP8X4 = mybir.dt.float8_e4m3fn_x4
 FP4X4 = mybir.dt.float4_e2m1fn_x4
-ALIGN = 64
-SHARE = 64
 ALU = mybir.AluOpType
 ACT = mybir.ActivationFunctionType
 
@@ -29,6 +27,9 @@ PER_COLUMN = 16
 PIECE = PASS // 2
 SIDE = S // 2
 OUT_TILES = N // P
+RING = 4
+ALIGN = 64
+ROW_BYTES = 4 * T2
 
 
 def tile_list_foothold_terrain_blend_kernel(
@@ -43,19 +44,175 @@ def tile_list_foothold_terrain_blend_kernel(
         place = {}
         top = [0]
 
+        def reserve(size):
+            top[0] = top[0] + (size + ALIGN - 1) // ALIGN * ALIGN
+
         def new(name, shape, dtype, on=None, skip=0):
             if on is None:
                 place[name] = top[0]
                 size = 1 if dtype == U8 else 2 if dtype == BF16 else 4
                 for n in shape[1:]:
                     size = size * n
-                top[0] = top[0] + (size + ALIGN - 1) // ALIGN * ALIGN
+                reserve(size)
             else:
                 place[name] = place[on] + skip
             return sb.tile(shape, dtype, name=name, offset=place[name], align_bytes=ALIGN)
 
-        def bank(tag, shape):
-            return psum.tile(shape, F32, name="acc", tag=tag)
+        def bank(tag, columns=BANK):
+            return psum.tile([P, columns], F32, name="acc", tag=tag)
+
+        turns = []
+
+        def next_bank(columns=BANK):
+            turns.append(columns)
+            return bank("s%d" % ((len(turns) - 1) % RING), columns)
+
+
+        def load_list(name, src):
+            tile = lists.tile([P, S // PER_COLUMN], U16, name=name)
+            nc.sync.dma_start(tile[:], src)
+            return tile
+
+        page = [None] * PACK
+        patch = [None] * PACK
+
+        def load_grid_rows(t):
+            page[t] = new("page%d" % t, [P, T2], F32)
+            nc.sync.dma_start(page[t][:], base.rearrange("(p t) c -> p t c", t=PACK)[:, t, :])
+            patch[t] = new("patch%d" % t, [P, S], F32)
+            nc.sync.dma_start(patch[t][:], xs.rearrange("(p t) c -> p t c", t=PACK)[:, t, :])
+
+        def load_weight(name, rows, first, width):
+            raw = new(name, [P, PACK, width], F32)
+            nc.sync.dma_start(raw[:], rows.rearrange("(p j) c -> p j c", j=PACK)[:, :, first : first + width])
+            return raw
+
+        def load_table_words(ps):
+            tile = new("tab_w%d" % ps, [P, T], I32)
+            nc.sync.dma_start(tile[:], tab_words[ps].rearrange("p c i -> p (c i)").bitcast(I32))
+            return tile
+
+        def load_w2(ps):
+            tile = new("w2_raw%d" % ps, [P, 2 * H], U8)
+            nc.sync.dma_start(tile[:].bitcast(I32), w2_words[ps].bitcast(I32))
+            return tile
+
+        def move_table_plane(ps, row):
+            nc.sync.dma_start(
+                v_planes[row:P:QUAD, ps, :].bitcast(I32),
+                v_rows[BLOCKS * ps + row : BLOCKS * (ps + 1) : ROWS, :].bitcast(I32),
+            )
+
+
+        def round_weight(copy, raw, dst, at=0):
+            width = raw.shape[2]
+            copy(
+                out=dst.rearrange("p (t x j) -> p x j t", t=PACK, j=PACK)[:, at // PACK : (at + width) // PACK],
+                in_=raw.rearrange("p j (x t) -> p x j t", t=PACK),
+            )
+
+        def round_first_piece(raw, dst):
+            nc.gpsimd.tensor_copy(
+                out=dst.rearrange("p (t x j) -> p t x j", t=PACK, j=PACK)[:, :, 0 : PIECE // PACK],
+                in_=raw.rearrange("p j (x t) -> p t x j", t=PACK),
+            )
+
+        def quantise(name, src, columns, on=None, skip=0):
+            codes = new(name + "_codes", [P, columns], U32)
+            plane = new(name + "_plane", [P, columns], U8, on=on, skip=skip)
+            nc.vector.quantize_mx(out=codes[:].bitcast(FP8X4), scales=plane[:], in_=src)
+            return codes, plane
+
+        def scatter_patch(t):
+            nc.vector.tensor_copy(page[t][:].indirect(idx2[:]), patch[t][:])
+
+        def round_page(t, column_halves):
+            nc.scalar.copy(
+                out=pairs[:, column_halves, t // 2, :, t % 2],
+                in_=page[t][:].rearrange("p (h c) -> p h c", h=2)[:, column_halves, :],
+            )
+
+        def weave(copy, dst, src):
+            copy(out=dst.bitcast(F32), in_=src.rearrange("p u c e -> p u (c e)").bitcast(F32).rearrange("p u c -> p c u"))
+
+        def deal_w2(ps, raw):
+            nc.vector.tensor_copy(
+                out=w2_dealt[:, ps, :].bitcast(U16).rearrange("p (g t run y) -> p g run t y", g=2, t=PACK, y=8),
+                in_=raw[:].bitcast(U16).rearrange("p (g run y t) -> p g run t y", g=2, t=PACK, y=8),
+            )
+
+
+        page_q = [None, None]
+        w1_q = [None, None]
+        wg_q = {}
+        a_rows = {}
+        trust = {}
+
+        def make_a(s, h, acc, on=None, skip=0):
+            g, t = divmod(s, PACK)
+            rows = slice(t * P, (t + 1) * P)
+            if h == 0:
+                a_rows[s] = new("a%d" % s, [P, T2], F32, on=on, skip=skip)
+            nc.tensor.matmul_mx(
+                out=acc[:],
+                lhsT=w1_q[g][0][:, rows].bitcast(FP8X4),
+                lhsT_scale=w1_q[g][1][:, rows],
+                rhs=page_q[h][0][:].bitcast(FP8X4),
+                rhs_scale=page_q[h][1][:],
+                start=True,
+                stop=True,
+            )
+            nc.scalar.copy(out=a_rows[s][:, h * BANK : (h + 1) * BANK], in_=acc[:])
+
+        def make_trust(s, acc):
+            g, t = divmod(s, PACK)
+            rows = slice(t * P, (t + 1) * P)
+            for ps in range(2):
+                nc.tensor.matmul_mx(
+                    out=acc[:],
+                    lhsT=wg_q[g, ps][0][:, rows].bitcast(FP8X4),
+                    lhsT_scale=wg_q[g, ps][1][:, rows],
+                    rhs=v_words[:, ps, :].bitcast(FP8X4),
+                    rhs_scale=v_planes[:, ps, :],
+                    start=(ps == 0),
+                    stop=(ps == 1),
+                )
+            trust[s] = new("trust%d" % s, [P, S], F32)
+            nc.scalar.activation(out=trust[s][:], in_=acc[:], func=ACT.Sigmoid)
+
+        def make_rest(s, acc, dst):
+            columns = slice(s * P, (s + 1) * P)
+            for ps in range(2):
+                nc.tensor.matmul_mx(
+                    out=acc[:],
+                    lhsT=w2_dealt[:, ps, 2 * s * P : 2 * (s + 1) * P].bitcast(FP4X4),
+                    lhsT_scale=w2_dealt_planes[:, ps, columns],
+                    rhs=v_words[:, ps, :].bitcast(FP8X4),
+                    rhs_scale=v_planes[:, ps, :],
+                    start=(ps == 0),
+                    stop=(ps == 1),
+                )
+            nc.vector.scalar_tensor_tensor(
+                out=dst, in0=trust[s][:], scalar=1.0, in1=acc[:], op0=ALU.subtract, op1=ALU.mult
+            )
+
+        def pick(s, dst, first=0, width=S):
+            nc.vector.tensor_tensor(
+                out=dst,
+                in0=a_rows[s][:].indirect(idx3[:, first // PER_COLUMN : (first + width) // PER_COLUMN]),
+                in1=trust[s][:, first : first + width],
+                op=ALU.mult,
+            )
+
+        def subtract_interleaved(dst, picked, rest, slices):
+            run = 8 // slices
+            nc.vector.tensor_tensor(
+                out=dst.rearrange("p (c e t) -> p c t e", e=run, t=slices),
+                in0=picked.rearrange("p t (c e) -> p c t e", e=run),
+                in1=rest.rearrange("p t (c e) -> p c t e", e=run),
+                op=ALU.subtract,
+            )
+
 
         tab_rows = new("tab_rows", [P, T], U8)
         w2_planes = new("w2_planes", [P, 2, H], U8)
@@ -71,256 +228,45 @@ def tile_list_foothold_terrain_blend_kernel(
         nc.vector.memset(w2_planes[:].rearrange("p ps c -> p (ps c)").bitcast(I32), 0)
         nc.scalar.activation(out=warm[:, 1:2], in_=warm[:, 0:1], func=ACT.Sigmoid)
 
-        def load_list(name, src):
-            tile = lists.tile([P, S // PER_COLUMN], U16, name=name)
-            nc.sync.dma_start(tile[:], src)
-            return tile
-
-        page = [None] * PACK
-        patch = [None] * PACK
-
-        def load_page(t):
-            page[t] = new("page%d" % t, [P, T2], F32)
-            nc.sync.dma_start(page[t][:], base.rearrange("(p t) c -> p t c", t=PACK)[:, t, :])
-
-        def load_patch(t):
-            patch[t] = new("patch%d" % t, [P, S], F32)
-            nc.sync.dma_start(patch[t][:], xs.rearrange("(p t) c -> p t c", t=PACK)[:, t, :])
-
-        def load_weight(name, rows, first, width, on=None):
-            raw = new(name, [P, PACK, width], F32, on=on)
-            nc.sync.dma_start(raw[:], rows.rearrange("(p j) c -> p j c", j=PACK)[:, :, first : first + width])
-            return raw
-
-        def load_wg(g, ps):
-            return load_weight("raw_wg%d%d" % (g, ps), wg[ps * PASS : (ps + 1) * PASS, :], g * PASS, PASS)
-
-        def load_table_words(ps):
-            tile = new("tab_w%d" % ps, [P, T], I32)
-            nc.sync.dma_start(tile[:], tab_words[ps].rearrange("p c i -> p (c i)").bitcast(I32))
-            return tile
-
-        def move_table_plane(ps, row):
-            nc.sync.dma_start(
-                v_planes[row:P:QUAD, ps, :].bitcast(I32),
-                v_rows[BLOCKS * ps + row : BLOCKS * (ps + 1) : ROWS, :].bitcast(I32),
-            )
-
-        def load_w2_scale_rows(queue, row):
-            queue.dma_start(
+        for row in range(ROWS):
+            nc.gpsimd.dma_start(
                 w2_planes[row:P:QUAD, :, :].bitcast(I32),
                 w2_scales[:, row:BLOCKS:ROWS, :].rearrange("ps quad c -> quad ps c").bitcast(I32),
             )
 
-        def load_wo_scale_rows(queue, quad):
-            queue.dma_start(
-                wo_planes[QUAD * quad : QUAD * quad + 2 * ROWS, :].bitcast(I32),
-                wo_scales[:, ROWS * quad : ROWS * (quad + 1), :].bitcast(I32),
-            )
-
-        def quantise(name, src, columns, on=None, skip=0):
-            codes = new(name + "_codes", [P, columns], U32)
-            plane = new(name + "_plane", [P, columns], U8, on=on, skip=skip)
-            nc.vector.quantize_mx(out=codes[:].bitcast(FP8X4), scales=plane[:], in_=src)
-            return codes, plane
-
-        def round_piece(copy, src, dst, piece):
-            span = PIECE // PACK
-            copy(
-                out=dst.rearrange("p (t x j) -> p x j t", t=PACK, j=PACK)[:, piece * span : (piece + 1) * span],
-                in_=src.rearrange("p j (x t) -> p x j t", t=PACK),
-            )
-
-        def round_piece_in_order(src, dst, piece):
-            span = PIECE // PACK
-            nc.gpsimd.tensor_copy(
-                out=dst.rearrange("p (t x j) -> p t x j", t=PACK, j=PACK)[:, :, piece * span : (piece + 1) * span],
-                in_=src.rearrange("p j (x t) -> p t x j", t=PACK),
-            )
-
-        def round_columns(copy, raw, dst, at, first=0, last=None):
-            last = last or raw.shape[2]
-            copy(
-                out=dst[:].rearrange("p (t x j) -> p x j t", t=PACK, j=PACK)[:, (at + first) // PACK : (at + last) // PACK],
-                in_=raw[:].rearrange("p j (x t) -> p x j t", t=PACK)[:, first // PACK : last // PACK],
-            )
-
-        def dealt(name, copy, raw, on=None):
-            tile = new(name, [P, PASS * PACK], BF16, on=on)
-            copy(
-                out=tile[:].rearrange("p (t x j) -> p x j t", t=PACK, j=PACK),
-                in_=raw[:].rearrange("p j (x t) -> p x j t", t=PACK),
-            )
-            return tile
-
-        def finish_z(name, picked, left, first, width, skip):
-            z_bf = new(name + "_bf", [P, width * PACK], BF16, on="z0_rows", skip=skip)
-            nc.vector.tensor_tensor(
-                out=z_bf[:].rearrange("p (c e t) -> p c t e", e=2, t=PACK),
-                in0=picked.rearrange("p t (c e) -> p c t e", e=2),
-                in1=left[:, :, first : first + width].rearrange("p t (c e) -> p c t e", e=2),
-                op=ALU.subtract,
-            )
-            return z_bf
-
-        def pick_into(tile, s, first, width):
-            nc.vector.tensor_tensor(
-                out=tile,
-                in0=a_rows[s][:].indirect(idx3[:, first // PER_COLUMN : (first + width) // PER_COLUMN]),
-                in1=trust[s][:, first : first + width],
-                op=ALU.mult,
-            )
-
-        def make_b(s, words, planes, number):
-            first = (s % PACK) * P
-            acc = bank("b%d" % number, [P, BANK])
-            for ps in range(2):
-                nc.tensor.matmul_mx(
-                    out=acc[:],
-                    lhsT=words[:, ps, 2 * first : 2 * (first + P)].bitcast(FP4X4),
-                    lhsT_scale=planes[:, ps, first : first + P],
-                    rhs=v_words[:, ps, :].bitcast(FP8X4),
-                    rhs_scale=v_planes[:, ps, :],
-                    start=(ps == 0),
-                    stop=(ps == 1),
-                )
-            return acc
-
-        def rest_into(dst, s, acc):
-            nc.vector.scalar_tensor_tensor(
-                out=dst, in0=trust[s][:], scalar=1.0, in1=acc[:], op0=ALU.subtract, op1=ALU.mult
-            )
-
-
-        def scatter_patch(t):
-            nc.vector.tensor_copy(page[t][:].indirect(idx2[:]), patch[t][:])
-
-        def round_page(t, column_halves):
-            nc.scalar.copy(
-                out=pairs[:, column_halves, t // 2, :, t % 2],
-                in_=page[t][:].rearrange("p (h c) -> p h c", h=2)[:, column_halves, :],
-            )
-
-        def weave_page(h, copy):
-            copy(
-                out=page_bf[h][:].bitcast(F32),
-                in_=pairs[:, h].rearrange("p u c e -> p u (c e)").bitcast(F32).rearrange("p u c -> p c u"),
-            )
-
-        page_q = [None, None]
-        w1_q = [None, None]
-        wg_q = {}
-        a_rows = {}
-        trust = {}
-        rest = {}
-        weighted = {}
-        used = []
-
-        def next_bank(shape):
-            used.append(shape)
-            return bank("s%d" % ((len(used) - 1) % 4), shape)
-
-        def make_a(s, h, on=None, tag=None, skip=0):
-            g, x = divmod(s, PACK)
-            rows = slice(x * P, (x + 1) * P)
-            if h == 0:
-                a_rows[s] = new("a%d" % s, [P, T2], F32, on=on, skip=skip)
-            acc = bank(tag, [P, BANK]) if tag else next_bank([P, BANK])
-            nc.tensor.matmul_mx(
-                out=acc[:],
-                lhsT=w1_q[g][0][:, rows].bitcast(FP8X4),
-                lhsT_scale=w1_q[g][1][:, rows],
-                rhs=page_q[h][0][:].bitcast(FP8X4),
-                rhs_scale=page_q[h][1][:],
-                start=True,
-                stop=True,
-            )
-            nc.scalar.copy(out=a_rows[s][:, h * BANK : (h + 1) * BANK], in_=acc[:])
-
-        def make_trust(s, on=None, tag=None):
-            g, x = divmod(s, PACK)
-            rows = slice(x * P, (x + 1) * P)
-            acc = bank(tag, [P, BANK]) if tag else next_bank([P, BANK])
-            for ps in range(2):
-                nc.tensor.matmul_mx(
-                    out=acc[:],
-                    lhsT=wg_q[g, ps][0][:, rows].bitcast(FP8X4),
-                    lhsT_scale=wg_q[g, ps][1][:, rows],
-                    rhs=v_words[:, ps, :].bitcast(FP8X4),
-                    rhs_scale=v_planes[:, ps, :],
-                    start=(ps == 0),
-                    stop=(ps == 1),
-                )
-            trust[s] = new("trust%d" % s, [P, S], F32, on=on)
-            nc.scalar.activation(out=trust[s][:], in_=acc[:], func=ACT.Sigmoid)
-
-        def read_out(acc, g, o, codes, plane):
-            rows = slice(o * P, (o + 1) * P)
-            nc.tensor.matmul_mx(
-                out=acc,
-                lhsT=wo_w[:, g, rows].bitcast(FP8X4),
-                lhsT_scale=wo_planes[ROWS * g : P, rows],
-                rhs=codes.bitcast(FP8X4),
-                rhs_scale=plane,
-                start=(g == 0),
-                stop=(g == 1),
-            )
-
-        def store(acc, side, o, on_vector):
-            result = new("result%d%d" % (side, o), [P, SIDE], F32)
-            if on_vector:
-                nc.vector.tensor_scalar(
-                    out=result[:], in0=acc, scalar1=bias[:, o : o + 1], scalar2=None, op0=ALU.add
-                )
-            else:
-                nc.scalar.activation(out=result[:], in_=acc, func=ACT.Identity, bias=bias[:, o : o + 1])
-            nc.sync.dma_start(out[o * P : (o + 1) * P, side * SIDE : (side + 1) * SIDE], result[:])
-
-        for row in range(ROWS):
-            load_w2_scale_rows(nc.gpsimd, row)
-
-        w2_raw = [new("w2_raw%d" % ps, [P, 2 * H], U8) for ps in range(2)]
-
-        def load_w2(ps):
-            nc.sync.dma_start(w2_raw[ps][:].bitcast(I32), w2_words[ps].bitcast(I32))
 
         idx = load_list("idx", offs)
-        nc.scalar.dma_start(
-            tab_rows[0:QUAD, :].bitcast(I32), tab_scales.rearrange("ps q c -> (ps q) c").bitcast(I32)
-        )
-        top[0] = top[0] + 4096
+        nc.scalar.dma_start(tab_rows[0:QUAD, :].bitcast(I32), tab_scales.rearrange("ps q c -> (ps q) c").bitcast(I32))
+        reserve(ROW_BYTES - S // 2)
         v_rows = new("v_rows", [P, S], U8)
-        top[0] = top[0] + 1024
+        reserve(2 * PASS - S // 2)
         nc.vector.tensor_copy(v_rows[:], tab_rows[:].indirect(idx[:]))
-        load_page(0)
-        load_patch(0)
+
+        load_grid_rows(0)
         idx2 = load_list("idx2", offs2)
-        load_page(1)
-        load_patch(1)
+        load_grid_rows(1)
         raw_w1_0 = load_weight("raw_w1_0", w1, 0, PASS)
-        load_page(2)
-        load_patch(2)
-        raw_wg00 = load_wg(0, 0)
-        load_page(3)
-        load_patch(3)
-        move_table_plane(0, 0)
-        move_table_plane(0, 1)
+        load_grid_rows(2)
+        raw_wg00 = load_weight("raw_wg00", wg[0:PASS, :], 0, PASS)
+        load_grid_rows(3)
+        moves = [(ps, row) for ps in range(2) for row in range(ROWS)]
+        for ps, row in moves[0:2]:
+            move_table_plane(ps, row)
         raw_wg01a = load_weight("raw_wg01a", wg[PASS:, :], 0, PIECE)
-        move_table_plane(0, 2)
-        move_table_plane(0, 3)
-        move_table_plane(1, 0)
+        for ps, row in moves[2:5]:
+            move_table_plane(ps, row)
         tab_w0 = load_table_words(0)
-        move_table_plane(1, 1)
-        move_table_plane(1, 2)
-        move_table_plane(1, 3)
+        for ps, row in moves[5:8]:
+            move_table_plane(ps, row)
         tab_w1 = load_table_words(1)
-        top[0] = top[0] + 2048
+        reserve(ROW_BYTES // 2)
         raw_wg01b = load_weight("raw_wg01b", wg[PASS:, :], PIECE, PIECE)
-        top[0] = top[0] + 2048
+        reserve(ROW_BYTES // 2)
         idx3 = load_list("idx3", offs3)
-        load_w2(0)
-        raw_wg10 = load_wg(1, 0)
-        load_w2(1)
+        w2_raw0 = load_w2(0)
+        raw_wg10 = load_weight("raw_wg10", wg[0:PASS, :], PASS, PASS)
+        w2_raw1 = load_w2(1)
+
 
         w2_dealt_planes = new("w2_dealt_planes", [P, 2, H], U8)
         nc.gpsimd.tensor_copy(
@@ -331,153 +277,174 @@ def tile_list_foothold_terrain_blend_kernel(
 
         first_bf = new("first_bf", [P, 2, PASS * PACK], BF16)
         wg_bf01 = new("wg_bf01", [P, PASS * PACK], BF16)
-        round_columns(nc.scalar.copy, raw_w1_0, first_bf[:, 0, :], 0)
+        round_weight(nc.scalar.copy, raw_w1_0[:], first_bf[:, 0, :])
         pairs = new("pairs", [P, 2, 2, BANK, 2], BF16, on="raw_w1_0")
-        page_bf = [new("page_bf0", [P, BANK, PACK], BF16, on="v_rows", skip=64 - 4096), new("page_bf1", [P, BANK, PACK], BF16)]
+        page_bf = [
+            new("page_bf0", [P, BANK * PACK], BF16, on="v_rows", skip=S // 2 - ROW_BYTES),
+            new("page_bf1", [P, BANK * PACK], BF16),
+        ]
+        both = slice(0, 2)
         scatter_patch(0)
-        round_page(0, slice(0, 2))
+        round_page(0, both)
         scatter_patch(1)
-        round_page(1, slice(0, 2))
-        round_piece_in_order(raw_wg00[:, :, 0:PIECE], first_bf[:, 1, :], 0)
+        round_page(1, both)
+        round_first_piece(raw_wg00[:, :, 0:PIECE], first_bf[:, 1, :])
         scatter_patch(2)
-        round_page(2, slice(0, 2))
-        round_piece(nc.scalar.copy, raw_wg00[:, :, PIECE:], first_bf[:, 1, :], 1)
-        round_piece_in_order(raw_wg01a[:], wg_bf01[:], 0)
+        round_page(2, both)
+        round_weight(nc.scalar.copy, raw_wg00[:, :, PIECE:], first_bf[:, 1, :], PIECE)
+        round_first_piece(raw_wg01a[:], wg_bf01[:])
         scatter_patch(3)
         for h in range(2):
             round_page(3, slice(h, h + 1))
-        weave_page(1, nc.scalar.copy)
-        round_piece(nc.scalar.copy, raw_wg01b[:], wg_bf01[:], 1)
+        weave(nc.scalar.copy, page_bf[1][:], pairs[:, 1])
+        round_weight(nc.scalar.copy, raw_wg01b[:], wg_bf01[:], PIECE)
 
         v_words = new("v_words", [P, 2, S], U32)
-        raw_wg11 = load_wg(1, 1)
+        raw_wg11 = load_weight("raw_wg11", wg[PASS:, :], PASS, PASS)
         raw_w1_1 = load_weight("raw_w1_1", w1, PASS, PASS)
         wo_w = new("wo_w", [P, 2, N], I32)
         nc.sync.dma_start(wo_w[:], wo_words.rearrange("ps p c i -> p ps (c i)").bitcast(I32))
         for quad in range(P // QUAD):
-            load_wo_scale_rows(nc.sync, quad)
+            nc.sync.dma_start(
+                wo_planes[QUAD * quad : QUAD * quad + 2 * ROWS, :].bitcast(I32),
+                wo_scales[:, ROWS * quad : ROWS * (quad + 1), :].bitcast(I32),
+            )
         bias = new("bias", [P, OUT_TILES], F32)
         with nc.allow_non_contiguous_dma(reason="one bias value for each partition"):
             nc.sync.dma_start(bias[:], bo.rearrange("(o p) -> p o", p=P))
 
+
         nc.vector.tensor_copy(v_words[:, 0, :], tab_w0[:].bitcast(U32).indirect(idx[:]))
-        weave_page(0, nc.vector.tensor_copy)
-        first_codes, first_plane = quantise("first", first_bf[:].rearrange("p w c -> p (w c)"), 2 * PASS, "v_rows", 448)
+        weave(nc.vector.tensor_copy, page_bf[0][:], pairs[:, 0])
+        first_codes, first_plane = quantise(
+            "first", first_bf[:].rearrange("p w c -> p (w c)"), 2 * PASS, on="v_rows", skip=S // 2
+        )
         w1_q[0] = (first_codes[:, 0:PASS], first_plane[:, 0:PASS])
         wg_q[0, 0] = (first_codes[:, PASS:], first_plane[:, PASS:])
-        for h in range(2):
-            page_q[h] = quantise("page%d" % h, page_bf[h][:].rearrange("p c t -> p (c t)"), BANK, (None, "first_bf")[h])
+        page_q[0] = quantise("page0", page_bf[0][:], BANK)
+        page_q[1] = quantise("page1", page_bf[1][:], BANK, on="first_bf")
         nc.vector.tensor_copy(v_words[:, 1, :], tab_w1[:].bitcast(U32).indirect(idx[:]))
         wg_q[0, 1] = quantise("wg01", wg_bf01[:], PASS)
 
-        def deal_w2(ps):
-            nc.vector.tensor_copy(
-                out=w2_dealt[:, ps, :].bitcast(U16).rearrange("p (g t run y) -> p g run t y", g=2, t=PACK, y=8),
-                in_=w2_raw[ps][:].bitcast(U16).rearrange("p (g run y t) -> p g run t y", g=2, t=PACK, y=8),
-            )
+        deal_w2(0, w2_raw0)
+        wg_bf10 = new("wg_bf10", [P, PASS * PACK], BF16)
+        round_weight(nc.vector.tensor_copy, raw_wg10[:], wg_bf10[:])
+        deal_w2(1, w2_raw1)
 
-        w2_half = [
-            (w2_dealt[:, :, g * 2 * PASS : (g + 1) * 2 * PASS], w2_dealt_planes[:, :, g * PASS : (g + 1) * PASS])
-            for g in range(2)
-        ]
 
-        deal_w2(0)
-        wg_bf10 = dealt("wg_bf10", nc.vector.tensor_copy, raw_wg10)
-        deal_w2(1)
-        picked0 = [new("picked0%d" % pair, [P, 2, S], F32, on=("raw_wg10", None)[pair]) for pair in range(2)]
-        make_a(0, 0, "raw_wg01b", "s0", -2048)
-        make_a(1, 0, "raw_wg01b", "s1", 2048)
-        make_a(0, 1, None, "s2")
-        make_trust(0, None, "b0")
-        make_trust(1, None, "b1")
-        make_a(1, 1, None, "b0")
-        make_a(2, 0, "page0", "b1")
-        make_trust(2, None, "s0")
-        make_a(2, 1, None, "s0")
-        make_trust(3, None, "s1")
-        make_a(3, 0, "page1", "b1")
-        make_a(3, 1, None, "b0")
+        picked0 = [new("picked00", [P, 2, S], F32, on="raw_wg10"), new("picked01", [P, 2, S], F32)]
+        make_a(0, 0, bank("s0"), "raw_wg01b", -ROW_BYTES // 2)
+        make_a(1, 0, bank("s1"), "raw_wg01b", ROW_BYTES // 2)
+        make_a(0, 1, bank("s2"))
+        make_trust(0, bank("b0"))
+        make_trust(1, bank("b1"))
+        make_a(1, 1, bank("b0"))
+        make_a(2, 0, bank("b1"), "page0")
+        make_trust(2, bank("s0"))
+        make_a(2, 1, bank("s0"))
+        make_trust(3, bank("s1"))
+        make_a(3, 0, bank("b1"), "page1")
+        make_a(3, 1, bank("b0"))
         wg_bf11 = new("wg_bf11", [P, PASS * PACK], BF16)
-        round_columns(nc.scalar.copy, raw_wg11, wg_bf11, 0, 0, PASS - SHARE)
-        pick_into(picked0[0][:, 0, :], 0, 0, S)
+        round_weight(nc.scalar.copy, raw_wg11[:], wg_bf11[:])
+        pick(0, picked0[0][:, 0, :])
         wg_q[1, 0] = quantise("wg10", wg_bf10[:], PASS)
         for s in range(1, PACK):
-            pick_into(picked0[s // 2][:, s % 2, :], s, 0, S)
-        round_columns(nc.vector.tensor_copy, raw_wg11, wg_bf11, 0, PASS - SHARE, PASS)
-        rest_late = new("rest_late", [P, 2, S], F32)
+            pick(s, picked0[s // 2][:, s % 2, :])
+        rest23 = new("rest23", [P, 2, S], F32)
         for s in (2, 3):
-            rest_into(rest_late[:, s - 2, :], s, make_b(s, w2_half[0][0], w2_half[0][1], s))
+            make_rest(s, bank("b%d" % s), rest23[:, s - 2, :])
         wg_q[1, 1] = quantise("wg11", wg_bf11[:], PASS)
-        z0_rows = new("z0_rows", [P, 2, S, 2], BF16, on="raw_wg11")
-        nc.vector.tensor_tensor(
-            out=z0_rows[:, 1].rearrange("p (c e) t -> p c t e", e=PACK),
-            in0=picked0[1][:].rearrange("p t (c e) -> p c t e", e=PACK),
-            in1=rest_late[:].rearrange("p t (c e) -> p c t e", e=PACK),
-            op=ALU.subtract,
-        )
-        w1_bf1 = [new("w1_bf1", [P, PIECE * PACK], BF16)[:], z0_rows[:, 0].rearrange("p c e -> p (c e)")]
+
+        z0_pairs = new("z0_pairs", [P, 2, S, 2], BF16, on="raw_wg11")
+        subtract_interleaved(z0_pairs[:, 1].rearrange("p c e -> p (c e)"), picked0[1][:], rest23[:], 2)
+
+        w1_bf1 = [new("w1_bf1", [P, PIECE * PACK], BF16)[:], z0_pairs[:, 0].rearrange("p c e -> p (c e)")]
         w1_codes1 = new("w1_codes1", [P, PASS], U32, on="tab_w0")
         w1_plane1 = new("w1_plane1", [P, PASS], U8)
         w1_q[1] = (w1_codes1, w1_plane1)
-
-        def second_w1(pair):
+        rest01 = [new("rest%d" % s, [P, S], F32, on=("raw_wg11", "raw_w1_1")[s], skip=ROW_BYTES) for s in range(2)]
+        for pair in range(2):
             nc.scalar.copy(
                 out=w1_bf1[pair].rearrange("p (t x j) -> p x j t", t=2, j=PACK),
                 in_=raw_w1_1[:].rearrange("p j (x t) -> p x j t", t=PACK)[:, :, :, 2 * pair : 2 * pair + 2],
             )
             columns = slice(pair * PIECE, (pair + 1) * PIECE)
-            nc.vector.quantize_mx(out=w1_codes1[:, columns].bitcast(FP8X4), scales=w1_plane1[:, columns], in_=w1_bf1[pair])
-
-        second_w1(0)
-        rest_early = [new("rest_early%d" % s, [P, S], F32, on=(None, "raw_w1_1")[s]) for s in range(2)]
-        rest_into(rest_early[0][:], 0, make_b(0, w2_half[0][0], w2_half[0][1], 0))
-        second_w1(1)
-        rest_into(rest_early[1][:], 1, make_b(1, w2_half[0][0], w2_half[0][1], 1))
+            nc.vector.quantize_mx(
+                out=w1_codes1[:, columns].bitcast(FP8X4), scales=w1_plane1[:, columns], in_=w1_bf1[pair]
+            )
+            make_rest(pair, bank("b%d" % pair), rest01[pair][:])
         for s in range(2):
-            nc.gpsimd.tensor_tensor(out=z0_rows[:, 0, :, s], in0=picked0[0][:, s, :], in1=rest_early[s][:], op=ALU.subtract)
+            nc.gpsimd.tensor_tensor(out=z0_pairs[:, 0, :, s], in0=picked0[0][:, s, :], in1=rest01[s][:], op=ALU.subtract)
+
+
         for s in range(PACK, 2 * PACK):
-            make_trust(s)
+            make_trust(s, next_bank())
         rest1 = new("rest1", [P, PACK, S], F32)
 
         def second_rest(s):
-            rest_into(rest1[:, s - PACK, :], s, make_b(s, w2_half[1][0], w2_half[1][1], s - PACK))
+            make_rest(s, bank("b%d" % ((s + 2) % PACK)), rest1[:, s - PACK, :])
 
         def both_halves(s, on):
-            make_a(s, 0, on)
-            make_a(s, 1)
+            make_a(s, 0, next_bank(), on)
+            make_a(s, 1, next_bank())
 
-        second_rest(6)
-        second_rest(7)
+        for s in (4, 5, 6):
+            second_rest(s)
         both_halves(4, "page2")
-        make_a(5, 0, "page3")
-        second_rest(4)
-        second_rest(5)
-        make_a(5, 1)
+        second_rest(7)
+        both_halves(5, "page3")
         both_halves(6, "raw_wg00")
         both_halves(7, "raw_wg01a")
         z0_bf = new("z0_bf", [P, S * PACK], BF16, on="w1_codes1")
-        nc.scalar.copy(
-            out=z0_bf[:].bitcast(F32),
-            in_=z0_rows[:].rearrange("p u c e -> p u (c e)").bitcast(F32).rearrange("p u c -> p c u"),
-        )
+        weave(nc.scalar.copy, z0_bf[:], z0_pairs[:])
         picked1 = [new("picked1%d" % side, [P, PACK, SIDE], F32) for side in range(2)]
         for s in range(PACK, 2 * PACK):
             for side in range(2):
-                pick_into(picked1[side][:, s - PACK, :], s, side * SIDE, SIDE)
-        sums = [[bank("b%d" % o, [P, SIDE])[:] for o in range(OUT_TILES)], [next_bank([P, SIDE])[:] for o in range(OUT_TILES)]]
+                pick(s, picked1[side][:, s - PACK, :], side * SIDE, SIDE)
 
-        def last_passes(g, side, src):
+
+        sums = [
+            [bank("b%d" % o, SIDE) for o in range(OUT_TILES)],
+            [next_bank(SIDE) for o in range(OUT_TILES)],
+        ]
+
+        def second_z(side):
+            z_bf = new("z1%d_bf" % side, [P, SIDE * PACK], BF16, on="z0_pairs", skip=side * ROW_BYTES // 2)
+            subtract_interleaved(z_bf[:], picked1[side][:], rest1[:, :, side * SIDE : (side + 1) * SIDE], PACK)
+            return z_bf
+
+        def read_out(g, side, src):
             codes, plane = quantise("z%d%d" % (g, side), src, SIDE)
             for o in range(OUT_TILES):
-                read_out(sums[side][o], g, o, codes[:], plane[:])
+                rows = slice(o * P, (o + 1) * P)
+                nc.tensor.matmul_mx(
+                    out=sums[side][o][:],
+                    lhsT=wo_w[:, g, rows].bitcast(FP8X4),
+                    lhsT_scale=wo_planes[ROWS * g : P, rows],
+                    rhs=codes[:].bitcast(FP8X4),
+                    rhs_scale=plane[:],
+                    start=(g == 0),
+                    stop=(g == 1),
+                )
 
-        last_passes(0, 0, z0_bf[:, 0 : SIDE * PACK])
-        z10_bf = finish_z("z10", picked1[0][:], rest1, 0, SIDE, 0)
-        last_passes(0, 1, z0_bf[:, SIDE * PACK :])
-        last_passes(1, 0, z10_bf[:])
+        def store(side, o, on_vector):
+            result = new("result%d%d" % (side, o), [P, SIDE], F32)
+            if on_vector:
+                nc.vector.tensor_scalar(
+                    out=result[:], in0=sums[side][o][:], scalar1=bias[:, o : o + 1], scalar2=None, op0=ALU.add
+                )
+            else:
+                nc.scalar.activation(out=result[:], in_=sums[side][o][:], func=ACT.Identity, bias=bias[:, o : o + 1])
+            nc.sync.dma_start(out[o * P : (o + 1) * P, side * SIDE : (side + 1) * SIDE], result[:])
+
+        read_out(0, 0, z0_bf[:, 0 : SIDE * PACK])
+        z10_bf = second_z(0)
+        read_out(0, 1, z0_bf[:, SIDE * PACK :])
+        read_out(1, 0, z10_bf[:])
         for o in range(OUT_TILES):
-            store(sums[0][o], 0, o, False)
-        z11_bf = finish_z("z11", picked1[1][:], rest1, SIDE, SIDE, 2048)
-        last_passes(1, 1, z11_bf[:])
+            store(0, o, False)
+        z11_bf = second_z(1)
+        read_out(1, 1, z11_bf[:])
         for o in range(OUT_TILES):
-            store(sums[1][o], 1, o, o != 1)
+            store(1, o, o != 1)

@@ -196,13 +196,8 @@ def tile_list_foothold_terrain_blend_kernel(
                 out=dst, in0=trust[s][:], scalar=1.0, in1=acc[:], op0=ALU.subtract, op1=ALU.mult
             )
 
-        def pick(s, dst, first=0, width=S):
-            nc.vector.tensor_tensor(
-                out=dst,
-                in0=a_rows[s][:].indirect(idx3[:, first // PER_COLUMN : (first + width) // PER_COLUMN]),
-                in1=trust[s][:, first : first + width],
-                op=ALU.mult,
-            )
+        def pick(s, dst):
+            nc.vector.tensor_tensor(out=dst, in0=a_rows[s][:].indirect(idx3[:]), in1=trust[s][:], op=ALU.mult)
 
         def subtract_interleaved(dst, picked, rest, slices):
             run = 8 // slices
@@ -398,10 +393,9 @@ def tile_list_foothold_terrain_blend_kernel(
         both_halves(7, "raw_wg01a")
         z0_bf = new("z0_bf", [P, S * PACK], BF16, on="w1_codes1")
         weave(nc.scalar.copy, z0_bf[:], z0_pairs[:])
-        picked1 = [new("picked1%d" % side, [P, PACK, SIDE], F32) for side in range(2)]
+        picked1 = new("picked1", [P, PACK, S], F32)
         for s in range(PACK, 2 * PACK):
-            for side in range(2):
-                pick(s, picked1[side][:, s - PACK, :], side * SIDE, SIDE)
+            pick(s, picked1[:, s - PACK, :])
 
 
         sums = [
@@ -411,7 +405,8 @@ def tile_list_foothold_terrain_blend_kernel(
 
         def second_z(side):
             z_bf = new("z1%d_bf" % side, [P, SIDE * PACK], BF16, on="z0_pairs", skip=side * ROW_BYTES // 2)
-            subtract_interleaved(z_bf[:], picked1[side][:], rest1[:, :, side * SIDE : (side + 1) * SIDE], PACK)
+            entries = slice(side * SIDE, (side + 1) * SIDE)
+            subtract_interleaved(z_bf[:], picked1[:, :, entries], rest1[:, :, entries], PACK)
             return z_bf
 
         def read_out(g, side, src):

@@ -25,6 +25,7 @@ ROWS = 4
 BLOCKS = 16
 PER_COLUMN = 16
 PIECE = PASS // 2
+BESIDE = 256
 SIDE = S // 2
 OUT_TILES = N // P
 RING = 4
@@ -65,7 +66,7 @@ def tile_list_foothold_terrain_blend_kernel(
 
         def next_bank(columns=BANK):
             turns.append(columns)
-            return bank("s%d" % ((len(turns) - 1) % RING), columns)
+            return bank(("s1", "s2", "s0", "b0")[(len(turns) - 1) % RING], columns)
 
 
         def load_list(name, src):
@@ -82,8 +83,8 @@ def tile_list_foothold_terrain_blend_kernel(
             patch[t] = new("patch%d" % t, [P, S], F32)
             nc.sync.dma_start(patch[t][:], xs.rearrange("(p t) c -> p t c", t=PACK)[:, t, :])
 
-        def load_weight(name, rows, first, width):
-            raw = new(name, [P, PACK, width], F32)
+        def load_weight(name, rows, first, width, on=None, skip=0):
+            raw = new(name, [P, PACK, width], F32, on=on, skip=skip)
             nc.sync.dma_start(raw[:], rows.rearrange("(p j) c -> p j c", j=PACK)[:, :, first : first + width])
             return raw
 
@@ -111,11 +112,21 @@ def tile_list_foothold_terrain_blend_kernel(
                 in_=raw.rearrange("p j (x t) -> p x j t", t=PACK),
             )
 
-        def round_first_piece(raw, dst):
+        def round_first_piece(raw, dst, width=PIECE):
             nc.gpsimd.tensor_copy(
-                out=dst.rearrange("p (t x j) -> p t x j", t=PACK, j=PACK)[:, :, 0 : PIECE // PACK],
+                out=dst.rearrange("p (t x j) -> p t x j", t=PACK, j=PACK)[:, :, 0 : width // PACK],
                 in_=raw.rearrange("p j (x t) -> p t x j", t=PACK),
             )
+
+        def round_pair(copy, raw, pair, dst):
+            copy(
+                out=dst.rearrange("p (t x j) -> p x j t", t=2, j=PACK),
+                in_=raw.rearrange("p j (x t) -> p x j t", t=PACK)[:, :, :, 2 * pair : 2 * pair + 2],
+            )
+
+        def quantise_pair(codes, plane, pair, src):
+            columns = slice(pair * PIECE, (pair + 1) * PIECE)
+            nc.vector.quantize_mx(out=codes[:, columns].bitcast(FP8X4), scales=plane[:, columns], in_=src)
 
         def quantise(name, src, columns, on=None, skip=0):
             codes = new(name + "_codes", [P, columns], U32)
@@ -135,10 +146,10 @@ def tile_list_foothold_terrain_blend_kernel(
         def weave(copy, dst, src):
             copy(out=dst.bitcast(F32), in_=src.rearrange("p u c e -> p u (c e)").bitcast(F32).rearrange("p u c -> p c u"))
 
-        def deal_w2(ps, raw):
+        def deal_w2(ps):
             nc.vector.tensor_copy(
                 out=w2_dealt[:, ps, :].bitcast(U16).rearrange("p (g t run y) -> p g run t y", g=2, t=PACK, y=8),
-                in_=raw[:].bitcast(U16).rearrange("p (g run y t) -> p g run t y", g=2, t=PACK, y=8),
+                in_=w2_raw[ps][:].bitcast(U16).rearrange("p (g run y t) -> p g run t y", g=2, t=PACK, y=8),
             )
 
 
@@ -164,18 +175,18 @@ def tile_list_foothold_terrain_blend_kernel(
             )
             nc.scalar.copy(out=a_rows[s][:, h * BANK : (h + 1) * BANK], in_=acc[:])
 
-        def make_trust(s, acc):
+        def make_trust(s, acc, first=0):
             g, t = divmod(s, PACK)
             rows = slice(t * P, (t + 1) * P)
-            for ps in range(2):
+            for ps in (first, 1 - first):
                 nc.tensor.matmul_mx(
                     out=acc[:],
                     lhsT=wg_q[g, ps][0][:, rows].bitcast(FP8X4),
                     lhsT_scale=wg_q[g, ps][1][:, rows],
                     rhs=v_words[:, ps, :].bitcast(FP8X4),
                     rhs_scale=v_planes[:, ps, :],
-                    start=(ps == 0),
-                    stop=(ps == 1),
+                    start=(ps == first),
+                    stop=(ps != first),
                 )
             trust[s] = new("trust%d" % s, [P, S], F32)
             nc.scalar.activation(out=trust[s][:], in_=acc[:], func=ACT.Sigmoid)
@@ -257,10 +268,9 @@ def tile_list_foothold_terrain_blend_kernel(
         reserve(ROW_BYTES // 2)
         raw_wg01b = load_weight("raw_wg01b", wg[PASS:, :], PIECE, PIECE)
         reserve(ROW_BYTES // 2)
-        idx3 = load_list("idx3", offs3)
-        w2_raw0 = load_w2(0)
         raw_wg10 = load_weight("raw_wg10", wg[0:PASS, :], PASS, PASS)
-        w2_raw1 = load_w2(1)
+        w2_raw = [load_w2(0), load_w2(1)]
+        idx3 = load_list("idx3", offs3)
 
 
         w2_dealt_planes = new("w2_dealt_planes", [P, 2, H], U8)
@@ -295,7 +305,9 @@ def tile_list_foothold_terrain_blend_kernel(
         round_weight(nc.scalar.copy, raw_wg01b[:], wg_bf01[:], PIECE)
 
         v_words = new("v_words", [P, 2, S], U32)
-        raw_wg11 = load_weight("raw_wg11", wg[PASS:, :], PASS, PASS)
+        reserve(ROW_BYTES + 16 * BESIDE)
+        raw_wg11b = load_weight("raw_wg11b", wg[PASS:, :], PASS + BESIDE, PASS - BESIDE)
+        raw_wg11a = load_weight("raw_wg11a", wg[PASS:, :], PASS, BESIDE, "raw_wg11b", -16 * BESIDE)
         raw_w1_1 = load_weight("raw_w1_1", w1, PASS, PASS)
         wo_w = new("wo_w", [P, 2, N], I32)
         nc.sync.dma_start(wo_w[:], wo_words.rearrange("ps p c i -> p ps (c i)").bitcast(I32))
@@ -319,78 +331,77 @@ def tile_list_foothold_terrain_blend_kernel(
         page_q[0] = quantise("page0", page_bf[0][:], BANK)
         page_q[1] = quantise("page1", page_bf[1][:], BANK, on="first_bf")
         nc.vector.tensor_copy(v_words[:, 1, :], tab_w1[:].bitcast(U32).indirect(idx[:]))
+        reserve(ROW_BYTES // 2)
         wg_q[0, 1] = quantise("wg01", wg_bf01[:], PASS)
+        reserve(ROW_BYTES - PASS)
 
-        deal_w2(0, w2_raw0)
-        wg_bf10 = new("wg_bf10", [P, PASS * PACK], BF16)
-        round_weight(nc.vector.tensor_copy, raw_wg10[:], wg_bf10[:])
-        deal_w2(1, w2_raw1)
+        wg_bf10 = [new("wg_bf10a", [P, PIECE * PACK], BF16)]
+        round_pair(nc.vector.tensor_copy, raw_wg10[:], 0, wg_bf10[0][:])
+        deal_w2(0)
+        deal_w2(1)
 
 
-        picked0 = [new("picked00", [P, 2, S], F32, on="raw_wg10"), new("picked01", [P, 2, S], F32)]
         make_a(0, 0, bank("s0"), "raw_wg01b", -ROW_BYTES // 2)
         make_a(1, 0, bank("s1"), "raw_wg01b", ROW_BYTES // 2)
         make_a(0, 1, bank("s2"))
         make_trust(0, bank("b0"))
+        make_a(1, 1, bank("s0"))
         make_trust(1, bank("b1"))
-        make_a(1, 1, bank("b0"))
-        make_a(2, 0, bank("b1"), "page0")
-        make_trust(2, bank("s0"))
-        make_a(2, 1, bank("s0"))
-        make_trust(3, bank("s1"))
-        make_a(3, 0, bank("b1"), "page1")
-        make_a(3, 1, bank("b0"))
-        wg_bf11 = new("wg_bf11", [P, PASS * PACK], BF16)
-        round_weight(nc.scalar.copy, raw_wg11[:], wg_bf11[:])
-        pick(0, picked0[0][:, 0, :])
-        wg_q[1, 0] = quantise("wg10", wg_bf10[:], PASS)
-        for s in range(1, PACK):
-            pick(s, picked0[s // 2][:, s % 2, :])
-        rest23 = new("rest23", [P, 2, S], F32)
         for s in (2, 3):
-            make_rest(s, bank("b%d" % s), rest23[:, s - 2, :])
+            make_trust(s, bank("b%d" % s), 1)
+        make_a(2, 0, bank("s1"), "wg01_codes", -ROW_BYTES // 2)
+        make_a(2, 1, bank("s2"))
+        make_a(3, 0, bank("s0"), "wg01_plane")
+        make_a(3, 1, bank("b0"))
+        picked01 = new("picked01", [P, 2, S], F32)
+        rest0 = [new("rest0%d" % u, [P, 2, S], F32, on="page%d" % u) for u in range(2)]
+        for s in range(2):
+            pick(s, picked01[:, s, :])
+        wg_bf11 = new("wg_bf11", [P, PASS * PACK], BF16, on="a0")
+        round_first_piece(raw_wg11a[:], wg_bf11[:], BESIDE)
+        for s in range(PACK):
+            make_rest(s, bank(("b1", "b2", "b3", "s3")[s]), rest0[s // 2][:, s % 2, :])
+        wg_q[1, 0] = (
+            new("wg10_codes", [P, PASS], U32),
+            new("wg10_plane", [P, PASS], U8, on="raw_wg11a", skip=ALIGN),
+        )
+        picked2 = new("picked2", [P, S], F32, on="raw_wg11a", skip=ALIGN + PASS)
+        z0_pairs = new("z0_pairs", [P, 2, S, 2], BF16, on="raw_wg11a", skip=ALIGN - ROW_BYTES)
+        wg_bf10.append(new("wg_bf10b", [P, PIECE * PACK], BF16, on="first_codes"))
+        round_pair(nc.scalar.copy, raw_wg10[:], 1, wg_bf10[1][:])
+        round_weight(nc.scalar.copy, raw_wg11b[:], wg_bf11[:], BESIDE)
+        quantise_pair(wg_q[1, 0][0], wg_q[1, 0][1], 0, wg_bf10[0][:])
+        pick(2, picked2[:])
+        quantise_pair(wg_q[1, 0][0], wg_q[1, 0][1], 1, wg_bf10[1][:])
+        subtract_interleaved(z0_pairs[:, 0].rearrange("p c e -> p (c e)"), picked01[:], rest0[0][:], 2)
         wg_q[1, 1] = quantise("wg11", wg_bf11[:], PASS)
+        picked3 = new("picked3", [P, S], F32, on="raw_wg11b", skip=-ALIGN)
+        pick(3, picked3[:])
 
-        z0_pairs = new("z0_pairs", [P, 2, S, 2], BF16, on="raw_wg11")
-        subtract_interleaved(z0_pairs[:, 1].rearrange("p c e -> p (c e)"), picked0[1][:], rest23[:], 2)
-
-        w1_bf1 = [new("w1_bf1", [P, PIECE * PACK], BF16)[:], z0_pairs[:, 0].rearrange("p c e -> p (c e)")]
+        w1_bf1 = [
+            z0_pairs[:, 1].rearrange("p c e -> p (c e)"),
+            new("w1_bf1", [P, PIECE * PACK], BF16, on="raw_wg11b", skip=ROW_BYTES // 2)[:],
+        ]
         w1_codes1 = new("w1_codes1", [P, PASS], U32, on="tab_w0")
         w1_plane1 = new("w1_plane1", [P, PASS], U8)
         w1_q[1] = (w1_codes1, w1_plane1)
-        rest01 = [new("rest%d" % s, [P, S], F32, on=("raw_wg11", "raw_w1_1")[s], skip=ROW_BYTES) for s in range(2)]
         for pair in range(2):
-            nc.scalar.copy(
-                out=w1_bf1[pair].rearrange("p (t x j) -> p x j t", t=2, j=PACK),
-                in_=raw_w1_1[:].rearrange("p j (x t) -> p x j t", t=PACK)[:, :, :, 2 * pair : 2 * pair + 2],
+            round_pair(nc.scalar.copy, raw_w1_1[:], pair, w1_bf1[pair])
+            quantise_pair(w1_codes1, w1_plane1, pair, w1_bf1[pair])
+        for s in (2, 3):
+            nc.gpsimd.tensor_tensor(
+                out=z0_pairs[:, 1, :, s - 2], in0=(picked2, picked3)[s - 2][:], in1=rest0[1][:, s - 2, :], op=ALU.subtract
             )
-            columns = slice(pair * PIECE, (pair + 1) * PIECE)
-            nc.vector.quantize_mx(
-                out=w1_codes1[:, columns].bitcast(FP8X4), scales=w1_plane1[:, columns], in_=w1_bf1[pair]
-            )
-            make_rest(pair, bank("b%d" % pair), rest01[pair][:])
-        for s in range(2):
-            nc.gpsimd.tensor_tensor(out=z0_pairs[:, 0, :, s], in0=picked0[0][:, s, :], in1=rest01[s][:], op=ALU.subtract)
 
 
         for s in range(PACK, 2 * PACK):
             make_trust(s, next_bank())
         rest1 = new("rest1", [P, PACK, S], F32)
-
-        def second_rest(s):
-            make_rest(s, bank("b%d" % ((s + 2) % PACK)), rest1[:, s - PACK, :])
-
-        def both_halves(s, on):
+        for s in range(PACK, 2 * PACK):
+            make_rest(s, bank(("b1", "b2", "b3", "s3")[s - PACK]), rest1[:, s - PACK, :])
+        for s, on in ((4, "page2"), (5, "page3"), (6, "raw_wg00"), (7, "raw_wg01a")):
             make_a(s, 0, next_bank(), on)
             make_a(s, 1, next_bank())
-
-        for s in (4, 5, 6):
-            second_rest(s)
-        both_halves(4, "page2")
-        second_rest(7)
-        both_halves(5, "page3")
-        both_halves(6, "raw_wg00")
-        both_halves(7, "raw_wg01a")
         z0_bf = new("z0_bf", [P, S * PACK], BF16, on="w1_codes1")
         weave(nc.scalar.copy, z0_bf[:], z0_pairs[:])
         picked1 = new("picked1", [P, PACK, S], F32)
@@ -399,7 +410,7 @@ def tile_list_foothold_terrain_blend_kernel(
 
 
         sums = [
-            [bank("b%d" % o, SIDE) for o in range(OUT_TILES)],
+            [bank("b%d" % (o + 1), SIDE) for o in range(OUT_TILES)],
             [next_bank(SIDE) for o in range(OUT_TILES)],
         ]
 

@@ -25,7 +25,7 @@ ROWS = 4
 BLOCKS = 16
 PER_COLUMN = 16
 PIECE = PASS // 2
-BESIDE = 256
+BESIDE = 320
 SIDE = S // 2
 OUT_TILES = N // P
 RING = 4
@@ -66,7 +66,7 @@ def tile_list_foothold_terrain_blend_kernel(
 
         def next_bank(columns=BANK):
             turns.append(columns)
-            return bank(("s1", "s2", "s0", "b0")[(len(turns) - 1) % RING], columns)
+            return bank(("s1", "s2", "s0", "s3")[(len(turns) - 1) % RING], columns)
 
 
         def load_list(name, src):
@@ -110,12 +110,6 @@ def tile_list_foothold_terrain_blend_kernel(
             copy(
                 out=dst.rearrange("p (t x j) -> p x j t", t=PACK, j=PACK)[:, at // PACK : (at + width) // PACK],
                 in_=raw.rearrange("p j (x t) -> p x j t", t=PACK),
-            )
-
-        def round_first_piece(raw, dst, width=PIECE):
-            nc.gpsimd.tensor_copy(
-                out=dst.rearrange("p (t x j) -> p t x j", t=PACK, j=PACK)[:, :, 0 : width // PACK],
-                in_=raw.rearrange("p j (x t) -> p t x j", t=PACK),
             )
 
         def round_pair(copy, raw, pair, dst):
@@ -191,17 +185,17 @@ def tile_list_foothold_terrain_blend_kernel(
             trust[s] = new("trust%d" % s, [P, S], F32)
             nc.scalar.activation(out=trust[s][:], in_=acc[:], func=ACT.Sigmoid)
 
-        def make_rest(s, acc, dst):
+        def make_rest(s, acc, dst, first=0):
             columns = slice(s * P, (s + 1) * P)
-            for ps in range(2):
+            for ps in (first, 1 - first):
                 nc.tensor.matmul_mx(
                     out=acc[:],
                     lhsT=w2_dealt[:, ps, 2 * s * P : 2 * (s + 1) * P].bitcast(FP4X4),
                     lhsT_scale=w2_dealt_planes[:, ps, columns],
                     rhs=v_words[:, ps, :].bitcast(FP8X4),
                     rhs_scale=v_planes[:, ps, :],
-                    start=(ps == 0),
-                    stop=(ps == 1),
+                    start=(ps == first),
+                    stop=(ps != first),
                 )
             nc.vector.scalar_tensor_tensor(
                 out=dst, in0=trust[s][:], scalar=1.0, in1=acc[:], op0=ALU.subtract, op1=ALU.mult
@@ -293,11 +287,10 @@ def tile_list_foothold_terrain_blend_kernel(
         round_page(0, both)
         scatter_patch(1)
         round_page(1, both)
-        round_first_piece(raw_wg00[:, :, 0:PIECE], first_bf[:, 1, :])
+        round_weight(nc.gpsimd.tensor_copy, raw_wg00[:], first_bf[:, 1, :])
         scatter_patch(2)
         round_page(2, both)
-        round_weight(nc.scalar.copy, raw_wg00[:, :, PIECE:], first_bf[:, 1, :], PIECE)
-        round_first_piece(raw_wg01a[:], wg_bf01[:])
+        round_weight(nc.gpsimd.tensor_copy, raw_wg01a[:], wg_bf01[:])
         scatter_patch(3)
         for h in range(2):
             round_page(3, slice(h, h + 1))
@@ -305,9 +298,9 @@ def tile_list_foothold_terrain_blend_kernel(
         round_weight(nc.scalar.copy, raw_wg01b[:], wg_bf01[:], PIECE)
 
         v_words = new("v_words", [P, 2, S], U32)
-        reserve(ROW_BYTES + 16 * BESIDE)
         raw_wg11b = load_weight("raw_wg11b", wg[PASS:, :], PASS + BESIDE, PASS - BESIDE)
-        raw_wg11a = load_weight("raw_wg11a", wg[PASS:, :], PASS, BESIDE, "raw_wg11b", -16 * BESIDE)
+        reserve(ROW_BYTES)
+        raw_wg11a = load_weight("raw_wg11a", wg[PASS:, :], PASS, BESIDE)
         raw_w1_1 = load_weight("raw_w1_1", w1, PASS, PASS)
         wo_w = new("wo_w", [P, 2, N], I32)
         nc.sync.dma_start(wo_w[:], wo_words.rearrange("ps p c i -> p ps (c i)").bitcast(I32))
@@ -358,47 +351,46 @@ def tile_list_foothold_terrain_blend_kernel(
         for s in range(2):
             pick(s, picked01[:, s, :])
         wg_bf11 = new("wg_bf11", [P, PASS * PACK], BF16, on="a0")
-        round_first_piece(raw_wg11a[:], wg_bf11[:], BESIDE)
-        for s in range(PACK):
-            make_rest(s, bank(("b1", "b2", "b3", "s3")[s]), rest0[s // 2][:, s % 2, :])
+        round_weight(nc.gpsimd.tensor_copy, raw_wg11a[:], wg_bf11[:])
+        for s, tag in ((0, "b1"), (2, "b2"), (3, "b3")):
+            make_rest(s, bank(tag), rest0[s // 2][:, s % 2, :], s // 2)
         wg_q[1, 0] = (
             new("wg10_codes", [P, PASS], U32),
-            new("wg10_plane", [P, PASS], U8, on="raw_wg11a", skip=ALIGN),
+            new("wg10_plane", [P, PASS], U8, on="raw_wg11a"),
         )
-        picked2 = new("picked2", [P, S], F32, on="raw_wg11a", skip=ALIGN + PASS)
-        z0_pairs = new("z0_pairs", [P, 2, S, 2], BF16, on="raw_wg11a", skip=ALIGN - ROW_BYTES)
+        picked23 = new("picked23", [P, 2, S], F32, on="raw_wg11a", skip=PASS)
         wg_bf10.append(new("wg_bf10b", [P, PIECE * PACK], BF16, on="first_codes"))
         round_pair(nc.scalar.copy, raw_wg10[:], 1, wg_bf10[1][:])
         round_weight(nc.scalar.copy, raw_wg11b[:], wg_bf11[:], BESIDE)
         quantise_pair(wg_q[1, 0][0], wg_q[1, 0][1], 0, wg_bf10[0][:])
-        pick(2, picked2[:])
+        pick(2, picked23[:, 0, :])
         quantise_pair(wg_q[1, 0][0], wg_q[1, 0][1], 1, wg_bf10[1][:])
-        subtract_interleaved(z0_pairs[:, 0].rearrange("p c e -> p (c e)"), picked01[:], rest0[0][:], 2)
+        pick(3, picked23[:, 1, :])
         wg_q[1, 1] = quantise("wg11", wg_bf11[:], PASS)
-        picked3 = new("picked3", [P, S], F32, on="raw_wg11b", skip=-ALIGN)
-        pick(3, picked3[:])
 
+        z0_pairs = new("z0_pairs", [P, 2, S, 2], BF16, on="raw_wg11b", skip=ALIGN)
         w1_bf1 = [
-            z0_pairs[:, 1].rearrange("p c e -> p (c e)"),
-            new("w1_bf1", [P, PIECE * PACK], BF16, on="raw_wg11b", skip=ROW_BYTES // 2)[:],
+            new("w1_bf1", [P, PIECE * PACK], BF16, on="raw_wg10")[:],
+            z0_pairs[:, 0].rearrange("p c e -> p (c e)"),
         ]
         w1_codes1 = new("w1_codes1", [P, PASS], U32, on="tab_w0")
         w1_plane1 = new("w1_plane1", [P, PASS], U8)
         w1_q[1] = (w1_codes1, w1_plane1)
+        subtract_interleaved(z0_pairs[:, 1].rearrange("p c e -> p (c e)"), picked23[:], rest0[1][:], 2)
         for pair in range(2):
             round_pair(nc.scalar.copy, raw_w1_1[:], pair, w1_bf1[pair])
             quantise_pair(w1_codes1, w1_plane1, pair, w1_bf1[pair])
-        for s in (2, 3):
-            nc.gpsimd.tensor_tensor(
-                out=z0_pairs[:, 1, :, s - 2], in0=(picked2, picked3)[s - 2][:], in1=rest0[1][:, s - 2, :], op=ALU.subtract
-            )
+        late_rest = new("late_rest", [P, S], F32, on="raw_w1_1")
+        make_rest(1, bank("b0"), late_rest[:])
+        for s, rest in ((0, rest0[0][:, 0, :]), (1, late_rest[:])):
+            nc.gpsimd.tensor_tensor(out=z0_pairs[:, 0, :, s], in0=picked01[:, s, :], in1=rest, op=ALU.subtract)
 
 
         for s in range(PACK, 2 * PACK):
             make_trust(s, next_bank())
         rest1 = new("rest1", [P, PACK, S], F32)
         for s in range(PACK, 2 * PACK):
-            make_rest(s, bank(("b1", "b2", "b3", "s3")[s - PACK]), rest1[:, s - PACK, :])
+            make_rest(s, bank(("b1", "b2", "b3", "b0")[s - PACK]), rest1[:, s - PACK, :])
         for s, on in ((4, "page2"), (5, "page3"), (6, "raw_wg00"), (7, "raw_wg01a")):
             make_a(s, 0, next_bank(), on)
             make_a(s, 1, next_bank())
@@ -409,29 +401,32 @@ def tile_list_foothold_terrain_blend_kernel(
             pick(s, picked1[:, s - PACK, :])
 
 
+        parts = ((0, SIDE), (SIDE, SIDE // 2), (SIDE + SIDE // 2, SIDE // 2))
         sums = [
             [bank("b%d" % (o + 1), SIDE) for o in range(OUT_TILES)],
             [next_bank(SIDE) for o in range(OUT_TILES)],
         ]
 
-        def second_z(side):
-            z_bf = new("z1%d_bf" % side, [P, SIDE * PACK], BF16, on="z0_pairs", skip=side * ROW_BYTES // 2)
-            entries = slice(side * SIDE, (side + 1) * SIDE)
+        def second_z(part):
+            first, width = parts[part]
+            z_bf = new("z1%d_bf" % part, [P, width * PACK], BF16, on="z0_pairs", skip=first * PACK * 2)
+            entries = slice(first, first + width)
             subtract_interleaved(z_bf[:], picked1[:, :, entries], rest1[:, :, entries], PACK)
             return z_bf
 
-        def read_out(g, side, src):
-            codes, plane = quantise("z%d%d" % (g, side), src, SIDE)
+        def read_out(g, name, first, width, src, stop):
+            codes, plane = quantise(name, src, width)
+            side, column = divmod(first, SIDE)
             for o in range(OUT_TILES):
                 rows = slice(o * P, (o + 1) * P)
                 nc.tensor.matmul_mx(
-                    out=sums[side][o][:],
+                    out=sums[side][o][:, column : column + width],
                     lhsT=wo_w[:, g, rows].bitcast(FP8X4),
                     lhsT_scale=wo_planes[ROWS * g : P, rows],
                     rhs=codes[:].bitcast(FP8X4),
                     rhs_scale=plane[:],
                     start=(g == 0),
-                    stop=(g == 1),
+                    stop=stop,
                 )
 
         def store(side, o, on_vector):
@@ -444,13 +439,14 @@ def tile_list_foothold_terrain_blend_kernel(
                 nc.scalar.activation(out=result[:], in_=sums[side][o][:], func=ACT.Identity, bias=bias[:, o : o + 1])
             nc.sync.dma_start(out[o * P : (o + 1) * P, side * SIDE : (side + 1) * SIDE], result[:])
 
-        read_out(0, 0, z0_bf[:, 0 : SIDE * PACK])
+        read_out(0, "z00", 0, SIDE, z0_bf[:, 0 : SIDE * PACK], False)
         z10_bf = second_z(0)
-        read_out(0, 1, z0_bf[:, SIDE * PACK :])
-        read_out(1, 0, z10_bf[:])
+        read_out(0, "z01", SIDE, SIDE, z0_bf[:, SIDE * PACK :], False)
+        read_out(1, "z10", 0, SIDE, z10_bf[:], True)
         for o in range(OUT_TILES):
             store(0, o, False)
-        z11_bf = second_z(1)
-        read_out(1, 1, z11_bf[:])
+        last = [second_z(part) for part in (1, 2)]
+        for part in (1, 2):
+            read_out(1, "z1%d" % part, parts[part][0], parts[part][1], last[part - 1][:], part == 2)
         for o in range(OUT_TILES):
             store(1, o, o != 1)

@@ -25,7 +25,7 @@ ROWS = 4
 BLOCKS = 16
 PER_COLUMN = 16
 PIECE = PASS // 2
-BESIDE = 320
+BESIDE = 256
 SIDE = S // 2
 OUT_TILES = N // P
 RING = 4
@@ -301,6 +301,7 @@ def tile_list_foothold_terrain_blend_kernel(
         raw_wg11b = load_weight("raw_wg11b", wg[PASS:, :], PASS + BESIDE, PASS - BESIDE)
         reserve(ROW_BYTES)
         raw_wg11a = load_weight("raw_wg11a", wg[PASS:, :], PASS, BESIDE)
+        reserve(PASS + ROW_BYTES - 16 * BESIDE)
         raw_w1_1 = load_weight("raw_w1_1", w1, PASS, PASS)
         wo_w = new("wo_w", [P, 2, N], I32)
         nc.sync.dma_start(wo_w[:], wo_words.rearrange("ps p c i -> p ps (c i)").bitcast(I32))

from contextlib import ExitStack

import concourse.mybir as mybir

K, T, K2, T2, S, H, N = 1024, 2048, 512, 1024, 512, 1024, 384
FLOPS = 2 * (K2 * H * T2 + 2 * K * H * S + H * N * S)

F32 = mybir.dt.float32
BF16 = mybir.dt.bfloat16
I32 = mybir.dt.int32
U32 = mybir.dt.uint32
U16 = mybir.dt.uint16
U8 = mybir.dt.uint8
FP8X4 = mybir.dt.float8_e4m3fn_x4
FP4X4 = mybir.dt.float4_e2m1fn_x4
ALU = mybir.AluOpType
ACT = mybir.ActivationFunctionType

P = 128
PACK = 4
PASS = P * PACK
BANK = 512
QUAD = 32
ROWS = 4
BLOCKS = 16
PER_COLUMN = 16
PIECE = PASS // 2
BESIDE = 256
SIDE = S // 2
OUT_TILES = N // P
RING = 4
ALIGN = 64
ROW_BYTES = 4 * T2


def tile_list_foothold_terrain_blend_kernel(
    tc, tab_words, tab_scales, offs, offs2, offs3, base, xs, w1, w2_words, w2_scales, wg, wo_words, wo_scales, bo, out
):
    nc = tc.nc
    with ExitStack() as ctx:
        lists = ctx.enter_context(tc.tile_pool(name="lists", bufs=1))
        sb = ctx.enter_context(tc.tile_pool(name="sb", bufs=1))
        psum = ctx.enter_context(tc.psum_pool(name="psum", bufs=1))

        place = {}
        top = [0]

        def reserve(size):
            top[0] = top[0] + (size + ALIGN - 1) // ALIGN * ALIGN

        def new(name, shape, dtype, on=None, skip=0):
            if on is None:
                place[name] = top[0]
                size = 1 if dtype == U8 else 2 if dtype == BF16 else 4
                for n in shape[1:]:
                    size = size * n
                reserve(size)
            else:
                place[name] = place[on] + skip
            return sb.tile(shape, dtype, name=name, offset=place[name], align_bytes=ALIGN)

        def bank(tag, columns=BANK):
            return psum.tile([P, columns], F32, name="acc", tag=tag)

        turns = []

        def next_bank(columns=BANK):
            turns.append(columns)
            return bank(("s1", "s2", "s0", "s3")[(len(turns) - 1) % RING], columns)


        def load_list(name, src):
            tile = lists.tile([P, S // PER_COLUMN], U16, name=name)
            nc.sync.dma_start(tile[:], src)
            return tile

        page = [None] * PACK
        patch = [None] * PACK

        def load_grid_rows(t):
            page[t] = new("page%d" % t, [P, T2], F32)
            nc.sync.dma_start(page[t][:], base.rearrange("(p t) c -> p t c", t=PACK)[:, t, :])
            patch[t] = new("patch%d" % t, [P, S], F32)
            nc.sync.dma_start(patch[t][:], xs.rearrange("(p t) c -> p t c", t=PACK)[:, t, :])

        def load_weight(name, rows, first, width, on=None, skip=0):
            raw = new(name, [P, PACK, width], F32, on=on, skip=skip)
            nc.sync.dma_start(raw[:], rows.rearrange("(p j) c -> p j c", j=PACK)[:, :, first : first + width])
            return raw

        def load_table_words(ps):
            tile = new("tab_w%d" % ps, [P, T], I32)
            nc.sync.dma_start(tile[:], tab_words[ps].rearrange("p c i -> p (c i)").bitcast(I32))
            return tile

        def load_w2(ps):
            tile = new("w2_raw%d" % ps, [P, 2 * H], U8)
            nc.sync.dma_start(tile[:].bitcast(I32), w2_words[ps].bitcast(I32))
            return tile

        def move_table_plane(ps, row):
            nc.sync.dma_start(
                v_planes[row:P:QUAD, ps, :].bitcast(I32),
                v_rows[BLOCKS * ps + row : BLOCKS * (ps + 1) : ROWS, :].bitcast(I32),
            )


        def round_weight(copy, raw, dst, at=0):
            width = raw.shape[2]
            copy(
                out=dst.rearrange("p (t x j) -> p x j t", t=PACK, j=PACK)[:, at // PACK : (at + width) // PACK],
                in_=raw.rearrange("p j (x t) -> p x j t", t=PACK),
            )

        def round_pair(copy, raw, pair, dst):
            copy(
                out=dst.rearrange("p (t x j) -> p x j t", t=2, j=PACK),
                in_=raw.rearrange("p j (x t) -> p x j t", t=PACK)[:, :, :, 2 * pair : 2 * pair + 2],
            )

        def quantise_pair(codes, plane, pair, src):
            columns = slice(pair * PIECE, (pair + 1) * PIECE)
            nc.vector.quantize_mx(out=codes[:, columns].bitcast(FP8X4), scales=plane[:, columns], in_=src)

        def quantise(name, src, columns, on=None, skip=0):
            codes = new(name + "_codes", [P, columns], U32)
            plane = new(name + "_plane", [P, columns], U8, on=on, skip=skip)
            nc.vector.quantize_mx(out=codes[:].bitcast(FP8X4), scales=plane[:], in_=src)
            return codes, plane

        def scatter_patch(t):
            nc.vector.tensor_copy(page[t][:].indirect(idx2[:]), patch[t][:])

        def round_page(t, column_halves):
            nc.scalar.copy(
                out=pairs[:, column_halves, t // 2, :, t % 2],
                in_=page[t][:].rearrange("p (h c) -> p h c", h=2)[:, column_halves, :],
            )

        def weave(copy, dst, src):
            copy(out=dst.bitcast(F32), in_=src.rearrange("p u c e -> p u (c e)").bitcast(F32).rearrange("p u c -> p c u"))

        def deal_w2(ps):
            nc.vector.tensor_copy(
                out=w2_dealt[:, ps, :].bitcast(U16).rearrange("p (g t run y) -> p g run t y", g=2, t=PACK, y=8),
                in_=w2_raw[ps][:].bitcast(U16).rearrange("p (g run y t) -> p g run t y", g=2, t=PACK, y=8),
            )


        page_q = [None, None]
        w1_q = [None, None]
        wg_q = {}
        a_rows = {}
        trust = {}

        def make_a(s, h, acc, on=None, skip=0):
            g, t = divmod(s, PACK)
            rows = slice(t * P, (t + 1) * P)
            if h == 0:
                a_rows[s] = new("a%d" % s, [P, T2], F32, on=on, skip=skip)
            nc.tensor.matmul_mx(
                out=acc[:],
                lhsT=w1_q[g][0][:, rows].bitcast(FP8X4),
                lhsT_scale=w1_q[g][1][:, rows],
                rhs=page_q[h][0][:].bitcast(FP8X4),
                rhs_scale=page_q[h][1][:],
                start=True,
                stop=True,
            )
            nc.scalar.copy(out=a_rows[s][:, h * BANK : (h + 1) * BANK], in_=acc[:])

        def make_trust(s, acc, first=0):
            g, t = divmod(s, PACK)
            rows = slice(t * P, (t + 1) * P)
            for ps in (first, 1 - first):
                nc.tensor.matmul_mx(
                    out=acc[:],
                    lhsT=wg_q[g, ps][0][:, rows].bitcast(FP8X4),
                    lhsT_scale=wg_q[g, ps][1][:, rows],
                    rhs=v_words[:, ps, :].bitcast(FP8X4),
                    rhs_scale=v_planes[:, ps, :],
                    start=(ps == first),
                    stop=(ps != first),
                )
            trust[s] = new("trust%d" % s, [P, S], F32)
            nc.scalar.activation(out=trust[s][:], in_=acc[:], func=ACT.Sigmoid)

        def make_rest(s, acc, dst, first=0):
            columns = slice(s * P, (s + 1) * P)
            for ps in (first, 1 - first):
                nc.tensor.matmul_mx(
                    out=acc[:],
                    lhsT=w2_dealt[:, ps, 2 * s * P : 2 * (s + 1) * P].bitcast(FP4X4),
                    lhsT_scale=w2_dealt_planes[:, ps, columns],
                    rhs=v_words[:, ps, :].bitcast(FP8X4),
                    rhs_scale=v_planes[:, ps, :],
                    start=(ps == first),
                    stop=(ps != first),
                )
            nc.vector.scalar_tensor_tensor(
                out=dst, in0=trust[s][:], scalar=1.0, in1=acc[:], op0=ALU.subtract, op1=ALU.mult
            )

        def pick(s, dst):
            nc.vector.tensor_tensor(out=dst, in0=a_rows[s][:].indirect(idx3[:]), in1=trust[s][:], op=ALU.mult)

        def subtract_interleaved(dst, picked, rest, slices):
            run = 8 // slices
            nc.vector.tensor_tensor(
                out=dst.rearrange("p (c e t) -> p c t e", e=run, t=slices),
                in0=picked.rearrange("p t (c e) -> p c t e", e=run),
                in1=rest.rearrange("p t (c e) -> p c t e", e=run),
                op=ALU.subtract,
            )


        tab_rows = new("tab_rows", [P, T], U8)
        w2_planes = new("w2_planes", [P, 2, H], U8)
        v_planes = new("v_planes", [P, 2, S], U8)
        wo_planes = new("wo_planes", [P, N], U8)
        nc.vector.memset(tab_rows[QUAD : 2 * QUAD, :].bitcast(I32), 0)
        nc.vector.memset(tab_rows[2 * QUAD :, :].bitcast(I32), 0)
        nc.vector.memset(v_planes[:].rearrange("p ps c -> p (ps c)").bitcast(I32), 0)
        nc.vector.memset(wo_planes[:].bitcast(I32), 0)

        warm = new("warm", [P, 2], F32)
        nc.vector.memset(warm[:, 0:1], 0.0)
        nc.vector.memset(w2_planes[:].rearrange("p ps c -> p (ps c)").bitcast(I32), 0)
        nc.scalar.activation(out=warm[:, 1:2], in_=warm[:, 0:1], func=ACT.Sigmoid)

        for row in range(ROWS):
            nc.gpsimd.dma_start(
                w2_planes[row:P:QUAD, :, :].bitcast(I32),
                w2_scales[:, row:BLOCKS:ROWS, :].rearrange("ps quad c -> quad ps c").bitcast(I32),
            )


        idx = load_list("idx", offs)
        nc.scalar.dma_start(tab_rows[0:QUAD, :].bitcast(I32), tab_scales.rearrange("ps q c -> (ps q) c").bitcast(I32))
        reserve(ROW_BYTES - S // 2)
        v_rows = new("v_rows", [P, S], U8)
        reserve(2 * PASS - S // 2)
        nc.vector.tensor_copy(v_rows[:], tab_rows[:].indirect(idx[:]))

        load_grid_rows(0)
        idx2 = load_list("idx2", offs2)
        load_grid_rows(1)
        raw_w1_0 = load_weight("raw_w1_0", w1, 0, PASS)
        load_grid_rows(2)
        raw_wg00 = load_weight("raw_wg00", wg[0:PASS, :], 0, PASS)
        load_grid_rows(3)
        moves = [(ps, row) for ps in range(2) for row in range(ROWS)]
        for ps, row in moves[0:2]:
            move_table_plane(ps, row)
        raw_wg01a = load_weight("raw_wg01a", wg[PASS:, :], 0, PIECE)
        for ps, row in moves[2:5]:
            move_table_plane(ps, row)
        tab_w0 = load_table_words(0)
        for ps, row in moves[5:8]:
            move_table_plane(ps, row)
        tab_w1 = load_table_words(1)
        reserve(ROW_BYTES // 2)
        raw_wg01b = load_weight("raw_wg01b", wg[PASS:, :], PIECE, PIECE)
        reserve(ROW_BYTES // 2)
        raw_wg10 = load_weight("raw_wg10", wg[0:PASS, :], PASS, PASS)
        w2_raw = [load_w2(0), load_w2(1)]
        idx3 = load_list("idx3", offs3)


        w2_dealt_planes = new("w2_dealt_planes", [P, 2, H], U8)
        nc.gpsimd.tensor_copy(
            out=w2_dealt_planes[:].rearrange("p ps (g t run y) -> p (ps g) run t y", g=2, t=PACK, y=16),
            in_=w2_planes[:].rearrange("p ps (g run y t) -> p (ps g) run t y", g=2, t=PACK, y=16),
        )
        w2_dealt = new("w2_dealt", [P, 2, 2 * H], U8)

        first_bf = new("first_bf", [P, 2, PASS * PACK], BF16)
        wg_bf01 = new("wg_bf01", [P, PASS * PACK], BF16)
        round_weight(nc.scalar.copy, raw_w1_0[:], first_bf[:, 0, :])
        pairs = new("pairs", [P, 2, 2, BANK, 2], BF16, on="raw_w1_0")
        page_bf = [
            new("page_bf0", [P, BANK * PACK], BF16, on="v_rows", skip=S // 2 - ROW_BYTES),
            new("page_bf1", [P, BANK * PACK], BF16),
        ]
        both = slice(0, 2)
        scatter_patch(0)
        round_page(0, both)
        scatter_patch(1)
        round_page(1, both)
        round_weight(nc.gpsimd.tensor_copy, raw_wg00[:], first_bf[:, 1, :])
        scatter_patch(2)
        round_page(2, both)
        round_weight(nc.gpsimd.tensor_copy, raw_wg01a[:], wg_bf01[:])
        scatter_patch(3)
        for h in range(2):
            round_page(3, slice(h, h + 1))
        weave(nc.scalar.copy, page_bf[1][:], pairs[:, 1])
        round_weight(nc.scalar.copy, raw_wg01b[:], wg_bf01[:], PIECE)

        v_words = new("v_words", [P, 2, S], U32)
        raw_wg11b = load_weight("raw_wg11b", wg[PASS:, :], PASS + BESIDE, PASS - BESIDE)
        reserve(ROW_BYTES)
        raw_wg11a = load_weight("raw_wg11a", wg[PASS:, :], PASS, BESIDE)
        reserve(PASS + ROW_BYTES - 16 * BESIDE)
        raw_w1_1 = load_weight("raw_w1_1", w1, PASS, PASS)
        wo_w = new("wo_w", [P, 2, N], I32)
        nc.sync.dma_start(wo_w[:], wo_words.rearrange("ps p c i -> p ps (c i)").bitcast(I32))
        for quad in range(P // QUAD):
            nc.sync.dma_start(
                wo_planes[QUAD * quad : QUAD * quad + 2 * ROWS, :].bitcast(I32),
                wo_scales[:, ROWS * quad : ROWS * (quad + 1), :].bitcast(I32),
            )
        bias = new("bias", [P, OUT_TILES], F32)
        with nc.allow_non_contiguous_dma(reason="one bias value for each partition"):
            nc.sync.dma_start(bias[:], bo.rearrange("(o p) -> p o", p=P))


        nc.vector.tensor_copy(v_words[:, 0, :], tab_w0[:].bitcast(U32).indirect(idx[:]))
        weave(nc.vector.tensor_copy, page_bf[0][:], pairs[:, 0])
        first_codes, first_plane = quantise(
            "first", first_bf[:].rearrange("p w c -> p (w c)"), 2 * PASS, on="v_rows", skip=S // 2
        )
        w1_q[0] = (first_codes[:, 0:PASS], first_plane[:, 0:PASS])
        wg_q[0, 0] = (first_codes[:, PASS:], first_plane[:, PASS:])
        page_q[0] = quantise("page0", page_bf[0][:], BANK)
        page_q[1] = quantise("page1", page_bf[1][:], BANK, on="first_bf")
        nc.vector.tensor_copy(v_words[:, 1, :], tab_w1[:].bitcast(U32).indirect(idx[:]))
        reserve(ROW_BYTES // 2)
        wg_q[0, 1] = quantise("wg01", wg_bf01[:], PASS)
        reserve(ROW_BYTES - PASS)

        wg_bf10 = [new("wg_bf10a", [P, PIECE * PACK], BF16)]
        round_pair(nc.vector.tensor_copy, raw_wg10[:], 0, wg_bf10[0][:])
        deal_w2(0)
        deal_w2(1)


        make_a(0, 0, bank("s0"), "raw_wg01b", -ROW_BYTES // 2)
        make_a(1, 0, bank("s1"), "raw_wg01b", ROW_BYTES // 2)
        make_a(0, 1, bank("s2"))
        make_trust(0, bank("b0"))
        make_a(1, 1, bank("s0"))
        make_trust(1, bank("b1"))
        for s in (2, 3):
            make_trust(s, bank("b%d" % s), 1)
        make_a(2, 0, bank("s1"), "wg01_codes", -ROW_BYTES // 2)
        make_a(2, 1, bank("s2"))
        make_a(3, 0, bank("s0"), "wg01_plane")
        make_a(3, 1, bank("b0"))
        picked01 = new("picked01", [P, 2, S], F32)
        rest0 = [new("rest0%d" % u, [P, 2, S], F32, on="page%d" % u) for u in range(2)]
        for s in range(2):
            pick(s, picked01[:, s, :])
        wg_bf11 = new("wg_bf11", [P, PASS * PACK], BF16, on="a0")
        round_weight(nc.gpsimd.tensor_copy, raw_wg11a[:], wg_bf11[:])
        for s, tag in ((0, "b1"), (2, "b2"), (3, "b3")):
            make_rest(s, bank(tag), rest0[s // 2][:, s % 2, :], s // 2)
        wg_q[1, 0] = (
            new("wg10_codes", [P, PASS], U32),
            new("wg10_plane", [P, PASS], U8, on="raw_wg11a"),
        )
        picked23 = new("picked23", [P, 2, S], F32, on="raw_wg11a", skip=PASS)
        wg_bf10.append(new("wg_bf10b", [P, PIECE * PACK], BF16, on="first_codes"))
        round_pair(nc.scalar.copy, raw_wg10[:], 1, wg_bf10[1][:])
        round_weight(nc.scalar.copy, raw_wg11b[:], wg_bf11[:], BESIDE)
        quantise_pair(wg_q[1, 0][0], wg_q[1, 0][1], 0, wg_bf10[0][:])
        pick(2, picked23[:, 0, :])
        quantise_pair(wg_q[1, 0][0], wg_q[1, 0][1], 1, wg_bf10[1][:])
        pick(3, picked23[:, 1, :])
        wg_q[1, 1] = quantise("wg11", wg_bf11[:], PASS)

        z0_pairs = new("z0_pairs", [P, 2, S, 2], BF16, on="raw_wg11b", skip=ALIGN)
        w1_bf1 = [
            new("w1_bf1", [P, PIECE * PACK], BF16, on="raw_wg10")[:],
            z0_pairs[:, 0].rearrange("p c e -> p (c e)"),
        ]
        w1_codes1 = new("w1_codes1", [P, PASS], U32, on="tab_w0")
        w1_plane1 = new("w1_plane1", [P, PASS], U8)
        w1_q[1] = (w1_codes1, w1_plane1)
        subtract_interleaved(z0_pairs[:, 1].rearrange("p c e -> p (c e)"), picked23[:], rest0[1][:], 2)
        for pair in range(2):
            round_pair(nc.scalar.copy, raw_w1_1[:], pair, w1_bf1[pair])
            quantise_pair(w1_codes1, w1_plane1, pair, w1_bf1[pair])
        late_rest = new("late_rest", [P, S], F32, on="raw_w1_1")
        make_rest(1, bank("b0"), late_rest[:])
        for s, rest in ((0, rest0[0][:, 0, :]), (1, late_rest[:])):
            nc.gpsimd.tensor_tensor(out=z0_pairs[:, 0, :, s], in0=picked01[:, s, :], in1=rest, op=ALU.subtract)


        for s in range(PACK, 2 * PACK):
            make_trust(s, next_bank())
        rest1 = new("rest1", [P, PACK, S], F32)
        for s in range(PACK, 2 * PACK):
            make_rest(s, bank(("b1", "b2", "b3", "b0")[s - PACK]), rest1[:, s - PACK, :])
        for s, on in ((4, "page2"), (5, "page3"), (6, "raw_wg00"), (7, "raw_wg01a")):
            make_a(s, 0, next_bank(), on)
            make_a(s, 1, next_bank())
        z0_bf = new("z0_bf", [P, S * PACK], BF16, on="w1_codes1")
        weave(nc.scalar.copy, z0_bf[:], z0_pairs[:])
        picked1 = new("picked1", [P, PACK, S], F32)
        for s in range(PACK, 2 * PACK):
            pick(s, picked1[:, s - PACK, :])


        parts = ((0, SIDE), (SIDE, SIDE // 2), (SIDE + SIDE // 2, SIDE // 2))
        sums = [
            [bank("b%d" % (o + 1), SIDE) for o in range(OUT_TILES)],
            [next_bank(SIDE) for o in range(OUT_TILES)],
        ]

        def second_z(part):
            first, width = parts[part]
            z_bf = new("z1%d_bf" % part, [P, width * PACK], BF16, on="z0_pairs", skip=first * PACK * 2)
            entries = slice(first, first + width)
            subtract_interleaved(z_bf[:], picked1[:, :, entries], rest1[:, :, entries], PACK)
            return z_bf

        def read_out(g, name, first, width, src, stop):
            codes, plane = quantise(name, src, width)
            side, column = divmod(first, SIDE)
            for o in range(OUT_TILES):
                rows = slice(o * P, (o + 1) * P)
                nc.tensor.matmul_mx(
                    out=sums[side][o][:, column : column + width],
                    lhsT=wo_w[:, g, rows].bitcast(FP8X4),
                    lhsT_scale=wo_planes[ROWS * g : P, rows],
                    rhs=codes[:].bitcast(FP8X4),
                    rhs_scale=plane[:],
                    start=(g == 0),
                    stop=stop,
                )

        def store(side, o, on_vector):
            result = new("result%d%d" % (side, o), [P, SIDE], F32)
            if on_vector:
                nc.vector.tensor_scalar(
                    out=result[:], in0=sums[side][o][:], scalar1=bias[:, o : o + 1], scalar2=None, op0=ALU.add
                )
            else:
                nc.scalar.activation(out=result[:], in_=sums[side][o][:], func=ACT.Identity, bias=bias[:, o : o + 1])
            nc.sync.dma_start(out[o * P : (o + 1) * P, side * SIDE : (side + 1) * SIDE], result[:])

        read_out(0, "z00", 0, SIDE, z0_bf[:, 0 : SIDE * PACK], False)
        z10_bf = second_z(0)
        read_out(0, "z01", SIDE, SIDE, z0_bf[:, SIDE * PACK :], False)
        read_out(1, "z10", 0, SIDE, z10_bf[:], True)
        for o in range(OUT_TILES):
            store(0, o, False)
        last = [second_z(part) for part in (1, 2)]
        for part in (1, 2):
            read_out(1, "z1%d" % part, parts[part][0], parts[part][1], last[part - 1][:], part == 2)
        for o in range(OUT_TILES):
            store(1, o, o != 1)
